import numpy as np
import ml_dtypes


def mxq(x, axis, fmt="e4m3"):
    dtype, down = {"e4m3": (ml_dtypes.float8_e4m3fn, 7), "e5m2": (ml_dtypes.float8_e5m2, 14)}[fmt]
    v = np.moveaxis(np.asarray(x, np.float32).astype(ml_dtypes.bfloat16).astype(np.float64), axis, -1)
    blocks = v.reshape(v.shape[:-1] + (-1, 32))
    amax = np.abs(blocks).max(-1, keepdims=True)
    byte = np.maximum(np.where(amax > 0, np.frexp(amax)[1] - 1 + 127, 0) - down, 1)
    scale = np.exp2(byte - 127.0)
    codes = (blocks / scale).astype(np.float32).astype(dtype).astype(np.float64)
    return np.moveaxis((codes * scale).reshape(v.shape), -1, axis)


WIDE = False


def mx_kscale(k):
    if not WIDE:
        return np.ones(k)
    levels = np.array([24, -24, 12, -12, 0])
    if k % 512:
        return np.exp2(np.random.permutation(np.resize(levels, k // 32))).repeat(32)
    a = np.empty((k // 512, 16))
    for p in range(k // 512):
        a[p, :8] = np.random.permutation(np.resize(levels, 8))
        for g in range(8):
            far = levels[np.abs(levels - a[p, g]) >= 10]
            a[p, g + 8] = far[np.random.randint(len(far))]
    return np.exp2(a.ravel()).repeat(32)


def f64(x):
    return np.asarray(x).astype(np.float64)


def striped(idx):
    return np.tile(idx.reshape(-1, 16).T, (8, 1)).astype(np.uint16)


def unstriped(offs):
    return offs[:16].T.reshape(-1).astype(np.int64)


E2M1 = np.array([0.0, 0.5, 1.0, 1.5, 2.0, 3.0, 4.0, 6.0, -0.0, -0.5, -1.0, -1.5, -2.0, -3.0, -4.0, -6.0])


def pack_weight(w, fmt):
    k, n = w.shape
    w = f64(np.asarray(w, np.float32).astype(ml_dtypes.bfloat16)).reshape(k // 32, 32, n)
    amax = np.abs(w).max(1)
    if fmt == "e4m3":
        byte = np.frexp(amax)[1] - 1 + 127 - 7
    else:
        mant, ex = np.frexp(amax / 6.0)
        byte = np.where(mant > 0.5, ex, ex - 1) + 127
    byte = np.clip(np.where(amax > 0, byte, 1), 1, 254)
    scaled = (w * np.exp2(127.0 - byte)[:, None, :]).reshape(k, n).astype(np.float32)
    by_word = np.ascontiguousarray(scaled.reshape(k // 512, 128, 4, n).transpose(0, 1, 3, 2))
    if fmt == "e4m3":
        words = by_word.astype(ml_dtypes.float8_e4m3fn).view(np.uint8)
    else:
        c = by_word.astype(ml_dtypes.float4_e2m1fn).view(np.uint8) & 0xF
        words = (c[..., 0::2] | (c[..., 1::2] << 4)).reshape(k // 512, 128, 2 * n)
    return np.ascontiguousarray(words), np.ascontiguousarray(byte.astype(np.uint8).reshape(k // 512, 16, n))


def unpack_weight(words, scales, fmt):
    g, _, n = scales.shape
    words = np.ascontiguousarray(words).reshape(g, 128, n, -1)
    if fmt == "e4m3":
        vals = words.view(ml_dtypes.float8_e4m3fn).astype(np.float64)
    else:
        nib = np.empty((g, 128, n, 4), np.uint8)
        nib[..., 0::2] = words & 0xF
        nib[..., 1::2] = words >> 4
        vals = E2M1[nib]
    vals = vals * np.repeat(np.exp2(scales.astype(np.float64) - 127.0), 8, axis=1)[..., None]
    return vals.transpose(0, 1, 3, 2).reshape(g * 512, n)


K, L, R, N, T, J = 512, 512, 512, 256, 2048, 1024


def setup_inputs():
    n = np.random.standard_normal
    s = mx_kscale(K)[:, None]
    s2 = mx_kscale(L)[:, None]
    u = mx_kscale(R)[:, None]
    p_tab = pack_weight(n((K, T)) * s, "e4m3")
    p_tab2 = pack_weight(n((L, T)) * s2, "e4m3")
    p_wer = pack_weight(n((K, R)) / np.sqrt(K) / s * u.T, "e4m3")
    p_wei = pack_weight(n((K, R)) / np.sqrt(K) / s * u.T, "e4m3")
    p_wrr = pack_weight(n((L, R)) / np.sqrt(L) / s2, "e2m1")
    p_wri = pack_weight(n((L, R)) / np.sqrt(L) / s2, "e2m1")
    p_nr = pack_weight(n((R, N)) / np.sqrt(R) / u, "e4m3")
    p_ni = pack_weight(n((R, N)) / np.sqrt(R) / u, "e2m1")
    return {
        "tab_words": p_tab[0],
        "tab_scales": p_tab[1],
        "tab2_words": p_tab2[0],
        "tab2_scales": p_tab2[1],
        "wer_words": p_wer[0],
        "wer_scales": p_wer[1],
        "wei_words": p_wei[0],
        "wei_scales": p_wei[1],
        "wrr_words": p_wrr[0],
        "wrr_scales": p_wrr[1],
        "wri_words": p_wri[0],
        "wri_scales": p_wri[1],
        "nr_words": p_nr[0],
        "nr_scales": p_nr[1],
        "ni_words": p_ni[0],
        "ni_scales": p_ni[1],
        "offs": striped(np.random.permutation(T)[:J]),
        "offs2": striped(np.random.permutation(T)[:J]),
    }


def reference(tab_words, tab_scales, tab2_words, tab2_scales, wer_words, wer_scales, wei_words, wei_scales, wrr_words, wrr_scales, wri_words, wri_scales, nr_words, nr_scales, ni_words, ni_scales, offs, offs2):
    idx = unstriped(offs)
    idx2 = unstriped(offs2)
    tab_ = unpack_weight(tab_words, tab_scales, "e4m3")[:, idx]
    tab2_ = unpack_weight(tab2_words, tab2_scales, "e4m3")[:, idx2]
    wer_ = unpack_weight(wer_words, wer_scales, "e4m3")
    aer = wer_.T @ tab_
    wei_ = unpack_weight(wei_words, wei_scales, "e4m3")
    aei = wei_.T @ tab_
    wrr_ = unpack_weight(wrr_words, wrr_scales, "e2m1")
    arr = wrr_.T @ tab2_
    wri_ = unpack_weight(wri_words, wri_scales, "e2m1")
    ari = wri_.T @ tab2_
    hr = aer * arr - aei * ari
    hi = aer * ari + aei * arr
    hr_ = mxq(hr, 0, "e4m3")
    hi_ = mxq(hi, 0, "e4m3")
    nr_ = unpack_weight(nr_words, nr_scales, "e4m3")
    ni_ = unpack_weight(ni_words, ni_scales, "e2m1")
    y = nr_.T @ hr_ + ni_.T @ hi_
    return y

@@ -1,0 +1,222 @@
+from contextlib import ExitStack
+
+import concourse.mybir as mybir
+from concourse.masks import make_identity
+
+K, L, R, N, T, J = 512, 512, 512, 256, 2048, 1024
+FLOPS = 2 * 4 * K * R * J + 2 * 2 * R * N * J
+
+F32 = mybir.dt.float32
+BF16 = mybir.dt.bfloat16
+I32 = mybir.dt.int32
+U32 = mybir.dt.uint32
+U16 = mybir.dt.uint16
+U8 = mybir.dt.uint8
+FP8X4 = mybir.dt.float8_e4m3fn_x4
+FP4X4 = mybir.dt.float4_e2m1fn_x4
+MULT = mybir.AluOpType.mult
+
+P = 128
+PACK = 4
+TILES = J // P
+WORD_CHUNK = 256
+SCALE_CHUNK = 512
+
+
+def tile_list_ckg_none_kernel(
+    tc, tab_words, tab_scales, tab2_words, tab2_scales, wer_words, wer_scales, wei_words, wei_scales,
+    wrr_words, wrr_scales, wri_words, wri_scales, nr_words, nr_scales, ni_words, ni_scales, offs, offs2, out,
+):
+    nc = tc.nc
+    with ExitStack() as ctx:
+        keep = ctx.enter_context(tc.tile_pool(name="keep", bufs=1))
+        ring = ctx.enter_context(tc.tile_pool(name="ring", bufs=3))
+        psum = ctx.enter_context(tc.psum_pool(name="psum", bufs=1))
+
+        list1 = keep.tile([P, J // 16], U16, name="list1")
+        list2 = keep.tile([P, J // 16], U16, name="list2")
+        tab1_w = keep.tile([P, T], I32, name="tab1_w", align_bytes=64)
+        tab2_w = keep.tile([P, T], I32, name="tab2_w", align_bytes=64)
+        tab1_s = keep.tile([P, T // 4], I32, name="tab1_s", align_bytes=64)
+        tab2_s = keep.tile([P, T // 4], I32, name="tab2_s", align_bytes=64)
+        wer_w = keep.tile([P, R], I32, name="wer_w", align_bytes=64)
+        wei_w = keep.tile([P, R], I32, name="wei_w", align_bytes=64)
+        wrr_w = keep.tile([P, R // 2], I32, name="wrr_w", align_bytes=64)
+        wri_w = keep.tile([P, R // 2], I32, name="wri_w", align_bytes=64)
+        nr_w = keep.tile([P, N], I32, name="nr_w", align_bytes=64)
+        ni_w = keep.tile([P, N // 2], I32, name="ni_w", align_bytes=64)
+        planes = keep.tile([P, (4 * R + 2 * N) // 4], I32, name="planes", align_bytes=64)
+        ident = keep.tile([P, P], F32, name="ident")
+
+        plane_cols = {}
+        col = 0
+        for name, width in (("wrr", R), ("wri", R), ("wer", R), ("wei", R), ("nr", N), ("ni", N)):
+            plane_cols[name] = (col, col + width)
+            col += width
+
+        def plane_words(name):
+            lo, hi = plane_cols[name]
+            return slice(lo // 4, hi // 4)
+
+        def plane(name, lo, hi):
+            base = plane_cols[name][0]
+            return planes[:].bitcast(U8)[:, base + lo : base + hi]
+
+        def load_words(tile, words):
+            src = words[0]
+            if len(src.shape) == 3:
+                src = src.rearrange("p n t -> p (n t)")
+            nc.sync.dma_start(out=tile[:], in_=src.bitcast(I32))
+
+        def load_scales(queue, tile, cols, scales, rows=range(4)):
+            by_row = scales[0].bitcast(I32).rearrange("(q r) n -> r q n", r=4)
+            for r in rows:
+                queue.dma_start(out=tile[r:P:32, cols], in_=by_row[r])
+
+        whole = slice(0, T // 4)
+        nc.vector.memset(tab2_s[:], 0)
+        nc.vector.memset(tab1_s[:], 0)
+        nc.gpsimd.memset(planes[:], 0)
+        make_identity(nc, ident[:])
+
+        nc.sync.dma_start(list2[:], offs2)
+        load_scales(nc.sync, tab2_s, whole, tab2_scales)
+        nc.sync.dma_start(list1[:], offs)
+        load_words(tab2_w, tab2_words)
+        load_scales(nc.sync, tab1_s, whole, tab_scales)
+        load_words(tab1_w, tab_words)
+        load_words(wrr_w, wrr_words)
+        load_words(wri_w, wri_words)
+        load_scales(nc.scalar, planes, plane_words("wrr"), wrr_scales)
+        load_scales(nc.scalar, planes, plane_words("wri"), wri_scales)
+        load_words(wer_w, wer_words)
+        load_words(wei_w, wei_words)
+        load_scales(nc.scalar, planes, plane_words("wer"), wer_scales)
+        load_scales(nc.scalar, planes, plane_words("wei"), wei_scales)
+        load_words(nr_w, nr_words)
+        load_words(ni_w, ni_words)
+        load_scales(nc.sync, planes, plane_words("nr"), nr_scales)
+        load_scales(nc.sync, planes, plane_words("ni"), ni_scales)
+
+        def gather(table, view, offsets, chunk, c, name):
+            picked = keep.tile([P, chunk], view, name=name + str(c), align_bytes=64)
+            cols = slice(c * chunk // 16, (c + 1) * chunk // 16)
+            nc.vector.tensor_copy(picked[:], table[:].bitcast(view).indirect(offsets[:, cols]))
+            return picked
+
+        s1, s2, w1, w2 = {}, {}, {}, {}
+        for c in range(J // SCALE_CHUNK):
+            s2[c] = gather(tab2_s, U8, list2, SCALE_CHUNK, c, "s2_")
+        for c in range(J // SCALE_CHUNK):
+            s1[c] = gather(tab1_s, U8, list1, SCALE_CHUNK, c, "s1_")
+
+        def gather_words(c):
+            w2[c] = gather(tab2_w, U32, list2, WORD_CHUNK, c, "w2_")
+            w1[c] = gather(tab1_w, U32, list1, WORD_CHUNK, c, "w1_")
+
+        def project(i, codes, scales, weight, fmt, name, tag, bufs):
+            acc = psum.tile([P, R], F32, name=tag, bufs=bufs)
+            c, lo = divmod(i * P, WORD_CHUNK)
+            cs, los = divmod(i * P, SCALE_CHUNK)
+            nc.tensor.matmul_mx(
+                out=acc[:],
+                lhsT=codes[c][:, lo : lo + P].bitcast(FP8X4),
+                lhsT_scale=scales[cs][:, los : los + P],
+                rhs=weight[:].bitcast(fmt),
+                rhs_scale=plane(name, 0, R),
+                start=True,
+                stop=True,
+            )
+            return acc[:].rearrange("j (m t) -> j t m", t=PACK)
+
+        aer, aei, arr, ari, hq = {}, {}, {}, {}, {}
+
+        def relation(i):
+            for store, weight, name in ((arr, wrr_w, "wrr"), (ari, wri_w, "wri")):
+                acc = project(i, w2, s2, weight, FP4X4, name, "rel", 2)
+                store[i] = ring.tile([P, PACK, P], F32, name="sb_" + name)
+                nc.scalar.copy(out=store[i][:], in_=acc)
+
+        def entity_real(i):
+            aer[i] = project(i, w1, s1, wer_w, FP8X4, "wer", "ent", 3)
+
+        def entity_imag(i):
+            aei[i] = project(i, w1, s1, wei_w, FP8X4, "wei", "ent", 3)
+
+        def product(ent, rel, name, negate=False):
+            prod = ring.tile([P, PACK, P], F32, name=name, bufs=2)
+            if negate:
+                nc.vector.scalar_tensor_tensor(out=prod[:], in0=ent, scalar=-1.0, in1=rel[:], op0=MULT, op1=MULT)
+            else:
+                nc.vector.tensor_tensor(out=prod[:], in0=ent, in1=rel[:], op=MULT)
+            return prod
+
+        def turn_and_add(i, part, first, second):
+            turned = psum.tile([P, PACK, P], F32, name="turned", bufs=2)
+            for t in range(PACK):
+                nc.tensor.matmul(out=turned[:, t, :], lhsT=first[:, t, :], rhs=ident[:], is_transpose=True, start=True, stop=False)
+                nc.tensor.matmul(out=turned[:, t, :], lhsT=second[:, t, :], rhs=ident[:], is_transpose=True, start=False, stop=True)
+            hq[i, part] = ring.tile([P, P, PACK], BF16, name="hq" + part, align_bytes=64)
+            nc.scalar.copy(out=hq[i, part][:], in_=turned[:].rearrange("p t j -> p j t"))
+
+        def score(i):
+            codes, scales = {}, {}
+            for part in "ri":
+                codes[part] = ring.tile([P, P], U32, name="hc" + part, align_bytes=64)
+                scales[part] = ring.tile([P, P], U8, name="hs" + part, align_bytes=64)
+                nc.vector.quantize_mx(
+                    out=codes[part][:].bitcast(FP8X4),
+                    scales=scales[part][:],
+                    in_=hq[i, part][:].rearrange("p j t -> p (j t)"),
+                )
+            y = psum.tile([P, N // P, P], F32, name="y", bufs=1)
+            for h in range(N // P):
+                nc.tensor.matmul_mx(
+                    out=y[:, h, :],
+                    lhsT=nr_w[:, h * P : (h + 1) * P].bitcast(FP8X4),
+                    lhsT_scale=plane("nr", h * P, (h + 1) * P),
+                    rhs=codes["r"][:].bitcast(FP8X4),
+                    rhs_scale=scales["r"][:],
+                    start=True,
+                    stop=False,
+                )
+                nc.tensor.matmul_mx(
+                    out=y[:, h, :],
+                    lhsT=ni_w[:, h * P // 2 : (h + 1) * P // 2].bitcast(FP4X4),
+                    lhsT_scale=plane("ni", h * P, (h + 1) * P),
+                    rhs=codes["i"][:].bitcast(FP8X4),
+                    rhs_scale=scales["i"][:],
+                    start=False,
+                    stop=True,
+                )
+            y_sb = ring.tile([P, N // P, P], F32, name="y_sb")
+            nc.scalar.copy(out=y_sb[:], in_=y[:])
+            nc.sync.dma_start(
+                out=out[:, i * P : (i + 1) * P].rearrange("(h p) j -> p h j", p=P), in_=y_sb[:]
+            )
+
+        tiles_per_chunk = WORD_CHUNK // P
+        gather_words(0)
+        gather_words(1)
+        relation(0)
+        entity_real(0)
+        entity_imag(0)
+        relation(1)
+        entity_real(1)
+        for i in range(TILES):
+            p1 = product(aer[i], arr[i], "p1")
+            p2 = product(aei[i], ari[i], "p2", negate=True)
+            turn_and_add(i, "r", p1, p2)
+            if i > 0:
+                score(i - 1)
+            p3 = product(aer[i], ari[i], "p3")
+            if i + 1 < TILES:
+                entity_imag(i + 1)
+            p4 = product(aei[i], arr[i], "p4")
+            turn_and_add(i, "i", p3, p4)
+            if i % tiles_per_chunk == 0 and i // tiles_per_chunk + 2 < J // WORD_CHUNK:
+                gather_words(i // tiles_per_chunk + 2)
+            if i + 2 < TILES:
+                entity_real(i + 2)
+                relation(i + 2)
+        score(TILES - 1)

@@ -20,7 +20,7 @@ P = 128
 PACK = 4
 TILES = J // P
 WORD_CHUNK = 256
-SCALE_CHUNK = 512
+SCALE_CHUNK = 256
 
 
 def tile_list_ckg_none_kernel(
@@ -45,58 +45,66 @@ def tile_list_ckg_none_kernel(
         wri_w = keep.tile([P, R // 2], I32, name="wri_w", align_bytes=64)
         nr_w = keep.tile([P, N], I32, name="nr_w", align_bytes=64)
         ni_w = keep.tile([P, N // 2], I32, name="ni_w", align_bytes=64)
-        planes = keep.tile([P, (4 * R + 2 * N) // 4], I32, name="planes", align_bytes=64)
+        planes1 = keep.tile([P, 4, R], I32, name="planes1", align_bytes=64)
+        planes2 = keep.tile([P, 4, N // 2], I32, name="planes2", align_bytes=64)
         ident = keep.tile([P, P], F32, name="ident")
 
-        plane_cols = {}
-        col = 0
-        for name, width in (("wrr", R), ("wri", R), ("wer", R), ("wei", R), ("nr", N), ("ni", N)):
-            plane_cols[name] = (col, col + width)
-            col += width
-
-        def plane_words(name):
-            lo, hi = plane_cols[name]
-            return slice(lo // 4, hi // 4)
+        plane_at = {
+            "wrr": (planes1, 0), "wri": (planes1, R), "wer": (planes1, 2 * R), "wei": (planes1, 3 * R),
+            "nr": (planes2, 0), "ni": (planes2, N),
+        }
 
         def plane(name, lo, hi):
-            base = plane_cols[name][0]
-            return planes[:].bitcast(U8)[:, base + lo : base + hi]
+            tile, base = plane_at[name]
+            return tile[:, 0, :].bitcast(U8)[:, base + lo : base + hi]
 
-        def load_words(tile, words):
+        def load_words(queue, tile, words):
             src = words[0]
             if len(src.shape) == 3:
                 src = src.rearrange("p n t -> p (n t)")
-            nc.sync.dma_start(out=tile[:], in_=src.bitcast(I32))
+            queue.dma_start(out=tile[:], in_=src.bitcast(I32))
 
-        def load_scales(queue, tile, cols, scales, rows=range(4)):
+        def load_table_scales(queue, tile, scales):
             by_row = scales[0].bitcast(I32).rearrange("(q r) n -> r q n", r=4)
-            for r in rows:
-                queue.dma_start(out=tile[r:P:32, cols], in_=by_row[r])
+            for r in range(4):
+                queue.dma_start(out=tile[r:P:32, :], in_=by_row[r])
 
-        whole = slice(0, T // 4)
-        nc.vector.memset(tab2_s[:], 0)
+        def stage_scales(queue, name, scales):
+            tile, base = plane_at[name]
+            by_quadrant = scales[0].bitcast(I32).rearrange("(q r) n -> q r n", r=4)
+            width = by_quadrant.shape[2]
+            queue.dma_start(out=tile[0:P:32, :, base // 4 : base // 4 + width], in_=by_quadrant)
+
+        def spread_scales(queue, tile):
+            for r in range(1, 4):
+                queue.dma_start(out=tile[r:P:32, 0, :], in_=tile[0:P:32, r, :])
+
+        nc.gpsimd.memset(tab2_s[:], 0)
+        nc.vector.memset(planes1[:, 0, :], 0)
         nc.vector.memset(tab1_s[:], 0)
-        nc.gpsimd.memset(planes[:], 0)
-        make_identity(nc, ident[:])
+        nc.vector.memset(planes2[:, 0, :], 0)
 
         nc.sync.dma_start(list2[:], offs2)
-        load_scales(nc.sync, tab2_s, whole, tab2_scales)
+        load_table_scales(nc.sync, tab2_s, tab2_scales)
         nc.sync.dma_start(list1[:], offs)
-        load_words(tab2_w, tab2_words)
-        load_scales(nc.sync, tab1_s, whole, tab_scales)
-        load_words(tab1_w, tab_words)
-        load_words(wrr_w, wrr_words)
-        load_words(wri_w, wri_words)
-        load_scales(nc.scalar, planes, plane_words("wrr"), wrr_scales)
-        load_scales(nc.scalar, planes, plane_words("wri"), wri_scales)
-        load_words(wer_w, wer_words)
-        load_words(wei_w, wei_words)
-        load_scales(nc.scalar, planes, plane_words("wer"), wer_scales)
-        load_scales(nc.scalar, planes, plane_words("wei"), wei_scales)
-        load_words(nr_w, nr_words)
-        load_words(ni_w, ni_words)
-        load_scales(nc.sync, planes, plane_words("nr"), nr_scales)
-        load_scales(nc.sync, planes, plane_words("ni"), ni_scales)
+        load_words(nc.sync, tab2_w, tab2_words)
+        stage_scales(nc.gpsimd, "wrr", wrr_scales)
+        stage_scales(nc.gpsimd, "wri", wri_scales)
+        stage_scales(nc.gpsimd, "wer", wer_scales)
+        stage_scales(nc.gpsimd, "wei", wei_scales)
+        load_table_scales(nc.sync, tab1_s, tab_scales)
+        load_words(nc.sync, wrr_w, wrr_words)
+        load_words(nc.sync, wri_w, wri_words)
+        load_words(nc.sync, tab1_w, tab_words)
+        spread_scales(nc.sync, planes1)
+        load_words(nc.sync, wer_w, wer_words)
+        load_words(nc.sync, wei_w, wei_words)
+        make_identity(nc, ident[:])
+        stage_scales(nc.gpsimd, "nr", nr_scales)
+        stage_scales(nc.gpsimd, "ni", ni_scales)
+        load_words(nc.sync, nr_w, nr_words)
+        load_words(nc.sync, ni_w, ni_words)
+        spread_scales(nc.sync, planes2)
 
         def gather(table, view, offsets, chunk, c, name):
             picked = keep.tile([P, chunk], view, name=name + str(c), align_bytes=64)
@@ -107,11 +115,11 @@ def tile_list_ckg_none_kernel(
         s1, s2, w1, w2 = {}, {}, {}, {}
         for c in range(J // SCALE_CHUNK):
             s2[c] = gather(tab2_s, U8, list2, SCALE_CHUNK, c, "s2_")
-        for c in range(J // SCALE_CHUNK):
-            s1[c] = gather(tab1_s, U8, list1, SCALE_CHUNK, c, "s1_")
+        for c in range(J // WORD_CHUNK):
+            w2[c] = gather(tab2_w, U32, list2, WORD_CHUNK, c, "w2_")
 
         def gather_words(c):
-            w2[c] = gather(tab2_w, U32, list2, WORD_CHUNK, c, "w2_")
+            s1[c] = gather(tab1_s, U8, list1, SCALE_CHUNK, c, "s1_")
             w1[c] = gather(tab1_w, U32, list1, WORD_CHUNK, c, "w1_")
 
         def project(i, codes, scales, weight, fmt, name, tag, bufs):

@@ -15,12 +15,12 @@ U8 = mybir.dt.uint8
 FP8X4 = mybir.dt.float8_e4m3fn_x4
 FP4X4 = mybir.dt.float4_e2m1fn_x4
 MULT = mybir.AluOpType.mult
+SUBTRACT = mybir.AluOpType.subtract
 
 P = 128
 PACK = 4
 TILES = J // P
-WORD_CHUNK = 256
-SCALE_CHUNK = 256
+CHUNK = 256
 
 
 def tile_list_ckg_none_kernel(
@@ -48,6 +48,7 @@ def tile_list_ckg_none_kernel(
         planes1 = keep.tile([P, 4, R], I32, name="planes1", align_bytes=64)
         planes2 = keep.tile([P, 4, N // 2], I32, name="planes2", align_bytes=64)
         ident = keep.tile([P, P], F32, name="ident")
+        ident16 = keep.tile([P, P], BF16, name="ident16")
 
         plane_at = {
             "wrr": (planes1, 0), "wri": (planes1, R), "wer": (planes1, 2 * R), "wei": (planes1, 3 * R),
@@ -64,10 +65,10 @@ def tile_list_ckg_none_kernel(
                 src = src.rearrange("p n t -> p (n t)")
             queue.dma_start(out=tile[:], in_=src.bitcast(I32))
 
-        def load_table_scales(queue, tile, scales):
+        def load_table_scales(tile, scales):
             by_row = scales[0].bitcast(I32).rearrange("(q r) n -> r q n", r=4)
             for r in range(4):
-                queue.dma_start(out=tile[r:P:32, :], in_=by_row[r])
+                (nc.sync, nc.scalar)[r % 2].dma_start(out=tile[r:P:32, :], in_=by_row[r])
 
         def stage_scales(queue, name, scales):
             tile, base = plane_at[name]
@@ -84,52 +85,50 @@ def tile_list_ckg_none_kernel(
         nc.vector.memset(tab1_s[:], 0)
         nc.vector.memset(planes2[:, 0, :], 0)
 
-        nc.sync.dma_start(list2[:], offs2)
-        load_table_scales(nc.sync, tab2_s, tab2_scales)
-        nc.sync.dma_start(list1[:], offs)
-        load_words(nc.sync, tab2_w, tab2_words)
-        stage_scales(nc.gpsimd, "wrr", wrr_scales)
-        stage_scales(nc.gpsimd, "wri", wri_scales)
-        stage_scales(nc.gpsimd, "wer", wer_scales)
-        stage_scales(nc.gpsimd, "wei", wei_scales)
-        load_table_scales(nc.sync, tab1_s, tab_scales)
-        load_words(nc.sync, wrr_w, wrr_words)
-        load_words(nc.sync, wri_w, wri_words)
-        load_words(nc.sync, tab1_w, tab_words)
-        spread_scales(nc.sync, planes1)
-        load_words(nc.sync, wer_w, wer_words)
-        load_words(nc.sync, wei_w, wei_words)
+        load_words(nc.gpsimd, tab2_w, tab2_words)
+        load_words(nc.gpsimd, tab1_w, tab_words)
+        load_words(nc.gpsimd, wer_w, wer_words)
+        load_words(nc.gpsimd, wei_w, wei_words)
         make_identity(nc, ident[:])
-        stage_scales(nc.gpsimd, "nr", nr_scales)
-        stage_scales(nc.gpsimd, "ni", ni_scales)
-        load_words(nc.sync, nr_w, nr_words)
-        load_words(nc.sync, ni_w, ni_words)
+        make_identity(nc, ident16[:])
+        load_words(nc.gpsimd, nr_w, nr_words)
+        load_words(nc.gpsimd, ni_w, ni_words)
+        nc.sync.dma_start(list2[:], offs2)
+        load_words(nc.scalar, wrr_w, wrr_words)
+        load_table_scales(tab2_s, tab2_scales)
+        nc.sync.dma_start(list1[:], offs)
+        load_words(nc.scalar, wri_w, wri_words)
+        stage_scales(nc.sync, "wrr", wrr_scales)
+        stage_scales(nc.scalar, "wri", wri_scales)
+        stage_scales(nc.sync, "wer", wer_scales)
+        stage_scales(nc.scalar, "wei", wei_scales)
+        load_table_scales(tab1_s, tab_scales)
+        spread_scales(nc.sync, planes1)
+        stage_scales(nc.scalar, "nr", nr_scales)
+        stage_scales(nc.scalar, "ni", ni_scales)
         spread_scales(nc.sync, planes2)
 
-        def gather(table, view, offsets, chunk, c, name):
-            picked = keep.tile([P, chunk], view, name=name + str(c), align_bytes=64)
-            cols = slice(c * chunk // 16, (c + 1) * chunk // 16)
-            nc.vector.tensor_copy(picked[:], table[:].bitcast(view).indirect(offsets[:, cols]))
-            return picked
+        def gather(table, view, offsets, lo, hi, name):
+            picked = keep.tile([P, hi - lo], view, name=name + str(lo), align_bytes=64)
+            nc.vector.tensor_copy(picked[:], table[:].bitcast(view).indirect(offsets[:, lo // 16 : hi // 16]))
+            return {i: picked[:, i * P - lo : (i + 1) * P - lo] for i in range(lo // P, hi // P)}
 
-        s1, s2, w1, w2 = {}, {}, {}, {}
-        for c in range(J // SCALE_CHUNK):
-            s2[c] = gather(tab2_s, U8, list2, SCALE_CHUNK, c, "s2_")
-        for c in range(J // WORD_CHUNK):
-            w2[c] = gather(tab2_w, U32, list2, WORD_CHUNK, c, "w2_")
+        s1, w1 = {}, {}
+        s2 = gather(tab2_s, U8, list2, 0, J, "s2_")
+        w2 = gather(tab2_w, U32, list2, 0, CHUNK, "w2_")
 
-        def gather_words(c):
-            s1[c] = gather(tab1_s, U8, list1, SCALE_CHUNK, c, "s1_")
-            w1[c] = gather(tab1_w, U32, list1, WORD_CHUNK, c, "w1_")
+        def gather_entity_scales(c):
+            s1.update(gather(tab1_s, U8, list1, c * CHUNK, (c + 1) * CHUNK, "s1_"))
+
+        def gather_entity_words(c):
+            w1.update(gather(tab1_w, U32, list1, c * CHUNK, (c + 1) * CHUNK, "w1_"))
 
         def project(i, codes, scales, weight, fmt, name, tag, bufs):
             acc = psum.tile([P, R], F32, name=tag, bufs=bufs)
-            c, lo = divmod(i * P, WORD_CHUNK)
-            cs, los = divmod(i * P, SCALE_CHUNK)
             nc.tensor.matmul_mx(
                 out=acc[:],
-                lhsT=codes[c][:, lo : lo + P].bitcast(FP8X4),
-                lhsT_scale=scales[cs][:, los : los + P],
+                lhsT=codes[i].bitcast(FP8X4),
+                lhsT_scale=scales[i],
                 rhs=weight[:].bitcast(fmt),
                 rhs_scale=plane(name, 0, R),
                 start=True,
@@ -137,13 +136,13 @@ def tile_list_ckg_none_kernel(
             )
             return acc[:].rearrange("j (m t) -> j t m", t=PACK)
 
-        aer, aei, arr, ari, hq = {}, {}, {}, {}, {}
+        aer, aei, rel, hq = {}, {}, {}, {}
 
         def relation(i):
-            for store, weight, name in ((arr, wrr_w, "wrr"), (ari, wri_w, "wri")):
+            rel[i] = ring.tile([P, 2, PACK, P], F32, name="rel_sb")
+            for part, weight, name in ((0, wrr_w, "wrr"), (1, wri_w, "wri")):
                 acc = project(i, w2, s2, weight, FP4X4, name, "rel", 2)
-                store[i] = ring.tile([P, PACK, P], F32, name="sb_" + name)
-                nc.scalar.copy(out=store[i][:], in_=acc)
+                nc.scalar.copy(out=rel[i][:, part], in_=acc)
 
         def entity_real(i):
             aer[i] = project(i, w1, s1, wer_w, FP8X4, "wer", "ent", 3)
@@ -151,40 +150,42 @@ def tile_list_ckg_none_kernel(
         def entity_imag(i):
             aei[i] = project(i, w1, s1, wei_w, FP8X4, "wei", "ent", 3)
 
-        def product(ent, rel, name, negate=False):
-            prod = ring.tile([P, PACK, P], F32, name=name, bufs=2)
-            if negate:
-                nc.vector.scalar_tensor_tensor(out=prod[:], in0=ent, scalar=-1.0, in1=rel[:], op0=MULT, op1=MULT)
-            else:
-                nc.vector.tensor_tensor(out=prod[:], in0=ent, in1=rel[:], op=MULT)
-            return prod
+        def hq_tile(i):
+            if i not in hq:
+                hq[i] = ring.tile([P, 2, P, PACK], BF16, name="hq", align_bytes=64)
+            return hq[i]
 
         def turn_and_add(i, part, first, second):
-            turned = psum.tile([P, PACK, P], F32, name="turned", bufs=2)
+            turned = psum.tile([P, PACK, P], F32, name="turned" + str(part), bufs=1)
             for t in range(PACK):
                 nc.tensor.matmul(out=turned[:, t, :], lhsT=first[:, t, :], rhs=ident[:], is_transpose=True, start=True, stop=False)
                 nc.tensor.matmul(out=turned[:, t, :], lhsT=second[:, t, :], rhs=ident[:], is_transpose=True, start=False, stop=True)
-            hq[i, part] = ring.tile([P, P, PACK], BF16, name="hq" + part, align_bytes=64)
-            nc.scalar.copy(out=hq[i, part][:], in_=turned[:].rearrange("p t j -> p j t"))
+            nc.scalar.copy(out=hq_tile(i)[:, part], in_=turned[:].rearrange("p t j -> p j t"))
+
+        def subtract_and_turn(i, part, first, second):
+            diff = ring.tile([P, PACK, P], BF16, name="diff", bufs=2)
+            nc.gpsimd.tensor_tensor(out=diff[:], in0=first, in1=second, op=SUBTRACT)
+            turned = psum.tile([P, PACK, P], BF16, name="turned" + str(part), bufs=1)
+            for t in range(PACK):
+                nc.tensor.transpose(turned[:, t, :], diff[:, t, :], ident16[:])
+            nc.scalar.copy(out=hq_tile(i)[:, part], in_=turned[:].rearrange("p t j -> p j t"))
 
         def score(i):
-            codes, scales = {}, {}
-            for part in "ri":
-                codes[part] = ring.tile([P, P], U32, name="hc" + part, align_bytes=64)
-                scales[part] = ring.tile([P, P], U8, name="hs" + part, align_bytes=64)
-                nc.vector.quantize_mx(
-                    out=codes[part][:].bitcast(FP8X4),
-                    scales=scales[part][:],
-                    in_=hq[i, part][:].rearrange("p j t -> p (j t)"),
-                )
+            codes = ring.tile([P, 2 * P], U32, name="h_codes", align_bytes=64)
+            scales = ring.tile([P, 2 * P], U8, name="h_scales", align_bytes=64)
+            nc.vector.quantize_mx(
+                out=codes[:].bitcast(FP8X4),
+                scales=scales[:],
+                in_=hq[i][:].rearrange("p c j t -> p (c j t)"),
+            )
             y = psum.tile([P, N // P, P], F32, name="y", bufs=1)
             for h in range(N // P):
                 nc.tensor.matmul_mx(
                     out=y[:, h, :],
                     lhsT=nr_w[:, h * P : (h + 1) * P].bitcast(FP8X4),
                     lhsT_scale=plane("nr", h * P, (h + 1) * P),
-                    rhs=codes["r"][:].bitcast(FP8X4),
-                    rhs_scale=scales["r"][:],
+                    rhs=codes[:, 0:P].bitcast(FP8X4),
+                    rhs_scale=scales[:, 0:P],
                     start=True,
                     stop=False,
                 )
@@ -192,8 +193,8 @@ def tile_list_ckg_none_kernel(
                     out=y[:, h, :],
                     lhsT=ni_w[:, h * P // 2 : (h + 1) * P // 2].bitcast(FP4X4),
                     lhsT_scale=plane("ni", h * P, (h + 1) * P),
-                    rhs=codes["i"][:].bitcast(FP8X4),
-                    rhs_scale=scales["i"][:],
+                    rhs=codes[:, P : 2 * P].bitcast(FP8X4),
+                    rhs_scale=scales[:, P : 2 * P],
                     start=False,
                     stop=True,
                 )
@@ -203,28 +204,43 @@ def tile_list_ckg_none_kernel(
                 out=out[:, i * P : (i + 1) * P].rearrange("(h p) j -> p h j", p=P), in_=y_sb[:]
             )
 
-        tiles_per_chunk = WORD_CHUNK // P
-        gather_words(0)
-        gather_words(1)
+        gather_entity_scales(0)
+        gather_entity_words(0)
+        w2.update(gather(tab2_w, U32, list2, CHUNK, J, "w2_"))
+        gather_entity_scales(1)
+        gather_entity_words(1)
+        late_gathers = [(gather_entity_scales, 2), (gather_entity_words, 2), (gather_entity_scales, 3), (gather_entity_words, 3)]
         relation(0)
         entity_real(0)
         entity_imag(0)
         relation(1)
         entity_real(1)
         for i in range(TILES):
-            p1 = product(aer[i], arr[i], "p1")
-            p2 = product(aei[i], ari[i], "p2", negate=True)
-            turn_and_add(i, "r", p1, p2)
-            if i > 0:
-                score(i - 1)
-            p3 = product(aer[i], ari[i], "p3")
-            if i + 1 < TILES:
+            last = i == TILES - 1
+            by_real = ring.tile([P, 2, PACK, P], F32, name="by_real", bufs=2)
+            nc.vector.tensor_tensor(
+                out=by_real[:], in0=aer[i].unsqueeze(1).to_broadcast([P, 2, PACK, P]), in1=rel[i][:], op=MULT
+            )
+            if i >= 2:
+                score(i - 2)
+            if i < len(late_gathers):
+                late_gathers[i][0](late_gathers[i][1])
+            imag_imag = ring.tile([P, PACK, P], F32, name="imag_imag", bufs=2)
+            imag_real = ring.tile([P, PACK, P], F32, name="imag_real", bufs=2)
+            if last:
+                nc.vector.scalar_tensor_tensor(
+                    out=imag_imag[:], in0=aei[i], scalar=-1.0, in1=rel[i][:, 1], op0=MULT, op1=MULT
+                )
+                turn_and_add(i, 0, by_real[:, 0], imag_imag)
+            else:
+                nc.vector.tensor_tensor(out=imag_imag[:], in0=aei[i], in1=rel[i][:, 1], op=MULT)
+            nc.vector.tensor_tensor(out=imag_real[:], in0=aei[i], in1=rel[i][:, 0], op=MULT)
+            turn_and_add(i, 1, by_real[:, 1], imag_real)
+            if not last:
+                subtract_and_turn(i, 0, by_real[:, 0], imag_imag[:])
                 entity_imag(i + 1)
-            p4 = product(aei[i], arr[i], "p4")
-            turn_and_add(i, "i", p3, p4)
-            if i % tiles_per_chunk == 0 and i // tiles_per_chunk + 2 < J // WORD_CHUNK:
-                gather_words(i // tiles_per_chunk + 2)
             if i + 2 < TILES:
                 entity_real(i + 2)
                 relation(i + 2)
+        score(TILES - 2)
         score(TILES - 1)

@@ -15,7 +15,6 @@ U8 = mybir.dt.uint8
 FP8X4 = mybir.dt.float8_e4m3fn_x4
 FP4X4 = mybir.dt.float4_e2m1fn_x4
 MULT = mybir.AluOpType.mult
-SUBTRACT = mybir.AluOpType.subtract
 
 P = 128
 PACK = 4
@@ -45,19 +44,21 @@ def tile_list_ckg_none_kernel(
         wri_w = keep.tile([P, R // 2], I32, name="wri_w", align_bytes=64)
         nr_w = keep.tile([P, N], I32, name="nr_w", align_bytes=64)
         ni_w = keep.tile([P, N // 2], I32, name="ni_w", align_bytes=64)
-        planes1 = keep.tile([P, 4, R], I32, name="planes1", align_bytes=64)
-        planes2 = keep.tile([P, 4, N // 2], I32, name="planes2", align_bytes=64)
+        staged1 = keep.tile([P, 4, R], I32, name="staged1", align_bytes=64)
+        staged2 = keep.tile([P, 4, N // 2], I32, name="staged2", align_bytes=64)
+        planes1 = keep.tile([P, R], I32, name="planes1", align_bytes=64)
+        planes2 = keep.tile([P, N // 2], I32, name="planes2", align_bytes=64)
         ident = keep.tile([P, P], F32, name="ident")
-        ident16 = keep.tile([P, P], BF16, name="ident16")
 
         plane_at = {
-            "wrr": (planes1, 0), "wri": (planes1, R), "wer": (planes1, 2 * R), "wei": (planes1, 3 * R),
-            "nr": (planes2, 0), "ni": (planes2, N),
+            "wrr": (staged1, planes1, 0), "wri": (staged1, planes1, R),
+            "wer": (staged1, planes1, 2 * R), "wei": (staged1, planes1, 3 * R),
+            "nr": (staged2, planes2, 0), "ni": (staged2, planes2, N),
         }
 
         def plane(name, lo, hi):
-            tile, base = plane_at[name]
-            return tile[:, 0, :].bitcast(U8)[:, base + lo : base + hi]
+            tile, base = plane_at[name][1:]
+            return tile[:].bitcast(U8)[:, base + lo : base + hi]
 
         def load_words(queue, tile, words):
             src = words[0]
@@ -71,57 +72,63 @@ def tile_list_ckg_none_kernel(
                 (nc.sync, nc.scalar)[r % 2].dma_start(out=tile[r:P:32, :], in_=by_row[r])
 
         def stage_scales(queue, name, scales):
-            tile, base = plane_at[name]
+            tile, base = plane_at[name][0], plane_at[name][2]
             by_quadrant = scales[0].bitcast(I32).rearrange("(q r) n -> q r n", r=4)
             width = by_quadrant.shape[2]
             queue.dma_start(out=tile[0:P:32, :, base // 4 : base // 4 + width], in_=by_quadrant)
 
-        def spread_scales(queue, tile):
-            for r in range(1, 4):
-                queue.dma_start(out=tile[r:P:32, 0, :], in_=tile[0:P:32, r, :])
+        def spread_scales(queues, planes, staged):
+            for r in range(4):
+                queues[r % len(queues)].dma_start(out=planes[r:P:32, :], in_=staged[0:P:32, r, :])
 
-        nc.gpsimd.memset(tab2_s[:], 0)
-        nc.vector.memset(planes1[:, 0, :], 0)
-        nc.vector.memset(tab1_s[:], 0)
-        nc.vector.memset(planes2[:, 0, :], 0)
-
+        nc.vector.memset(tab2_s[:], 0)
+        nc.vector.memset(planes1[:], 0)
+        nc.vector.memset(planes2[:], 0)
+        stage_scales(nc.gpsimd, "wei", wei_scales)
         load_words(nc.gpsimd, tab2_w, tab2_words)
+        make_identity(nc, ident[:])
+        nc.gpsimd.memset(tab1_s[:], 0)
         load_words(nc.gpsimd, tab1_w, tab_words)
         load_words(nc.gpsimd, wer_w, wer_words)
         load_words(nc.gpsimd, wei_w, wei_words)
-        make_identity(nc, ident[:])
-        make_identity(nc, ident16[:])
+        stage_scales(nc.gpsimd, "nr", nr_scales)
+        stage_scales(nc.gpsimd, "ni", ni_scales)
         load_words(nc.gpsimd, nr_w, nr_words)
         load_words(nc.gpsimd, ni_w, ni_words)
+
         nc.sync.dma_start(list2[:], offs2)
-        load_words(nc.scalar, wrr_w, wrr_words)
         load_table_scales(tab2_s, tab2_scales)
-        nc.sync.dma_start(list1[:], offs)
-        load_words(nc.scalar, wri_w, wri_words)
-        stage_scales(nc.sync, "wrr", wrr_scales)
+        stage_scales(nc.scalar, "wrr", wrr_scales)
         stage_scales(nc.scalar, "wri", wri_scales)
         stage_scales(nc.sync, "wer", wer_scales)
-        stage_scales(nc.scalar, "wei", wei_scales)
+        spread_scales((nc.sync, nc.scalar), planes1, staged1)
+        nc.sync.dma_start(list1[:], offs)
+        load_words(nc.scalar, wrr_w, wrr_words)
+        load_words(nc.scalar, wri_w, wri_words)
         load_table_scales(tab1_s, tab_scales)
-        spread_scales(nc.sync, planes1)
-        stage_scales(nc.scalar, "nr", nr_scales)
-        stage_scales(nc.scalar, "ni", ni_scales)
-        spread_scales(nc.sync, planes2)
+        spread_scales((nc.sync,), planes2, staged2)
 
-        def gather(table, view, offsets, lo, hi, name):
-            picked = keep.tile([P, hi - lo], view, name=name + str(lo), align_bytes=64)
+        def gather(picked, table, view, offsets, lo, hi):
             nc.vector.tensor_copy(picked[:], table[:].bitcast(view).indirect(offsets[:, lo // 16 : hi // 16]))
             return {i: picked[:, i * P - lo : (i + 1) * P - lo] for i in range(lo // P, hi // P)}
 
         s1, w1 = {}, {}
-        s2 = gather(tab2_s, U8, list2, 0, J, "s2_")
-        w2 = gather(tab2_w, U32, list2, 0, CHUNK, "w2_")
+        s2_all = keep.tile([P, J], U8, name="s2_all", align_bytes=64)
+        w2_head = keep.tile([P, CHUNK], U32, name="w2_head", align_bytes=64)
+        w2_rest = keep.tile([P, J - CHUNK], U32, name="w2_rest", align_bytes=64)
+        s2 = gather(s2_all, tab2_s, U8, list2, 0, J)
+        w2 = gather(w2_head, tab2_w, U32, list2, 0, CHUNK)
+        w2.update(gather(w2_rest, tab2_w, U32, list2, CHUNK, J))
+
+        def gather_entity(found, table, view, name, c):
+            picked = ring.tile([P, CHUNK], view, name=name, bufs=2, align_bytes=64)
+            found.update(gather(picked, table, view, list1, c * CHUNK, (c + 1) * CHUNK))
 
         def gather_entity_scales(c):
-            s1.update(gather(tab1_s, U8, list1, c * CHUNK, (c + 1) * CHUNK, "s1_"))
+            gather_entity(s1, tab1_s, U8, "s1", c)
 
         def gather_entity_words(c):
-            w1.update(gather(tab1_w, U32, list1, c * CHUNK, (c + 1) * CHUNK, "w1_"))
+            gather_entity(w1, tab1_w, U32, "w1", c)
 
         def project(i, codes, scales, weight, fmt, name, tag, bufs):
             acc = psum.tile([P, R], F32, name=tag, bufs=bufs)
@@ -162,14 +169,6 @@ def tile_list_ckg_none_kernel(
                 nc.tensor.matmul(out=turned[:, t, :], lhsT=second[:, t, :], rhs=ident[:], is_transpose=True, start=False, stop=True)
             nc.scalar.copy(out=hq_tile(i)[:, part], in_=turned[:].rearrange("p t j -> p j t"))
 
-        def subtract_and_turn(i, part, first, second):
-            diff = ring.tile([P, PACK, P], BF16, name="diff", bufs=2)
-            nc.gpsimd.tensor_tensor(out=diff[:], in0=first, in1=second, op=SUBTRACT)
-            turned = psum.tile([P, PACK, P], BF16, name="turned" + str(part), bufs=1)
-            for t in range(PACK):
-                nc.tensor.transpose(turned[:, t, :], diff[:, t, :], ident16[:])
-            nc.scalar.copy(out=hq_tile(i)[:, part], in_=turned[:].rearrange("p t j -> p j t"))
-
         def score(i):
             codes = ring.tile([P, 2 * P], U32, name="h_codes", align_bytes=64)
             scales = ring.tile([P, 2 * P], U8, name="h_scales", align_bytes=64)
@@ -204,43 +203,37 @@ def tile_list_ckg_none_kernel(
                 out=out[:, i * P : (i + 1) * P].rearrange("(h p) j -> p h j", p=P), in_=y_sb[:]
             )
 
-        gather_entity_scales(0)
-        gather_entity_words(0)
-        w2.update(gather(tab2_w, U32, list2, CHUNK, J, "w2_"))
-        gather_entity_scales(1)
-        gather_entity_words(1)
-        late_gathers = [(gather_entity_scales, 2), (gather_entity_words, 2), (gather_entity_scales, 3), (gather_entity_words, 3)]
+        for c in range(2):
+            gather_entity_scales(c)
+            gather_entity_words(c)
         relation(0)
         entity_real(0)
         entity_imag(0)
         relation(1)
         entity_real(1)
         for i in range(TILES):
-            last = i == TILES - 1
             by_real = ring.tile([P, 2, PACK, P], F32, name="by_real", bufs=2)
             nc.vector.tensor_tensor(
                 out=by_real[:], in0=aer[i].unsqueeze(1).to_broadcast([P, 2, PACK, P]), in1=rel[i][:], op=MULT
             )
-            if i >= 2:
-                score(i - 2)
-            if i < len(late_gathers):
-                late_gathers[i][0](late_gathers[i][1])
-            imag_imag = ring.tile([P, PACK, P], F32, name="imag_imag", bufs=2)
-            imag_real = ring.tile([P, PACK, P], F32, name="imag_real", bufs=2)
-            if last:
-                nc.vector.scalar_tensor_tensor(
-                    out=imag_imag[:], in0=aei[i], scalar=-1.0, in1=rel[i][:, 1], op0=MULT, op1=MULT
-                )
-                turn_and_add(i, 0, by_real[:, 0], imag_imag)
-            else:
-                nc.vector.tensor_tensor(out=imag_imag[:], in0=aei[i], in1=rel[i][:, 1], op=MULT)
-            nc.vector.tensor_tensor(out=imag_real[:], in0=aei[i], in1=rel[i][:, 0], op=MULT)
-            turn_and_add(i, 1, by_real[:, 1], imag_real)
-            if not last:
-                subtract_and_turn(i, 0, by_real[:, 0], imag_imag[:])
+            if i + 1 < TILES:
                 entity_imag(i + 1)
             if i + 2 < TILES:
-                entity_real(i + 2)
                 relation(i + 2)
+            if i >= 2:
+                score(i - 2)
+            chunk = (i + 3) // 2
+            if i >= 1 and chunk < J // CHUNK:
+                (gather_entity_words, gather_entity_scales)[i % 2](chunk)
+            imag_imag = ring.tile([P, PACK, P], F32, name="imag_imag", bufs=2)
+            imag_real = ring.tile([P, PACK, P], F32, name="imag_real", bufs=2)
+            nc.vector.scalar_tensor_tensor(
+                out=imag_imag[:], in0=aei[i], scalar=-1.0, in1=rel[i][:, 1], op0=MULT, op1=MULT
+            )
+            nc.vector.tensor_tensor(out=imag_real[:], in0=aei[i], in1=rel[i][:, 0], op=MULT)
+            turn_and_add(i, 0, by_real[:, 0], imag_imag)
+            turn_and_add(i, 1, by_real[:, 1], imag_real)
+            if i + 2 < TILES:
+                entity_real(i + 2)
         score(TILES - 2)
         score(TILES - 1)

@@ -20,6 +20,8 @@ P = 128
 PACK = 4
 TILES = J // P
 CHUNK = 256
+PARTS = ((0, CHUNK), (CHUNK, J))
+ROWS = 16
 
 
 def tile_list_ckg_none_kernel(
@@ -29,6 +31,7 @@ def tile_list_ckg_none_kernel(
     nc = tc.nc
     with ExitStack() as ctx:
         keep = ctx.enter_context(tc.tile_pool(name="keep", bufs=1))
+        second = ctx.enter_context(tc.tile_pool(name="second", bufs=1))
         ring = ctx.enter_context(tc.tile_pool(name="ring", bufs=3))
         psum = ctx.enter_context(tc.psum_pool(name="psum", bufs=1))
 
@@ -38,14 +41,19 @@ def tile_list_ckg_none_kernel(
         tab2_w = keep.tile([P, T], I32, name="tab2_w", align_bytes=64)
         tab1_s = keep.tile([P, T // 4], I32, name="tab1_s", align_bytes=64)
         tab2_s = keep.tile([P, T // 4], I32, name="tab2_s", align_bytes=64)
+        staged1 = keep.tile([P, R], I32, name="staged1", align_bytes=64)
         wer_w = keep.tile([P, R], I32, name="wer_w", align_bytes=64)
         wei_w = keep.tile([P, R], I32, name="wei_w", align_bytes=64)
         wrr_w = keep.tile([P, R // 2], I32, name="wrr_w", align_bytes=64)
         wri_w = keep.tile([P, R // 2], I32, name="wri_w", align_bytes=64)
-        nr_w = keep.tile([P, N], I32, name="nr_w", align_bytes=64)
-        ni_w = keep.tile([P, N // 2], I32, name="ni_w", align_bytes=64)
-        staged1 = keep.tile([P, 4, R], I32, name="staged1", align_bytes=64)
-        staged2 = keep.tile([P, 4, N // 2], I32, name="staged2", align_bytes=64)
+        picked_s = [
+            keep.tile([P, 2 * CHUNK], U8, name="picked_s0", align_bytes=64),
+            second.tile([P, 2 * (J - CHUNK)], U8, name="picked_s1", align_bytes=64, offset=2 * N),
+        ]
+        nr_w = second.tile([P, N], I32, name="nr_w", align_bytes=64, offset=0)
+        staged2 = second.tile([P, N // 2], I32, name="staged2", align_bytes=64, offset=4 * N)
+        ni_w = second.tile([P, N // 2], I32, name="ni_w", align_bytes=64, offset=6 * N)
+        planes_t = [keep.tile([P, (hi - lo) // 2], I32, name="planes_t" + str(lo), align_bytes=64) for lo, hi in PARTS]
         planes1 = keep.tile([P, R], I32, name="planes1", align_bytes=64)
         planes2 = keep.tile([P, N // 2], I32, name="planes2", align_bytes=64)
         ident = keep.tile([P, P], F32, name="ident")
@@ -66,69 +74,79 @@ def tile_list_ckg_none_kernel(
                 src = src.rearrange("p n t -> p (n t)")
             queue.dma_start(out=tile[:], in_=src.bitcast(I32))
 
-        def load_table_scales(tile, scales):
-            by_row = scales[0].bitcast(I32).rearrange("(q r) n -> r q n", r=4)
-            for r in range(4):
-                (nc.sync, nc.scalar)[r % 2].dma_start(out=tile[r:P:32, :], in_=by_row[r])
+        def load_table_half(tile, words, h):
+            src = words[0].rearrange("p n t -> p (n t)").bitcast(I32)
+            nc.gpsimd.dma_start(out=tile[:, h * T // 2 : (h + 1) * T // 2], in_=src[:, h * T // 2 : (h + 1) * T // 2])
+
+        def load_table_scales(queue, tile, scales):
+            queue.dma_start(out=tile[0:ROWS, :], in_=scales[0].bitcast(I32))
 
         def stage_scales(queue, name, scales):
             tile, base = plane_at[name][0], plane_at[name][2]
-            by_quadrant = scales[0].bitcast(I32).rearrange("(q r) n -> q r n", r=4)
-            width = by_quadrant.shape[2]
-            queue.dma_start(out=tile[0:P:32, :, base // 4 : base // 4 + width], in_=by_quadrant)
+            rows = scales[0].bitcast(I32)
+            queue.dma_start(out=tile[0:ROWS, base // 4 : base // 4 + rows.shape[1]], in_=rows)
 
         def spread_scales(queues, planes, staged):
-            for r in range(4):
-                queues[r % len(queues)].dma_start(out=planes[r:P:32, :], in_=staged[0:P:32, r, :])
+            for q in range(4):
+                queues[q % len(queues)].dma_start(out=planes[32 * q : 32 * q + 4, :], in_=staged[4 * q : 4 * q + 4, :])
 
         nc.vector.memset(tab2_s[:], 0)
+        nc.vector.memset(tab1_s[:], 0)
         nc.vector.memset(planes1[:], 0)
+        nc.vector.memset(planes_t[0][:], 0)
+        nc.vector.memset(planes_t[1][:], 0)
         nc.vector.memset(planes2[:], 0)
-        stage_scales(nc.gpsimd, "wei", wei_scales)
-        load_words(nc.gpsimd, tab2_w, tab2_words)
-        make_identity(nc, ident[:])
-        nc.gpsimd.memset(tab1_s[:], 0)
-        load_words(nc.gpsimd, tab1_w, tab_words)
+        load_table_half(tab2_w, tab2_words, 0)
+        load_table_half(tab2_w, tab2_words, 1)
+        load_table_half(tab1_w, tab_words, 0)
+        load_table_half(tab1_w, tab_words, 1)
         load_words(nc.gpsimd, wer_w, wer_words)
         load_words(nc.gpsimd, wei_w, wei_words)
-        stage_scales(nc.gpsimd, "nr", nr_scales)
-        stage_scales(nc.gpsimd, "ni", ni_scales)
-        load_words(nc.gpsimd, nr_w, nr_words)
-        load_words(nc.gpsimd, ni_w, ni_words)
+        make_identity(nc, ident[:])
 
         nc.sync.dma_start(list2[:], offs2)
-        load_table_scales(tab2_s, tab2_scales)
+        nc.sync.dma_start(list1[:], offs)
         stage_scales(nc.scalar, "wrr", wrr_scales)
         stage_scales(nc.scalar, "wri", wri_scales)
         stage_scales(nc.sync, "wer", wer_scales)
-        spread_scales((nc.sync, nc.scalar), planes1, staged1)
-        nc.sync.dma_start(list1[:], offs)
-        load_words(nc.scalar, wrr_w, wrr_words)
+        stage_scales(nc.scalar, "wei", wei_scales)
+        load_table_scales(nc.sync, tab2_s, tab2_scales)
+        load_table_scales(nc.scalar, tab1_s, tab_scales)
+        load_words(nc.sync, wrr_w, wrr_words)
         load_words(nc.scalar, wri_w, wri_words)
-        load_table_scales(tab1_s, tab_scales)
-        spread_scales((nc.sync,), planes2, staged2)
+        spread_scales((nc.sync, nc.scalar), planes1, staged1)
 
         def gather(picked, table, view, offsets, lo, hi):
-            nc.vector.tensor_copy(picked[:], table[:].bitcast(view).indirect(offsets[:, lo // 16 : hi // 16]))
-            return {i: picked[:, i * P - lo : (i + 1) * P - lo] for i in range(lo // P, hi // P)}
+            nc.vector.tensor_copy(picked, table[:].bitcast(view).indirect(offsets[:, lo // 16 : hi // 16]))
 
-        s1, w1 = {}, {}
-        s2_all = keep.tile([P, J], U8, name="s2_all", align_bytes=64)
-        w2_head = keep.tile([P, CHUNK], U32, name="w2_head", align_bytes=64)
-        w2_rest = keep.tile([P, J - CHUNK], U32, name="w2_rest", align_bytes=64)
-        s2 = gather(s2_all, tab2_s, U8, list2, 0, J)
-        w2 = gather(w2_head, tab2_w, U32, list2, 0, CHUNK)
-        w2.update(gather(w2_rest, tab2_w, U32, list2, CHUNK, J))
+        s1, s2, w1, w2 = {}, {}, {}, {}
+        for h in range(2):
+            lo, hi = PARTS[h]
+            width = hi - lo
+            gather(picked_s[h][:, 0:width], tab2_s, U8, list2, lo, hi)
+            gather(picked_s[h][:, width : 2 * width], tab1_s, U8, list1, lo, hi)
+            spread_scales((nc.sync,), planes_t[h], picked_s[h][:].bitcast(I32))
+            for i in range(lo // P, hi // P):
+                s2[i] = planes_t[h][:].bitcast(U8)[:, i * P - lo : (i + 1) * P - lo]
+                s1[i] = planes_t[h][:].bitcast(U8)[:, width + i * P - lo : width + (i + 1) * P - lo]
 
-        def gather_entity(found, table, view, name, c):
-            picked = ring.tile([P, CHUNK], view, name=name, bufs=2, align_bytes=64)
-            found.update(gather(picked, table, view, list1, c * CHUNK, (c + 1) * CHUNK))
+        stage_scales(nc.sync, "nr", nr_scales)
+        stage_scales(nc.sync, "ni", ni_scales)
+        load_words(nc.sync, nr_w, nr_words)
+        load_words(nc.sync, ni_w, ni_words)
+        spread_scales((nc.sync,), planes2, staged2)
 
-        def gather_entity_scales(c):
-            gather_entity(s1, tab1_s, U8, "s1", c)
+        def gather_words(found, table, offsets, name, c):
+            picked = ring.tile([P, CHUNK], U32, name=name, bufs=2, align_bytes=64)
+            gather(picked[:], table, U32, offsets, c * CHUNK, (c + 1) * CHUNK)
+            for i in range(2):
+                found[2 * c + i] = picked[:, i * P : (i + 1) * P]
 
-        def gather_entity_words(c):
-            gather_entity(w1, tab1_w, U32, "w1", c)
+        def gather_relation(c):
+            gather_words(w2, tab2_w, list2, "w2", c)
+
+        def gather_entity(c):
+            gather_words(w1, tab1_w, list1, "w1", c)
 
         def project(i, codes, scales, weight, fmt, name, tag, bufs):
             acc = psum.tile([P, R], F32, name=tag, bufs=bufs)
@@ -204,8 +222,9 @@ def tile_list_ckg_none_kernel(
             )
 
         for c in range(2):
-            gather_entity_scales(c)
-            gather_entity_words(c)
+            gather_relation(c)
+        for c in range(2):
+            gather_entity(c)
         relation(0)
         entity_real(0)
         entity_imag(0)
@@ -222,9 +241,9 @@ def tile_list_ckg_none_kernel(
                 relation(i + 2)
             if i >= 2:
                 score(i - 2)
-            chunk = (i + 3) // 2
-            if i >= 1 and chunk < J // CHUNK:
-                (gather_entity_words, gather_entity_scales)[i % 2](chunk)
+            chunk = (i + 4) // 2
+            if chunk < J // CHUNK:
+                (gather_relation, gather_entity)[i % 2](chunk)
             imag_imag = ring.tile([P, PACK, P], F32, name="imag_imag", bufs=2)
             imag_real = ring.tile([P, PACK, P], F32, name="imag_real", bufs=2)
             nc.vector.scalar_tensor_tensor(

@@ -31,6 +31,7 @@ def tile_list_ckg_none_kernel(
     nc = tc.nc
     with ExitStack() as ctx:
         keep = ctx.enter_context(tc.tile_pool(name="keep", bufs=1))
+        first = ctx.enter_context(tc.tile_pool(name="first", bufs=1))
         second = ctx.enter_context(tc.tile_pool(name="second", bufs=1))
         ring = ctx.enter_context(tc.tile_pool(name="ring", bufs=3))
         psum = ctx.enter_context(tc.psum_pool(name="psum", bufs=1))
@@ -41,13 +42,13 @@ def tile_list_ckg_none_kernel(
         tab2_w = keep.tile([P, T], I32, name="tab2_w", align_bytes=64)
         tab1_s = keep.tile([P, T // 4], I32, name="tab1_s", align_bytes=64)
         tab2_s = keep.tile([P, T // 4], I32, name="tab2_s", align_bytes=64)
-        staged1 = keep.tile([P, R], I32, name="staged1", align_bytes=64)
-        wer_w = keep.tile([P, R], I32, name="wer_w", align_bytes=64)
-        wei_w = keep.tile([P, R], I32, name="wei_w", align_bytes=64)
+        staged1 = first.tile([P, R], I32, name="staged1", align_bytes=64, offset=0)
+        wer_w = first.tile([P, R], I32, name="wer_w", align_bytes=64, offset=0)
+        wei_w = first.tile([P, R], I32, name="wei_w", align_bytes=64, offset=4 * R)
         wrr_w = keep.tile([P, R // 2], I32, name="wrr_w", align_bytes=64)
         wri_w = keep.tile([P, R // 2], I32, name="wri_w", align_bytes=64)
         picked_s = [
-            keep.tile([P, 2 * CHUNK], U8, name="picked_s0", align_bytes=64),
+            first.tile([P, 2 * CHUNK], U8, name="picked_s0", align_bytes=64, offset=4 * R),
             second.tile([P, 2 * (J - CHUNK)], U8, name="picked_s1", align_bytes=64, offset=2 * N),
         ]
         nr_w = second.tile([P, N], I32, name="nr_w", align_bytes=64, offset=0)
@@ -100,8 +101,6 @@ def tile_list_ckg_none_kernel(
         load_table_half(tab2_w, tab2_words, 1)
         load_table_half(tab1_w, tab_words, 0)
         load_table_half(tab1_w, tab_words, 1)
-        load_words(nc.gpsimd, wer_w, wer_words)
-        load_words(nc.gpsimd, wei_w, wei_words)
         make_identity(nc, ident[:])
 
         nc.sync.dma_start(list2[:], offs2)
@@ -115,6 +114,7 @@ def tile_list_ckg_none_kernel(
         load_words(nc.sync, wrr_w, wrr_words)
         load_words(nc.scalar, wri_w, wri_words)
         spread_scales((nc.sync, nc.scalar), planes1, staged1)
+        load_words(nc.scalar, wer_w, wer_words)
 
         def gather(picked, table, view, offsets, lo, hi):
             nc.vector.tensor_copy(picked, table[:].bitcast(view).indirect(offsets[:, lo // 16 : hi // 16]))
@@ -126,6 +126,8 @@ def tile_list_ckg_none_kernel(
             gather(picked_s[h][:, 0:width], tab2_s, U8, list2, lo, hi)
             gather(picked_s[h][:, width : 2 * width], tab1_s, U8, list1, lo, hi)
             spread_scales((nc.sync,), planes_t[h], picked_s[h][:].bitcast(I32))
+            if h == 0:
+                load_words(nc.sync, wei_w, wei_words)
             for i in range(lo // P, hi // P):
                 s2[i] = planes_t[h][:].bitcast(U8)[:, i * P - lo : (i + 1) * P - lo]
                 s1[i] = planes_t[h][:].bitcast(U8)[:, width + i * P - lo : width + (i + 1) * P - lo]
@@ -182,39 +184,39 @@ def tile_list_ckg_none_kernel(
 
         def turn_and_add(i, part, first, second):
             turned = psum.tile([P, PACK, P], F32, name="turned" + str(part), bufs=1)
-            for t in range(PACK):
-                nc.tensor.matmul(out=turned[:, t, :], lhsT=first[:, t, :], rhs=ident[:], is_transpose=True, start=True, stop=False)
-                nc.tensor.matmul(out=turned[:, t, :], lhsT=second[:, t, :], rhs=ident[:], is_transpose=True, start=False, stop=True)
+            for n, term in enumerate((first, second)):
+                for t in range(PACK):
+                    nc.tensor.matmul(
+                        out=turned[:, t, :], lhsT=term[:, t, :], rhs=ident[:], is_transpose=True,
+                        start=(n == 0 and t == 0), stop=(n == 1 and t == PACK - 1),
+                    )
             nc.scalar.copy(out=hq_tile(i)[:, part], in_=turned[:].rearrange("p t j -> p j t"))
 
-        def score(i):
+        def score(i, parts):
             codes = ring.tile([P, 2 * P], U32, name="h_codes", align_bytes=64)
             scales = ring.tile([P, 2 * P], U8, name="h_scales", align_bytes=64)
-            nc.vector.quantize_mx(
-                out=codes[:].bitcast(FP8X4),
-                scales=scales[:],
-                in_=hq[i][:].rearrange("p c j t -> p (c j t)"),
-            )
             y = psum.tile([P, N // P, P], F32, name="y", bufs=1)
-            for h in range(N // P):
-                nc.tensor.matmul_mx(
-                    out=y[:, h, :],
-                    lhsT=nr_w[:, h * P : (h + 1) * P].bitcast(FP8X4),
-                    lhsT_scale=plane("nr", h * P, (h + 1) * P),
-                    rhs=codes[:, 0:P].bitcast(FP8X4),
-                    rhs_scale=scales[:, 0:P],
-                    start=True,
-                    stop=False,
+            for lo, hi in parts:
+                nc.vector.quantize_mx(
+                    out=codes[:, lo * P : hi * P].bitcast(FP8X4),
+                    scales=scales[:, lo * P : hi * P],
+                    in_=hq[i][:, lo:hi].rearrange("p c j t -> p (c j t)"),
                 )
-                nc.tensor.matmul_mx(
-                    out=y[:, h, :],
-                    lhsT=ni_w[:, h * P // 2 : (h + 1) * P // 2].bitcast(FP4X4),
-                    lhsT_scale=plane("ni", h * P, (h + 1) * P),
-                    rhs=codes[:, P : 2 * P].bitcast(FP8X4),
-                    rhs_scale=scales[:, P : 2 * P],
-                    start=False,
-                    stop=True,
-                )
+                for c in range(lo, hi):
+                    for h in range(N // P):
+                        if c == 0:
+                            weight = nr_w[:, h * P : (h + 1) * P].bitcast(FP8X4)
+                        else:
+                            weight = ni_w[:, h * P // 2 : (h + 1) * P // 2].bitcast(FP4X4)
+                        nc.tensor.matmul_mx(
+                            out=y[:, h, :],
+                            lhsT=weight,
+                            lhsT_scale=plane(("nr", "ni")[c], h * P, (h + 1) * P),
+                            rhs=codes[:, c * P : (c + 1) * P].bitcast(FP8X4),
+                            rhs_scale=scales[:, c * P : (c + 1) * P],
+                            start=(c == 0 and h == 0),
+                            stop=(c == 1 and h == N // P - 1),
+                        )
             y_sb = ring.tile([P, N // P, P], F32, name="y_sb")
             nc.scalar.copy(out=y_sb[:], in_=y[:])
             nc.sync.dma_start(
@@ -230,29 +232,31 @@ def tile_list_ckg_none_kernel(
         entity_imag(0)
         relation(1)
         entity_real(1)
+        def product(name, entity, relation_part, sign):
+            made = ring.tile([P, PACK, P], F32, name=name, bufs=2)
+            if sign > 0:
+                nc.vector.tensor_tensor(out=made[:], in0=entity, in1=relation_part, op=MULT)
+            else:
+                nc.vector.scalar_tensor_tensor(out=made[:], in0=entity, scalar=-1.0, in1=relation_part, op0=MULT, op1=MULT)
+            return made
+
         for i in range(TILES):
-            by_real = ring.tile([P, 2, PACK, P], F32, name="by_real", bufs=2)
-            nc.vector.tensor_tensor(
-                out=by_real[:], in0=aer[i].unsqueeze(1).to_broadcast([P, 2, PACK, P]), in1=rel[i][:], op=MULT
-            )
+            if i >= 2:
+                score(i - 2, ((0, 2),))
+            real_real = product("real_real", aer[i], rel[i][:, 0], 1)
+            imag_imag = product("imag_imag", aei[i], rel[i][:, 1], -1)
+            turn_and_add(i, 0, real_real, imag_imag)
+            chunk = (i + 4) // 2
+            if chunk < J // CHUNK:
+                (gather_relation, gather_entity)[i % 2](chunk)
+            real_imag = product("real_imag", aer[i], rel[i][:, 1], 1)
             if i + 1 < TILES:
                 entity_imag(i + 1)
             if i + 2 < TILES:
                 relation(i + 2)
-            if i >= 2:
-                score(i - 2)
-            chunk = (i + 4) // 2
-            if chunk < J // CHUNK:
-                (gather_relation, gather_entity)[i % 2](chunk)
-            imag_imag = ring.tile([P, PACK, P], F32, name="imag_imag", bufs=2)
-            imag_real = ring.tile([P, PACK, P], F32, name="imag_real", bufs=2)
-            nc.vector.scalar_tensor_tensor(
-                out=imag_imag[:], in0=aei[i], scalar=-1.0, in1=rel[i][:, 1], op0=MULT, op1=MULT
-            )
-            nc.vector.tensor_tensor(out=imag_real[:], in0=aei[i], in1=rel[i][:, 0], op=MULT)
-            turn_and_add(i, 0, by_real[:, 0], imag_imag)
-            turn_and_add(i, 1, by_real[:, 1], imag_real)
+            imag_real = product("imag_real", aei[i], rel[i][:, 0], 1)
+            turn_and_add(i, 1, real_imag, imag_real)
             if i + 2 < TILES:
                 entity_real(i + 2)
-        score(TILES - 2)
-        score(TILES - 1)
+        score(TILES - 2, ((0, 2),))
+        score(TILES - 1, ((0, 1), (1, 2)))

@@ -161,7 +161,16 @@ def tile_list_ckg_none_kernel(
                 start=True,
                 stop=True,
             )
+            return acc
+
+        def by_slot(acc):
             return acc[:].rearrange("j (m t) -> j t m", t=PACK)
+
+        def bank_blocks(acc):
+            return acc[:].rearrange("j (b m t) -> j b t m", t=PACK, m=PACK)
+
+        def tile_blocks(part):
+            return part.rearrange("j t (b m) -> j b t m", m=PACK)
 
         aer, aei, rel, hq = {}, {}, {}, {}
 
@@ -169,7 +178,7 @@ def tile_list_ckg_none_kernel(
             rel[i] = ring.tile([P, 2, PACK, P], F32, name="rel_sb")
             for part, weight, name in ((0, wrr_w, "wrr"), (1, wri_w, "wri")):
                 acc = project(i, w2, s2, weight, FP4X4, name, "rel", 2)
-                nc.scalar.copy(out=rel[i][:, part], in_=acc)
+                nc.scalar.copy(out=tile_blocks(rel[i][:, part]), in_=bank_blocks(acc))
 
         def entity_real(i):
             aer[i] = project(i, w1, s1, wer_w, FP8X4, "wer", "ent", 3)
@@ -195,7 +204,10 @@ def tile_list_ckg_none_kernel(
         def score(i, parts):
             codes = ring.tile([P, 2 * P], U32, name="h_codes", align_bytes=64)
             scales = ring.tile([P, 2 * P], U8, name="h_scales", align_bytes=64)
-            y = psum.tile([P, N // P, P], F32, name="y", bufs=1)
+            if i < TILES - 2:
+                y = psum.tile([P, N // P, P], F32, name="y", bufs=1)
+            else:
+                y = psum.tile([P, N // P, P], F32, name="rel", bufs=2)
             for lo, hi in parts:
                 nc.vector.quantize_mx(
                     out=codes[:, lo * P : hi * P].bitcast(FP8X4),
@@ -235,13 +247,15 @@ def tile_list_ckg_none_kernel(
         def product(name, entity, relation_part, sign):
             made = ring.tile([P, PACK, P], F32, name=name, bufs=2)
             if sign > 0:
-                nc.vector.tensor_tensor(out=made[:], in0=entity, in1=relation_part, op=MULT)
+                nc.vector.tensor_tensor(
+                    out=tile_blocks(made[:]), in0=bank_blocks(entity), in1=tile_blocks(relation_part), op=MULT
+                )
             else:
-                nc.vector.scalar_tensor_tensor(out=made[:], in0=entity, scalar=-1.0, in1=relation_part, op0=MULT, op1=MULT)
+                nc.vector.scalar_tensor_tensor(out=made[:], in0=by_slot(entity), scalar=-1.0, in1=relation_part, op0=MULT, op1=MULT)
             return made
 
         for i in range(TILES):
-            if i >= 2:
+            if 2 <= i < TILES - 1:
                 score(i - 2, ((0, 2),))
             real_real = product("real_real", aer[i], rel[i][:, 0], 1)
             imag_imag = product("imag_imag", aei[i], rel[i][:, 1], -1)
@@ -258,5 +272,6 @@ def tile_list_ckg_none_kernel(
             turn_and_add(i, 1, real_imag, imag_real)
             if i + 2 < TILES:
                 entity_real(i + 2)
+        score(TILES - 3, ((0, 2),))
         score(TILES - 2, ((0, 2),))
         score(TILES - 1, ((0, 1), (1, 2)))

@@ -15,6 +15,7 @@ U8 = mybir.dt.uint8
 FP8X4 = mybir.dt.float8_e4m3fn_x4
 FP4X4 = mybir.dt.float4_e2m1fn_x4
 MULT = mybir.AluOpType.mult
+SUBTRACT = mybir.AluOpType.subtract
 
 P = 128
 PACK = 4
@@ -58,6 +59,7 @@ def tile_list_ckg_none_kernel(
         planes1 = keep.tile([P, R], I32, name="planes1", align_bytes=64)
         planes2 = keep.tile([P, N // 2], I32, name="planes2", align_bytes=64)
         ident = keep.tile([P, P], F32, name="ident")
+        ident_bf = keep.tile([P, P], BF16, name="ident_bf")
 
         plane_at = {
             "wrr": (staged1, planes1, 0), "wri": (staged1, planes1, R),
@@ -102,6 +104,7 @@ def tile_list_ckg_none_kernel(
         load_table_half(tab1_w, tab_words, 0)
         load_table_half(tab1_w, tab_words, 1)
         make_identity(nc, ident[:])
+        make_identity(nc, ident_bf[:])
 
         nc.sync.dma_start(list2[:], offs2)
         nc.sync.dma_start(list1[:], offs)
@@ -188,11 +191,14 @@ def tile_list_ckg_none_kernel(
 
         def hq_tile(i):
             if i not in hq:
-                hq[i] = ring.tile([P, 2, P, PACK], BF16, name="hq", align_bytes=64)
+                hq[i] = ring.tile([P, 2, P, PACK], BF16, name="hq", bufs=4, align_bytes=64)
             return hq[i]
 
         def turn_and_add(i, part, first, second):
-            turned = psum.tile([P, PACK, P], F32, name="turned" + str(part), bufs=1)
+            if part == 0:
+                turned = psum.tile([P, PACK, P], F32, name="rel", bufs=2)
+            else:
+                turned = psum.tile([P, PACK, P], F32, name="turned1", bufs=1)
             for n, term in enumerate((first, second)):
                 for t in range(PACK):
                     nc.tensor.matmul(
@@ -201,13 +207,26 @@ def tile_list_ckg_none_kernel(
                     )
             nc.scalar.copy(out=hq_tile(i)[:, part], in_=turned[:].rearrange("p t j -> p j t"))
 
+        def subtract(first, second):
+            hr = ring.tile([P, PACK, P], BF16, name="hr", bufs=2, align_bytes=64)
+            nc.gpsimd.tensor_tensor(out=hr[:], in0=first, in1=second, op=SUBTRACT)
+            return hr
+
+        def turn(i, hr):
+            turned = psum.tile([P, PACK, P], BF16, name="turned0", bufs=1)
+            for t in range(PACK):
+                nc.tensor.transpose(turned[:, t, :], hr[:, t, :], ident_bf[:])
+            nc.scalar.copy(out=hq_tile(i)[:, 0], in_=turned[:].rearrange("p t j -> p j t"))
+
         def score(i, parts):
             codes = ring.tile([P, 2 * P], U32, name="h_codes", align_bytes=64)
             scales = ring.tile([P, 2 * P], U8, name="h_scales", align_bytes=64)
             if i < TILES - 2:
                 y = psum.tile([P, N // P, P], F32, name="y", bufs=1)
-            else:
+            elif i == TILES - 2:
                 y = psum.tile([P, N // P, P], F32, name="rel", bufs=2)
+            else:
+                y = psum.tile([P, N // P, P], F32, name="ent", bufs=3)
             for lo, hi in parts:
                 nc.vector.quantize_mx(
                     out=codes[:, lo * P : hi * P].bitcast(FP8X4),
@@ -254,24 +273,41 @@ def tile_list_ckg_none_kernel(
                 nc.vector.scalar_tensor_tensor(out=made[:], in0=by_slot(entity), scalar=-1.0, in1=relation_part, op0=MULT, op1=MULT)
             return made
 
-        for i in range(TILES):
-            if 2 <= i < TILES - 1:
-                score(i - 2, ((0, 2),))
-            real_real = product("real_real", aer[i], rel[i][:, 0], 1)
-            imag_imag = product("imag_imag", aei[i], rel[i][:, 1], -1)
-            turn_and_add(i, 0, real_real, imag_imag)
+        def both_products(name, entity, i):
+            made = ring.tile([P, 2, PACK, P], F32, name=name, bufs=2)
+            nc.vector.tensor_tensor(
+                out=made[:], in0=by_slot(entity).unsqueeze(1).to_broadcast([P, 2, PACK, P]), in1=rel[i][:], op=MULT
+            )
+            return made
+
+        hr = {}
+        for i in range(TILES - 1):
+            if i >= 3:
+                score(i - 3, ((0, 2),))
+            by_real = both_products("by_real", aer[i], i)
+            entity_imag(i + 1)
+            if i + 2 < TILES:
+                relation(i + 2)
             chunk = (i + 4) // 2
             if chunk < J // CHUNK:
                 (gather_relation, gather_entity)[i % 2](chunk)
-            real_imag = product("real_imag", aer[i], rel[i][:, 1], 1)
-            if i + 1 < TILES:
-                entity_imag(i + 1)
-            if i + 2 < TILES:
-                relation(i + 2)
-            imag_real = product("imag_real", aei[i], rel[i][:, 0], 1)
-            turn_and_add(i, 1, real_imag, imag_real)
+            by_imag = both_products("by_imag", aei[i], i)
+            hr[i] = subtract(by_real[:, 0], by_imag[:, 1])
+            if i >= 1:
+                turn(i - 1, hr[i - 1])
+            turn_and_add(i, 1, by_real[:, 1], by_imag[:, 0])
             if i + 2 < TILES:
                 entity_real(i + 2)
+
+        i = TILES - 1
+        score(i - 3, ((0, 2),))
+        real_real = product("real_real", aer[i], rel[i][:, 0], 1)
+        imag_imag = product("imag_imag", aei[i], rel[i][:, 1], -1)
+        turn(i - 1, hr[i - 1])
+        turn_and_add(i, 0, real_real, imag_imag)
+        real_imag = product("real_imag", aer[i], rel[i][:, 1], 1)
+        imag_real = product("imag_real", aei[i], rel[i][:, 0], 1)
+        turn_and_add(i, 1, real_imag, imag_real)
         score(TILES - 3, ((0, 2),))
         score(TILES - 2, ((0, 2),))
         score(TILES - 1, ((0, 1), (1, 2)))

@@ -23,6 +23,7 @@ TILES = J // P
 CHUNK = 256
 PARTS = ((0, CHUNK), (CHUNK, J))
 ROWS = 16
+SHARED = 2
 
 
 def tile_list_ckg_none_kernel(
@@ -82,19 +83,19 @@ def tile_list_ckg_none_kernel(
             nc.gpsimd.dma_start(out=tile[:, h * T // 2 : (h + 1) * T // 2], in_=src[:, h * T // 2 : (h + 1) * T // 2])
 
         def load_table_scales(queue, tile, scales):
-            queue.dma_start(out=tile[0:ROWS, :], in_=scales[0].bitcast(I32))
+            queue.dma_start(out=tile[P - ROWS : P, :], in_=scales[0].bitcast(I32))
 
         def stage_scales(queue, name, scales):
             tile, base = plane_at[name][0], plane_at[name][2]
             rows = scales[0].bitcast(I32)
             queue.dma_start(out=tile[0:ROWS, base // 4 : base // 4 + rows.shape[1]], in_=rows)
 
-        def spread_scales(queues, planes, staged):
+        def spread_scales(queues, planes, staged, first_row):
             for q in range(4):
-                queues[q % len(queues)].dma_start(out=planes[32 * q : 32 * q + 4, :], in_=staged[4 * q : 4 * q + 4, :])
+                queues[q % len(queues)].dma_start(out=planes[32 * q : 32 * q + 4, :], in_=staged[first_row + 4 * q : first_row + 4 * q + 4, :])
 
-        nc.vector.memset(tab2_s[:], 0)
-        nc.vector.memset(tab1_s[:], 0)
+        nc.vector.memset(tab2_s[0 : P - ROWS, :], 0)
+        nc.vector.memset(tab1_s[0 : P - ROWS, :], 0)
         nc.vector.memset(planes1[:], 0)
         nc.vector.memset(planes_t[0][:], 0)
         nc.vector.memset(planes_t[1][:], 0)
@@ -116,7 +117,7 @@ def tile_list_ckg_none_kernel(
         load_table_scales(nc.scalar, tab1_s, tab_scales)
         load_words(nc.sync, wrr_w, wrr_words)
         load_words(nc.scalar, wri_w, wri_words)
-        spread_scales((nc.sync, nc.scalar), planes1, staged1)
+        spread_scales((nc.sync, nc.scalar), planes1, staged1, 0)
         load_words(nc.scalar, wer_w, wer_words)
 
         def gather(picked, table, view, offsets, lo, hi):
@@ -128,7 +129,7 @@ def tile_list_ckg_none_kernel(
             width = hi - lo
             gather(picked_s[h][:, 0:width], tab2_s, U8, list2, lo, hi)
             gather(picked_s[h][:, width : 2 * width], tab1_s, U8, list1, lo, hi)
-            spread_scales((nc.sync,), planes_t[h], picked_s[h][:].bitcast(I32))
+            spread_scales((nc.sync,), planes_t[h], picked_s[h][:].bitcast(I32), P - ROWS)
             if h == 0:
                 load_words(nc.sync, wei_w, wei_words)
             for i in range(lo // P, hi // P):
@@ -139,19 +140,19 @@ def tile_list_ckg_none_kernel(
         stage_scales(nc.sync, "ni", ni_scales)
         load_words(nc.sync, nr_w, nr_words)
         load_words(nc.sync, ni_w, ni_words)
-        spread_scales((nc.sync,), planes2, staged2)
+        spread_scales((nc.sync,), planes2, staged2, 0)
 
-        def gather_words(found, table, offsets, name, c):
-            picked = ring.tile([P, CHUNK], U32, name=name, bufs=2, align_bytes=64)
+        def gather_words(found, table, offsets, name, c, bufs):
+            picked = ring.tile([P, CHUNK], U32, name=name, bufs=bufs, align_bytes=64)
             gather(picked[:], table, U32, offsets, c * CHUNK, (c + 1) * CHUNK)
             for i in range(2):
                 found[2 * c + i] = picked[:, i * P : (i + 1) * P]
 
         def gather_relation(c):
-            gather_words(w2, tab2_w, list2, "w2", c)
+            gather_words(w2, tab2_w, list2, "w2", c, 4)
 
         def gather_entity(c):
-            gather_words(w1, tab1_w, list1, "w1", c)
+            gather_words(w1, tab1_w, list1, "w1", c, 2)
 
         def project(i, codes, scales, weight, fmt, name, tag, bufs):
             acc = psum.tile([P, R], F32, name=tag, bufs=bufs)
@@ -175,7 +176,7 @@ def tile_list_ckg_none_kernel(
         def tile_blocks(part):
             return part.rearrange("j t (b m) -> j b t m", m=PACK)
 
-        aer, aei, rel, hq = {}, {}, {}, {}
+        aer, aei, aei_sb, rel, hq = {}, {}, {}, {}, {}
 
         def relation(i):
             rel[i] = ring.tile([P, 2, PACK, P], F32, name="rel_sb")
@@ -188,6 +189,9 @@ def tile_list_ckg_none_kernel(
 
         def entity_imag(i):
             aei[i] = project(i, w1, s1, wei_w, FP8X4, "wei", "ent", 3)
+            if i < SHARED:
+                aei_sb[i] = ring.tile([P, PACK, P], F32, name="aei_sb", bufs=2)
+                nc.scalar.copy(out=aei_sb[i][:], in_=by_slot(aei[i]))
 
         def hq_tile(i):
             if i not in hq:
@@ -218,43 +222,62 @@ def tile_list_ckg_none_kernel(
                 nc.tensor.transpose(turned[:, t, :], hr[:, t, :], ident_bf[:])
             nc.scalar.copy(out=hq_tile(i)[:, 0], in_=turned[:].rearrange("p t j -> p j t"))
 
-        def score(i, parts):
+        def quantise(i, codes, scales, lo, hi):
+            nc.vector.quantize_mx(
+                out=codes[:, lo * P : hi * P].bitcast(FP8X4),
+                scales=scales[:, lo * P : hi * P],
+                in_=hq[i][:, lo:hi].rearrange("p c j t -> p (c j t)"),
+            )
+
+        def score_pass(y, codes, scales, c, h, start, stop):
+            if c == 0:
+                weight = nr_w[:, h * P : (h + 1) * P].bitcast(FP8X4)
+            else:
+                weight = ni_w[:, h * P // 2 : (h + 1) * P // 2].bitcast(FP4X4)
+            nc.tensor.matmul_mx(
+                out=y,
+                lhsT=weight,
+                lhsT_scale=plane(("nr", "ni")[c], h * P, (h + 1) * P),
+                rhs=codes[:, c * P : (c + 1) * P].bitcast(FP8X4),
+                rhs_scale=scales[:, c * P : (c + 1) * P],
+                start=start,
+                stop=stop,
+            )
+
+        def score(i):
             codes = ring.tile([P, 2 * P], U32, name="h_codes", align_bytes=64)
             scales = ring.tile([P, 2 * P], U8, name="h_scales", align_bytes=64)
             if i < TILES - 2:
                 y = psum.tile([P, N // P, P], F32, name="y", bufs=1)
-            elif i == TILES - 2:
-                y = psum.tile([P, N // P, P], F32, name="rel", bufs=2)
             else:
-                y = psum.tile([P, N // P, P], F32, name="ent", bufs=3)
-            for lo, hi in parts:
-                nc.vector.quantize_mx(
-                    out=codes[:, lo * P : hi * P].bitcast(FP8X4),
-                    scales=scales[:, lo * P : hi * P],
-                    in_=hq[i][:, lo:hi].rearrange("p c j t -> p (c j t)"),
-                )
-                for c in range(lo, hi):
-                    for h in range(N // P):
-                        if c == 0:
-                            weight = nr_w[:, h * P : (h + 1) * P].bitcast(FP8X4)
-                        else:
-                            weight = ni_w[:, h * P // 2 : (h + 1) * P // 2].bitcast(FP4X4)
-                        nc.tensor.matmul_mx(
-                            out=y[:, h, :],
-                            lhsT=weight,
-                            lhsT_scale=plane(("nr", "ni")[c], h * P, (h + 1) * P),
-                            rhs=codes[:, c * P : (c + 1) * P].bitcast(FP8X4),
-                            rhs_scale=scales[:, c * P : (c + 1) * P],
-                            start=(c == 0 and h == 0),
-                            stop=(c == 1 and h == N // P - 1),
-                        )
+                y = psum.tile([P, N // P, P], F32, name="rel", bufs=2)
+            quantise(i, codes, scales, 0, 2)
+            for h in range(N // P):
+                for c in range(2):
+                    score_pass(y[:, h, :], codes, scales, c, h, c == 0, c == 1)
             y_sb = ring.tile([P, N // P, P], F32, name="y_sb")
             nc.scalar.copy(out=y_sb[:], in_=y[:])
             nc.sync.dma_start(
                 out=out[:, i * P : (i + 1) * P].rearrange("(h p) j -> p h j", p=P), in_=y_sb[:]
             )
 
-        for c in range(2):
+        def score_last(i):
+            codes = ring.tile([P, 2 * P], U32, name="h_codes", align_bytes=64)
+            scales = ring.tile([P, 2 * P], U8, name="h_scales", align_bytes=64)
+            y = [psum.tile([P, P], F32, name="ent", bufs=3) for h in range(N // P)]
+            for c in range(2):
+                quantise(i, codes, scales, c, c + 1)
+                for h in range(N // P):
+                    score_pass(y[h][:], codes, scales, c, h, c == 0, c == 1)
+            for h in range(N // P):
+                half = keep.tile([P, P], F32, name="last" + str(h))
+                if h == 0:
+                    nc.vector.tensor_copy(half[:], y[h][:])
+                else:
+                    nc.scalar.copy(out=half[:], in_=y[h][:])
+                (nc.sync, nc.scalar)[h].dma_start(out=out[h * P : (h + 1) * P, i * P : (i + 1) * P], in_=half[:])
+
+        for c in range(4):
             gather_relation(c)
         for c in range(2):
             gather_entity(c)
@@ -274,7 +297,7 @@ def tile_list_ckg_none_kernel(
             return made
 
         def both_products(name, entity, i):
-            made = ring.tile([P, 2, PACK, P], F32, name=name, bufs=2)
+            made = ring.tile([P, 2, PACK, P], F32, name=name, bufs=3)
             nc.vector.tensor_tensor(
                 out=made[:], in0=by_slot(entity).unsqueeze(1).to_broadcast([P, 2, PACK, P]), in1=rel[i][:], op=MULT
             )
@@ -283,15 +306,19 @@ def tile_list_ckg_none_kernel(
         hr = {}
         for i in range(TILES - 1):
             if i >= 3:
-                score(i - 3, ((0, 2),))
+                score(i - 3)
             by_real = both_products("by_real", aer[i], i)
             entity_imag(i + 1)
             if i + 2 < TILES:
                 relation(i + 2)
-            chunk = (i + 4) // 2
-            if chunk < J // CHUNK:
-                (gather_relation, gather_entity)[i % 2](chunk)
-            by_imag = both_products("by_imag", aei[i], i)
+            if i in (2, 3):
+                gather_entity(i)
+            if i < SHARED:
+                by_imag = ring.tile([P, 2, PACK, P], F32, name="by_imag", bufs=3)
+                nc.vector.tensor_tensor(out=by_imag[:, 0], in0=by_slot(aei[i]), in1=rel[i][:, 0], op=MULT)
+                nc.gpsimd.tensor_tensor(out=by_imag[:, 1], in0=aei_sb[i][:], in1=rel[i][:, 1], op=MULT)
+            else:
+                by_imag = both_products("by_imag", aei[i], i)
             hr[i] = subtract(by_real[:, 0], by_imag[:, 1])
             if i >= 1:
                 turn(i - 1, hr[i - 1])
@@ -300,7 +327,7 @@ def tile_list_ckg_none_kernel(
                 entity_real(i + 2)
 
         i = TILES - 1
-        score(i - 3, ((0, 2),))
+        score(i - 3)
         real_real = product("real_real", aer[i], rel[i][:, 0], 1)
         imag_imag = product("imag_imag", aei[i], rel[i][:, 1], -1)
         turn(i - 1, hr[i - 1])
@@ -308,6 +335,6 @@ def tile_list_ckg_none_kernel(
         real_imag = product("real_imag", aer[i], rel[i][:, 1], 1)
         imag_real = product("imag_real", aei[i], rel[i][:, 0], 1)
         turn_and_add(i, 1, real_imag, imag_real)
-        score(TILES - 3, ((0, 2),))
-        score(TILES - 2, ((0, 2),))
-        score(TILES - 1, ((0, 1), (1, 2)))
+        score(TILES - 3)
+        score(TILES - 2)
+        score_last(TILES - 1)

@@ -19,10 +19,11 @@ SUBTRACT = mybir.AluOpType.subtract
 
 P = 128
 PACK = 4
-TILES = J // P
-CHUNK = 256
-PARTS = ((0, CHUNK), (CHUNK, J))
 ROWS = 16
+TILES = J // P
+CHUNK = 2 * P
+PARTS = ((0, CHUNK), (CHUNK, J))
+LAG = 3
 SHARED = 2
 
 
@@ -44,11 +45,12 @@ def tile_list_ckg_none_kernel(
         tab2_w = keep.tile([P, T], I32, name="tab2_w", align_bytes=64)
         tab1_s = keep.tile([P, T // 4], I32, name="tab1_s", align_bytes=64)
         tab2_s = keep.tile([P, T // 4], I32, name="tab2_s", align_bytes=64)
-        staged1 = first.tile([P, R], I32, name="staged1", align_bytes=64, offset=0)
-        wer_w = first.tile([P, R], I32, name="wer_w", align_bytes=64, offset=0)
-        wei_w = first.tile([P, R], I32, name="wei_w", align_bytes=64, offset=4 * R)
         wrr_w = keep.tile([P, R // 2], I32, name="wrr_w", align_bytes=64)
         wri_w = keep.tile([P, R // 2], I32, name="wri_w", align_bytes=64)
+
+        wer_w = first.tile([P, R], I32, name="wer_w", align_bytes=64, offset=0)
+        wei_w = first.tile([P, R], I32, name="wei_w", align_bytes=64, offset=4 * R)
+        staged1 = first.tile([P, R], I32, name="staged1", align_bytes=64, offset=0)
         picked_s = [
             first.tile([P, 2 * CHUNK], U8, name="picked_s0", align_bytes=64, offset=4 * R),
             second.tile([P, 2 * (J - CHUNK)], U8, name="picked_s1", align_bytes=64, offset=2 * N),
@@ -56,6 +58,7 @@ def tile_list_ckg_none_kernel(
         nr_w = second.tile([P, N], I32, name="nr_w", align_bytes=64, offset=0)
         staged2 = second.tile([P, N // 2], I32, name="staged2", align_bytes=64, offset=4 * N)
         ni_w = second.tile([P, N // 2], I32, name="ni_w", align_bytes=64, offset=6 * N)
+
         planes_t = [keep.tile([P, (hi - lo) // 2], I32, name="planes_t" + str(lo), align_bytes=64) for lo, hi in PARTS]
         planes1 = keep.tile([P, R], I32, name="planes1", align_bytes=64)
         planes2 = keep.tile([P, N // 2], I32, name="planes2", align_bytes=64)
@@ -78,9 +81,10 @@ def tile_list_ckg_none_kernel(
                 src = src.rearrange("p n t -> p (n t)")
             queue.dma_start(out=tile[:], in_=src.bitcast(I32))
 
-        def load_table_half(tile, words, h):
+        def load_table_words(tile, words):
             src = words[0].rearrange("p n t -> p (n t)").bitcast(I32)
-            nc.gpsimd.dma_start(out=tile[:, h * T // 2 : (h + 1) * T // 2], in_=src[:, h * T // 2 : (h + 1) * T // 2])
+            for lo in range(0, T, T // 2):
+                nc.gpsimd.dma_start(out=tile[:, lo : lo + T // 2], in_=src[:, lo : lo + T // 2])
 
         def load_table_scales(queue, tile, scales):
             queue.dma_start(out=tile[P - ROWS : P, :], in_=scales[0].bitcast(I32))
@@ -90,9 +94,10 @@ def tile_list_ckg_none_kernel(
             rows = scales[0].bitcast(I32)
             queue.dma_start(out=tile[0:ROWS, base // 4 : base // 4 + rows.shape[1]], in_=rows)
 
-        def spread_scales(queues, planes, staged, first_row):
+        def spread_scales(queues, planes, rows, first_row):
             for q in range(4):
-                queues[q % len(queues)].dma_start(out=planes[32 * q : 32 * q + 4, :], in_=staged[first_row + 4 * q : first_row + 4 * q + 4, :])
+                at = first_row + 4 * q
+                queues[q % len(queues)].dma_start(out=planes[32 * q : 32 * q + 4, :], in_=rows[at : at + 4, :])
 
         nc.vector.memset(tab2_s[0 : P - ROWS, :], 0)
         nc.vector.memset(tab1_s[0 : P - ROWS, :], 0)
@@ -100,10 +105,8 @@ def tile_list_ckg_none_kernel(
         nc.vector.memset(planes_t[0][:], 0)
         nc.vector.memset(planes_t[1][:], 0)
         nc.vector.memset(planes2[:], 0)
-        load_table_half(tab2_w, tab2_words, 0)
-        load_table_half(tab2_w, tab2_words, 1)
-        load_table_half(tab1_w, tab_words, 0)
-        load_table_half(tab1_w, tab_words, 1)
+        load_table_words(tab2_w, tab2_words)
+        load_table_words(tab1_w, tab_words)
         make_identity(nc, ident[:])
         make_identity(nc, ident_bf[:])
 
@@ -124,17 +127,20 @@ def tile_list_ckg_none_kernel(
             nc.vector.tensor_copy(picked, table[:].bitcast(view).indirect(offsets[:, lo // 16 : hi // 16]))
 
         s1, s2, w1, w2 = {}, {}, {}, {}
-        for h in range(2):
-            lo, hi = PARTS[h]
+
+        def gather_scales(part):
+            lo, hi = PARTS[part]
             width = hi - lo
-            gather(picked_s[h][:, 0:width], tab2_s, U8, list2, lo, hi)
-            gather(picked_s[h][:, width : 2 * width], tab1_s, U8, list1, lo, hi)
-            spread_scales((nc.sync,), planes_t[h], picked_s[h][:].bitcast(I32), P - ROWS)
-            if h == 0:
-                load_words(nc.sync, wei_w, wei_words)
+            gather(picked_s[part][:, 0:width], tab2_s, U8, list2, lo, hi)
+            gather(picked_s[part][:, width : 2 * width], tab1_s, U8, list1, lo, hi)
+            spread_scales((nc.sync,), planes_t[part], picked_s[part][:].bitcast(I32), P - ROWS)
             for i in range(lo // P, hi // P):
-                s2[i] = planes_t[h][:].bitcast(U8)[:, i * P - lo : (i + 1) * P - lo]
-                s1[i] = planes_t[h][:].bitcast(U8)[:, width + i * P - lo : width + (i + 1) * P - lo]
+                s2[i] = planes_t[part][:].bitcast(U8)[:, i * P - lo : (i + 1) * P - lo]
+                s1[i] = planes_t[part][:].bitcast(U8)[:, width + i * P - lo : width + (i + 1) * P - lo]
+
+        gather_scales(0)
+        load_words(nc.sync, wei_w, wei_words)
+        gather_scales(1)
 
         stage_scales(nc.sync, "nr", nr_scales)
         stage_scales(nc.sync, "ni", ni_scales)
@@ -145,17 +151,20 @@ def tile_list_ckg_none_kernel(
         def gather_words(found, table, offsets, name, c, bufs):
             picked = ring.tile([P, CHUNK], U32, name=name, bufs=bufs, align_bytes=64)
             gather(picked[:], table, U32, offsets, c * CHUNK, (c + 1) * CHUNK)
-            for i in range(2):
-                found[2 * c + i] = picked[:, i * P : (i + 1) * P]
+            for n in range(CHUNK // P):
+                found[c * CHUNK // P + n] = picked[:, n * P : (n + 1) * P]
 
         def gather_relation(c):
-            gather_words(w2, tab2_w, list2, "w2", c, 4)
+            gather_words(w2, tab2_w, list2, "w2", c, 3)
 
         def gather_entity(c):
             gather_words(w1, tab1_w, list1, "w1", c, 2)
 
-        def project(i, codes, scales, weight, fmt, name, tag, bufs):
-            acc = psum.tile([P, R], F32, name=tag, bufs=bufs)
+        def bank(tag, shape, dtype):
+            return psum.tile(shape, dtype, name=tag, bufs={"ent": 3, "rel": 2}.get(tag, 1))
+
+        def project(i, codes, scales, weight, fmt, name, tag):
+            acc = bank(tag, [P, R], F32)
             nc.tensor.matmul_mx(
                 out=acc[:],
                 lhsT=codes[i].bitcast(FP8X4),
@@ -165,62 +174,60 @@ def tile_list_ckg_none_kernel(
                 start=True,
                 stop=True,
             )
-            return acc
-
-        def by_slot(acc):
             return acc[:].rearrange("j (m t) -> j t m", t=PACK)
 
-        def bank_blocks(acc):
-            return acc[:].rearrange("j (b m t) -> j b t m", t=PACK, m=PACK)
-
-        def tile_blocks(part):
-            return part.rearrange("j t (b m) -> j b t m", m=PACK)
-
-        aer, aei, aei_sb, rel, hq = {}, {}, {}, {}, {}
+        aer, aei, aei_sb, rel, hr, hq = {}, {}, {}, {}, {}, {}
 
         def relation(i):
             rel[i] = ring.tile([P, 2, PACK, P], F32, name="rel_sb")
             for part, weight, name in ((0, wrr_w, "wrr"), (1, wri_w, "wri")):
-                acc = project(i, w2, s2, weight, FP4X4, name, "rel", 2)
-                nc.scalar.copy(out=tile_blocks(rel[i][:, part]), in_=bank_blocks(acc))
+                nc.scalar.copy(out=rel[i][:, part], in_=project(i, w2, s2, weight, FP4X4, name, "rel"))
 
         def entity_real(i):
-            aer[i] = project(i, w1, s1, wer_w, FP8X4, "wer", "ent", 3)
+            aer[i] = project(i, w1, s1, wer_w, FP8X4, "wer", "ent")
 
         def entity_imag(i):
-            aei[i] = project(i, w1, s1, wei_w, FP8X4, "wei", "ent", 3)
+            aei[i] = project(i, w1, s1, wei_w, FP8X4, "wei", "ent")
             if i < SHARED:
-                aei_sb[i] = ring.tile([P, PACK, P], F32, name="aei_sb", bufs=2)
-                nc.scalar.copy(out=aei_sb[i][:], in_=by_slot(aei[i]))
+                aei_sb[i] = ring.tile([P, PACK, P], F32, name="aei_sb", bufs=SHARED)
+                nc.scalar.copy(out=aei_sb[i][:], in_=aei[i])
 
-        def hq_tile(i):
+        def product(name, entity, relation_part):
+            made = ring.tile([P, PACK, P], F32, name=name, bufs=2)
+            nc.vector.tensor_tensor(out=made[:], in0=entity, in1=relation_part, op=MULT)
+            return made
+
+        def both_products(name, entity, i):
+            made = ring.tile([P, 2, PACK, P], F32, name=name)
+            nc.vector.tensor_tensor(
+                out=made[:], in0=entity.unsqueeze(1).to_broadcast([P, 2, PACK, P]), in1=rel[i][:], op=MULT
+            )
+            return made
+
+        def subtract(i, real_real, imag_imag):
+            hr[i] = ring.tile([P, PACK, P], BF16, name="hr", bufs=2, align_bytes=64)
+            nc.gpsimd.tensor_tensor(out=hr[i][:], in0=real_real, in1=imag_imag, op=SUBTRACT)
+
+        def interleave(i, part, turned):
             if i not in hq:
-                hq[i] = ring.tile([P, 2, P, PACK], BF16, name="hq", bufs=4, align_bytes=64)
-            return hq[i]
+                hq[i] = ring.tile([P, 2, P, PACK], BF16, name="hq", bufs=LAG + 1, align_bytes=64)
+            nc.scalar.copy(out=hq[i][:, part], in_=turned[:].rearrange("p t j -> p j t"))
 
-        def turn_and_add(i, part, first, second):
-            if part == 0:
-                turned = psum.tile([P, PACK, P], F32, name="rel", bufs=2)
-            else:
-                turned = psum.tile([P, PACK, P], F32, name="turned1", bufs=1)
-            for n, term in enumerate((first, second)):
+        def turn_hr(i):
+            turned = bank("turned_hr", [P, PACK, P], BF16)
+            for t in range(PACK):
+                nc.tensor.transpose(turned[:, t, :], hr[i][:, t, :], ident_bf[:])
+            interleave(i, 0, turned)
+
+        def turn_and_add(i, part, tag, terms):
+            turned = bank(tag, [P, PACK, P], F32)
+            for n, term in enumerate(terms):
                 for t in range(PACK):
                     nc.tensor.matmul(
                         out=turned[:, t, :], lhsT=term[:, t, :], rhs=ident[:], is_transpose=True,
                         start=(n == 0 and t == 0), stop=(n == 1 and t == PACK - 1),
                     )
-            nc.scalar.copy(out=hq_tile(i)[:, part], in_=turned[:].rearrange("p t j -> p j t"))
-
-        def subtract(first, second):
-            hr = ring.tile([P, PACK, P], BF16, name="hr", bufs=2, align_bytes=64)
-            nc.gpsimd.tensor_tensor(out=hr[:], in0=first, in1=second, op=SUBTRACT)
-            return hr
-
-        def turn(i, hr):
-            turned = psum.tile([P, PACK, P], BF16, name="turned0", bufs=1)
-            for t in range(PACK):
-                nc.tensor.transpose(turned[:, t, :], hr[:, t, :], ident_bf[:])
-            nc.scalar.copy(out=hq_tile(i)[:, 0], in_=turned[:].rearrange("p t j -> p j t"))
+            interleave(i, part, turned)
 
         def quantise(i, codes, scales, lo, hi):
             nc.vector.quantize_mx(
@@ -229,55 +236,52 @@ def tile_list_ckg_none_kernel(
                 in_=hq[i][:, lo:hi].rearrange("p c j t -> p (c j t)"),
             )
 
-        def score_pass(y, codes, scales, c, h, start, stop):
-            if c == 0:
+        def score_pass(y, codes, scales, part, h):
+            if part == 0:
                 weight = nr_w[:, h * P : (h + 1) * P].bitcast(FP8X4)
             else:
                 weight = ni_w[:, h * P // 2 : (h + 1) * P // 2].bitcast(FP4X4)
             nc.tensor.matmul_mx(
                 out=y,
                 lhsT=weight,
-                lhsT_scale=plane(("nr", "ni")[c], h * P, (h + 1) * P),
-                rhs=codes[:, c * P : (c + 1) * P].bitcast(FP8X4),
-                rhs_scale=scales[:, c * P : (c + 1) * P],
-                start=start,
-                stop=stop,
+                lhsT_scale=plane(("nr", "ni")[part], h * P, (h + 1) * P),
+                rhs=codes[:, part * P : (part + 1) * P].bitcast(FP8X4),
+                rhs_scale=scales[:, part * P : (part + 1) * P],
+                start=(part == 0),
+                stop=(part == 1),
             )
 
-        def score(i):
+        def quantised_tiles():
             codes = ring.tile([P, 2 * P], U32, name="h_codes", align_bytes=64)
             scales = ring.tile([P, 2 * P], U8, name="h_scales", align_bytes=64)
-            if i < TILES - 2:
-                y = psum.tile([P, N // P, P], F32, name="y", bufs=1)
-            else:
-                y = psum.tile([P, N // P, P], F32, name="rel", bufs=2)
+            return codes, scales
+
+        def score(i, tag):
+            codes, scales = quantised_tiles()
+            y = bank(tag, [P, N // P, P], F32)
             quantise(i, codes, scales, 0, 2)
             for h in range(N // P):
-                for c in range(2):
-                    score_pass(y[:, h, :], codes, scales, c, h, c == 0, c == 1)
+                for part in range(2):
+                    score_pass(y[:, h, :], codes, scales, part, h)
             y_sb = ring.tile([P, N // P, P], F32, name="y_sb")
             nc.scalar.copy(out=y_sb[:], in_=y[:])
-            nc.sync.dma_start(
-                out=out[:, i * P : (i + 1) * P].rearrange("(h p) j -> p h j", p=P), in_=y_sb[:]
-            )
+            nc.sync.dma_start(out=out[:, i * P : (i + 1) * P].rearrange("(h p) j -> p h j", p=P), in_=y_sb[:])
 
         def score_last(i):
-            codes = ring.tile([P, 2 * P], U32, name="h_codes", align_bytes=64)
-            scales = ring.tile([P, 2 * P], U8, name="h_scales", align_bytes=64)
-            y = [psum.tile([P, P], F32, name="ent", bufs=3) for h in range(N // P)]
-            for c in range(2):
-                quantise(i, codes, scales, c, c + 1)
+            codes, scales = quantised_tiles()
+            y = [bank("ent", [P, P], F32) for h in range(N // P)]
+            for part in range(2):
+                quantise(i, codes, scales, part, part + 1)
                 for h in range(N // P):
-                    score_pass(y[h][:], codes, scales, c, h, c == 0, c == 1)
-            for h in range(N // P):
-                half = keep.tile([P, P], F32, name="last" + str(h))
-                if h == 0:
-                    nc.vector.tensor_copy(half[:], y[h][:])
-                else:
-                    nc.scalar.copy(out=half[:], in_=y[h][:])
-                (nc.sync, nc.scalar)[h].dma_start(out=out[h * P : (h + 1) * P, i * P : (i + 1) * P], in_=half[:])
+                    score_pass(y[h][:], codes, scales, part, h)
+            low = keep.tile([P, P], F32, name="last_low")
+            nc.vector.tensor_copy(low[:], y[0][:])
+            nc.sync.dma_start(out=out[0:P, i * P : (i + 1) * P], in_=low[:])
+            high = keep.tile([P, P], F32, name="last_high")
+            nc.scalar.copy(out=high[:], in_=y[1][:])
+            nc.scalar.dma_start(out=out[P:N, i * P : (i + 1) * P], in_=high[:])
 
-        for c in range(4):
+        for c in range(3):
             gather_relation(c)
         for c in range(2):
             gather_entity(c)
@@ -286,55 +290,52 @@ def tile_list_ckg_none_kernel(
         entity_imag(0)
         relation(1)
         entity_real(1)
-        def product(name, entity, relation_part, sign):
-            made = ring.tile([P, PACK, P], F32, name=name, bufs=2)
-            if sign > 0:
-                nc.vector.tensor_tensor(
-                    out=tile_blocks(made[:]), in0=bank_blocks(entity), in1=tile_blocks(relation_part), op=MULT
-                )
-            else:
-                nc.vector.scalar_tensor_tensor(out=made[:], in0=by_slot(entity), scalar=-1.0, in1=relation_part, op0=MULT, op1=MULT)
-            return made
 
-        def both_products(name, entity, i):
-            made = ring.tile([P, 2, PACK, P], F32, name=name, bufs=3)
-            nc.vector.tensor_tensor(
-                out=made[:], in0=by_slot(entity).unsqueeze(1).to_broadcast([P, 2, PACK, P]), in1=rel[i][:], op=MULT
-            )
-            return made
-
-        hr = {}
-        for i in range(TILES - 1):
-            if i >= 3:
-                score(i - 3)
+        for i in range(TILES - 2):
+            if i >= LAG:
+                score(i - LAG, "y")
             by_real = both_products("by_real", aer[i], i)
             entity_imag(i + 1)
-            if i + 2 < TILES:
-                relation(i + 2)
-            if i in (2, 3):
+            relation(i + 2)
+            if i == 0:
+                gather_relation(J // CHUNK - 1)
+            if SHARED <= i < J // CHUNK:
                 gather_entity(i)
             if i < SHARED:
-                by_imag = ring.tile([P, 2, PACK, P], F32, name="by_imag", bufs=3)
-                nc.vector.tensor_tensor(out=by_imag[:, 0], in0=by_slot(aei[i]), in1=rel[i][:, 0], op=MULT)
+                by_imag = ring.tile([P, 2, PACK, P], F32, name="by_imag")
+                nc.vector.tensor_tensor(out=by_imag[:, 0], in0=aei[i], in1=rel[i][:, 0], op=MULT)
                 nc.gpsimd.tensor_tensor(out=by_imag[:, 1], in0=aei_sb[i][:], in1=rel[i][:, 1], op=MULT)
             else:
                 by_imag = both_products("by_imag", aei[i], i)
-            hr[i] = subtract(by_real[:, 0], by_imag[:, 1])
+            subtract(i, by_real[:, 0], by_imag[:, 1])
             if i >= 1:
-                turn(i - 1, hr[i - 1])
-            turn_and_add(i, 1, by_real[:, 1], by_imag[:, 0])
-            if i + 2 < TILES:
-                entity_real(i + 2)
+                turn_hr(i - 1)
+            turn_and_add(i, 1, "turned_hi", (by_real[:, 1], by_imag[:, 0]))
+            entity_real(i + 2)
+
+        i = TILES - 2
+        score(i - LAG, "y")
+        real_real = product("real_real", aer[i], rel[i][:, 0])
+        imag_imag = product("imag_imag", aei[i], rel[i][:, 1])
+        subtract(i, real_real[:], imag_imag[:])
+        real_imag = product("real_imag", aer[i], rel[i][:, 1])
+        entity_imag(i + 1)
+        imag_real = product("imag_real", aei[i], rel[i][:, 0])
+        turn_hr(i - 1)
+        turn_and_add(i, 1, "turned_hi", (real_imag, imag_real))
 
         i = TILES - 1
-        score(i - 3)
-        real_real = product("real_real", aer[i], rel[i][:, 0], 1)
-        imag_imag = product("imag_imag", aei[i], rel[i][:, 1], -1)
-        turn(i - 1, hr[i - 1])
-        turn_and_add(i, 0, real_real, imag_imag)
-        real_imag = product("real_imag", aer[i], rel[i][:, 1], 1)
-        imag_real = product("imag_real", aei[i], rel[i][:, 0], 1)
-        turn_and_add(i, 1, real_imag, imag_real)
-        score(TILES - 3)
-        score(TILES - 2)
-        score_last(TILES - 1)
+        real_real = product("real_real", aer[i], rel[i][:, 0])
+        score(i - LAG, "y")
+        minus_imag_imag = ring.tile([P, PACK, P], F32, name="imag_imag", bufs=2)
+        nc.vector.scalar_tensor_tensor(
+            out=minus_imag_imag[:], in0=aei[i], scalar=-1.0, in1=rel[i][:, 1], op0=MULT, op1=MULT
+        )
+        turn_hr(i - 1)
+        turn_and_add(i, 0, "rel", (real_real, minus_imag_imag))
+        real_imag = product("real_imag", aer[i], rel[i][:, 1])
+        imag_real = product("imag_real", aei[i], rel[i][:, 0])
+        turn_and_add(i, 1, "turned_hi", (real_imag, imag_real))
+        score(i - 2, "y")
+        score(i - 1, "rel")
+        score_last(i)

@@ -23,8 +23,8 @@ ROWS = 16
 TILES = J // P
 CHUNK = 2 * P
 PARTS = ((0, CHUNK), (CHUNK, J))
-LAG = 3
-SHARED = 2
+GROUPS = ((0, 1), (2, 3), (4,), (5,), (6,), (7,))
+SHARED = (0, 1, 2, 4)
 
 
 def tile_list_ckg_none_kernel(
@@ -63,7 +63,6 @@ def tile_list_ckg_none_kernel(
         planes1 = keep.tile([P, R], I32, name="planes1", align_bytes=64)
         planes2 = keep.tile([P, N // 2], I32, name="planes2", align_bytes=64)
         ident = keep.tile([P, P], F32, name="ident")
-        ident_bf = keep.tile([P, P], BF16, name="ident_bf")
 
         plane_at = {
             "wrr": (staged1, planes1, 0), "wri": (staged1, planes1, R),
@@ -108,7 +107,6 @@ def tile_list_ckg_none_kernel(
         load_table_words(tab2_w, tab2_words)
         load_table_words(tab1_w, tab_words)
         make_identity(nc, ident[:])
-        make_identity(nc, ident_bf[:])
 
         nc.sync.dma_start(list2[:], offs2)
         nc.sync.dma_start(list1[:], offs)
@@ -161,7 +159,7 @@ def tile_list_ckg_none_kernel(
             gather_words(w1, tab1_w, list1, "w1", c, 2)
 
         def bank(tag, shape, dtype):
-            return psum.tile(shape, dtype, name=tag, bufs={"ent": 3, "rel": 2}.get(tag, 1))
+            return psum.tile(shape, dtype, name=tag, bufs={"ent": 4, "rel": 2}.get(tag, 1))
 
         def project(i, codes, scales, weight, fmt, name, tag):
             acc = bank(tag, [P, R], F32)
@@ -174,69 +172,79 @@ def tile_list_ckg_none_kernel(
                 start=True,
                 stop=True,
             )
+            return acc
+
+        def by_slot(acc):
             return acc[:].rearrange("j (m t) -> j t m", t=PACK)
 
+        def by_pair(acc):
+            return acc[:].rearrange("j (m u e) -> j u m e", u=2, e=2)
+
         aer, aei, aei_sb, rel, hr, hq = {}, {}, {}, {}, {}, {}
+        hq_group = {}
+        for group in GROUPS:
+            hq_group[group] = keep.tile([P, 2, len(group) * P, PACK], BF16, name="hq" + str(group[0]), align_bytes=64)
+            for n, i in enumerate(group):
+                hq[i] = hq_group[group][:, :, n * P : (n + 1) * P]
 
         def relation(i):
-            rel[i] = ring.tile([P, 2, PACK, P], F32, name="rel_sb")
+            rel[i] = ring.tile([P, 2, PACK, P], F32, name="rel_sb", align_bytes=64)
             for part, weight, name in ((0, wrr_w, "wrr"), (1, wri_w, "wri")):
-                nc.scalar.copy(out=rel[i][:, part], in_=project(i, w2, s2, weight, FP4X4, name, "rel"))
+                nc.scalar.copy(out=rel[i][:, part], in_=by_slot(project(i, w2, s2, weight, FP4X4, name, "rel")))
 
-        def entity_real(i):
+        def entity(i):
             aer[i] = project(i, w1, s1, wer_w, FP8X4, "wer", "ent")
-
-        def entity_imag(i):
             aei[i] = project(i, w1, s1, wei_w, FP8X4, "wei", "ent")
-            if i < SHARED:
-                aei_sb[i] = ring.tile([P, PACK, P], F32, name="aei_sb", bufs=SHARED)
-                nc.scalar.copy(out=aei_sb[i][:], in_=aei[i])
+            if i in SHARED:
+                aei_sb[i] = ring.tile([P, PACK, P], F32, name="aei_sb", bufs=2)
+                nc.scalar.copy(out=aei_sb[i][:], in_=by_slot(aei[i]))
 
-        def product(name, entity, relation_part):
-            made = ring.tile([P, PACK, P], F32, name=name, bufs=2)
-            nc.vector.tensor_tensor(out=made[:], in0=entity, in1=relation_part, op=MULT)
-            return made
-
-        def both_products(name, entity, i):
-            made = ring.tile([P, 2, PACK, P], F32, name=name)
+        def hr_term(name, acc, i, part):
+            made = ring.tile([P, 2, P, 2], F32, name=name, bufs=2)
             nc.vector.tensor_tensor(
-                out=made[:], in0=entity.unsqueeze(1).to_broadcast([P, 2, PACK, P]), in1=rel[i][:], op=MULT
+                out=made[:], in0=by_pair(acc), in1=rel[i][:, part].rearrange("j (u e) m -> j u m e", e=2), op=MULT
             )
             return made
 
+        def hi_term(name, engine, entity_part, i, part):
+            made = ring.tile([P, PACK, P], F32, name=name, bufs=2)
+            engine.tensor_tensor(out=made[:], in0=entity_part, in1=rel[i][:, part], op=MULT)
+            return made
+
         def subtract(i, real_real, imag_imag):
-            hr[i] = ring.tile([P, PACK, P], BF16, name="hr", bufs=2, align_bytes=64)
-            nc.gpsimd.tensor_tensor(out=hr[i][:], in0=real_real, in1=imag_imag, op=SUBTRACT)
+            hr[i] = ring.tile([P, 2, P, 2], BF16, name="hr", bufs=2, align_bytes=64)
+            nc.gpsimd.tensor_tensor(out=hr[i][:], in0=real_real[:], in1=imag_imag[:], op=SUBTRACT)
 
-        def interleave(i, part, turned):
-            if i not in hq:
-                hq[i] = ring.tile([P, 2, P, PACK], BF16, name="hq", bufs=LAG + 1, align_bytes=64)
-            nc.scalar.copy(out=hq[i][:, part], in_=turned[:].rearrange("p t j -> p j t"))
+        def turn_hr(i, tag, copy):
+            words = hr[i][:].rearrange("j u m e -> j (u m e)").bitcast(F32)
+            turned = bank(tag, [P, 2, P], F32)
+            for u in range(2):
+                nc.tensor.transpose(turned[:, u, :], words[:, u * P : (u + 1) * P], ident[:])
+            pairs = hq[i][:, 0].rearrange("p j t -> p (j t)").bitcast(F32).rearrange("p (j u) -> p j u", u=2)
+            copy(pairs, turned[:].rearrange("p u j -> p j u"))
 
-        def turn_hr(i):
-            turned = bank("turned_hr", [P, PACK, P], BF16)
-            for t in range(PACK):
-                nc.tensor.transpose(turned[:, t, :], hr[i][:, t, :], ident_bf[:])
-            interleave(i, 0, turned)
-
-        def turn_and_add(i, part, tag, terms):
-            turned = bank(tag, [P, PACK, P], F32)
+        def turn_hi(i, terms):
+            turned = bank("turned_hi", [P, PACK, P], F32)
             for n, term in enumerate(terms):
                 for t in range(PACK):
                     nc.tensor.matmul(
                         out=turned[:, t, :], lhsT=term[:, t, :], rhs=ident[:], is_transpose=True,
                         start=(n == 0 and t == 0), stop=(n == 1 and t == PACK - 1),
                     )
-            interleave(i, part, turned)
+            nc.scalar.copy(out=hq[i][:, 1], in_=turned[:].rearrange("p t j -> p j t"))
 
-        def quantise(i, codes, scales, lo, hi):
+        def quantise(group, room, lo, hi):
+            codes, scales = room
+            width = len(group) * P
             nc.vector.quantize_mx(
-                out=codes[:, lo * P : hi * P].bitcast(FP8X4),
-                scales=scales[:, lo * P : hi * P],
-                in_=hq[i][:, lo:hi].rearrange("p c j t -> p (c j t)"),
+                out=codes[:, lo * width : hi * width].bitcast(FP8X4),
+                scales=scales[:, lo * width : hi * width],
+                in_=hq_group[group][:, lo:hi].rearrange("p c j t -> p (c j t)"),
             )
 
-        def score_pass(y, codes, scales, part, h):
+        def score_pass(y, group, room, part, h):
+            codes, scales = room
+            width = len(group) * P
             if part == 0:
                 weight = nr_w[:, h * P : (h + 1) * P].bitcast(FP8X4)
             else:
@@ -245,35 +253,41 @@ def tile_list_ckg_none_kernel(
                 out=y,
                 lhsT=weight,
                 lhsT_scale=plane(("nr", "ni")[part], h * P, (h + 1) * P),
-                rhs=codes[:, part * P : (part + 1) * P].bitcast(FP8X4),
-                rhs_scale=scales[:, part * P : (part + 1) * P],
+                rhs=codes[:, part * width : (part + 1) * width].bitcast(FP8X4),
+                rhs_scale=scales[:, part * width : (part + 1) * width],
                 start=(part == 0),
                 stop=(part == 1),
             )
 
-        def quantised_tiles():
-            codes = ring.tile([P, 2 * P], U32, name="h_codes", align_bytes=64)
-            scales = ring.tile([P, 2 * P], U8, name="h_scales", align_bytes=64)
-            return codes, scales
+        def quantised_tiles(groups):
+            room = ring.tile([P, 2 * R], U32, name="rel_sb", align_bytes=64)
+            planes = room[:, 6 * P :].bitcast(U8)
+            found = {}
+            for group in groups:
+                lo = 2 * P * (group[0] - groups[0][0])
+                hi = lo + 2 * P * len(group)
+                found[group] = (room[:, lo:hi], planes[:, lo:hi])
+            return found
 
-        def score(i, tag):
-            codes, scales = quantised_tiles()
-            y = bank(tag, [P, N // P, P], F32)
-            quantise(i, codes, scales, 0, 2)
+        def score(group, tag, room):
+            width = len(group) * P
+            y = bank(tag, [P, N // P, width], F32)
+            quantise(group, room, 0, 2)
             for h in range(N // P):
                 for part in range(2):
-                    score_pass(y[:, h, :], codes, scales, part, h)
-            y_sb = ring.tile([P, N // P, P], F32, name="y_sb")
+                    score_pass(y[:, h, :], group, room, part, h)
+            y_sb = keep.tile([P, N // P, width], F32, name="y_sb" + str(group[0]))
             nc.scalar.copy(out=y_sb[:], in_=y[:])
-            nc.sync.dma_start(out=out[:, i * P : (i + 1) * P].rearrange("(h p) j -> p h j", p=P), in_=y_sb[:])
+            columns = out[:, group[0] * P : group[0] * P + width]
+            nc.sync.dma_start(out=columns.rearrange("(h p) j -> p h j", p=P), in_=y_sb[:])
 
-        def score_last(i):
-            codes, scales = quantised_tiles()
+        def score_last(group, room):
+            i = group[0]
             y = [bank("ent", [P, P], F32) for h in range(N // P)]
             for part in range(2):
-                quantise(i, codes, scales, part, part + 1)
+                quantise(group, room, part, part + 1)
                 for h in range(N // P):
-                    score_pass(y[h][:], codes, scales, part, h)
+                    score_pass(y[h][:], group, room, part, h)
             low = keep.tile([P, P], F32, name="last_low")
             nc.vector.tensor_copy(low[:], y[0][:])
             nc.sync.dma_start(out=out[0:P, i * P : (i + 1) * P], in_=low[:])
@@ -286,56 +300,41 @@ def tile_list_ckg_none_kernel(
         for c in range(2):
             gather_entity(c)
         relation(0)
-        entity_real(0)
-        entity_imag(0)
+        entity(0)
         relation(1)
-        entity_real(1)
+        entity(1)
+        relation(2)
 
-        for i in range(TILES - 2):
-            if i >= LAG:
-                score(i - LAG, "y")
-            by_real = both_products("by_real", aer[i], i)
-            entity_imag(i + 1)
-            relation(i + 2)
+        for i in range(TILES):
+            real_real = hr_term("real_real", aer[i], i, 0)
+            if i == TILES - 2:
+                score(GROUPS[0], "rel", quantised_tiles(GROUPS[0:1])[GROUPS[0]])
+            if i == TILES - 1:
+                room = quantised_tiles(GROUPS[1:3])
+                score(GROUPS[1], "rel", room[GROUPS[1]])
+                score(GROUPS[2], "ent", room[GROUPS[2]])
+            if 1 <= i < TILES - 2:
+                relation(i + 2)
             if i == 0:
+                real_imag = hi_term("real_imag", nc.vector, by_slot(aer[i]), i, 1)
                 gather_relation(J // CHUNK - 1)
-            if SHARED <= i < J // CHUNK:
-                gather_entity(i)
-            if i < SHARED:
-                by_imag = ring.tile([P, 2, PACK, P], F32, name="by_imag")
-                nc.vector.tensor_tensor(out=by_imag[:, 0], in0=aei[i], in1=rel[i][:, 0], op=MULT)
-                nc.gpsimd.tensor_tensor(out=by_imag[:, 1], in0=aei_sb[i][:], in1=rel[i][:, 1], op=MULT)
-            else:
-                by_imag = both_products("by_imag", aei[i], i)
-            subtract(i, by_real[:, 0], by_imag[:, 1])
+            imag_imag = hr_term("imag_imag", aei[i], i, 1)
+            if i in SHARED:
+                imag_real = hi_term("imag_real", nc.gpsimd, aei_sb[i][:], i, 0)
+            subtract(i, real_real, imag_imag)
+            if 2 <= i + 1 < J // CHUNK:
+                gather_entity(i + 1)
             if i >= 1:
-                turn_hr(i - 1)
-            turn_and_add(i, 1, "turned_hi", (by_real[:, 1], by_imag[:, 0]))
-            entity_real(i + 2)
+                turn_hr(i - 1, "y", nc.scalar.copy)
+                real_imag = hi_term("real_imag", nc.vector, by_slot(aer[i]), i, 1)
+            if i not in SHARED:
+                imag_real = hi_term("imag_real", nc.vector, by_slot(aei[i]), i, 0)
+            turn_hi(i, (real_imag, imag_real))
+            if i + 2 < TILES:
+                entity(i + 2)
+        turn_hr(TILES - 1, "y", nc.vector.tensor_copy)
 
-        i = TILES - 2
-        score(i - LAG, "y")
-        real_real = product("real_real", aer[i], rel[i][:, 0])
-        imag_imag = product("imag_imag", aei[i], rel[i][:, 1])
-        subtract(i, real_real[:], imag_imag[:])
-        real_imag = product("real_imag", aer[i], rel[i][:, 1])
-        entity_imag(i + 1)
-        imag_real = product("imag_real", aei[i], rel[i][:, 0])
-        turn_hr(i - 1)
-        turn_and_add(i, 1, "turned_hi", (real_imag, imag_real))
-
-        i = TILES - 1
-        real_real = product("real_real", aer[i], rel[i][:, 0])
-        score(i - LAG, "y")
-        minus_imag_imag = ring.tile([P, PACK, P], F32, name="imag_imag", bufs=2)
-        nc.vector.scalar_tensor_tensor(
-            out=minus_imag_imag[:], in0=aei[i], scalar=-1.0, in1=rel[i][:, 1], op0=MULT, op1=MULT
-        )
-        turn_hr(i - 1)
-        turn_and_add(i, 0, "rel", (real_real, minus_imag_imag))
-        real_imag = product("real_imag", aer[i], rel[i][:, 1])
-        imag_real = product("imag_real", aei[i], rel[i][:, 0])
-        turn_and_add(i, 1, "turned_hi", (real_imag, imag_real))
-        score(i - 2, "y")
-        score(i - 1, "rel")
-        score_last(i)
+        room = quantised_tiles(GROUPS[3:])
+        score(GROUPS[3], "ent", room[GROUPS[3]])
+        score(GROUPS[4], "rel", room[GROUPS[4]])
+        score_last(GROUPS[5], room[GROUPS[5]])

@@ -180,7 +180,7 @@ def tile_list_ckg_none_kernel(
         def by_pair(acc):
             return acc[:].rearrange("j (m u e) -> j u m e", u=2, e=2)
 
-        aer, aei, aei_sb, rel, hr, hq = {}, {}, {}, {}, {}, {}
+        aer, aei, aer_sb, rel, hr, hq = {}, {}, {}, {}, {}, {}
         hq_group = {}
         for group in GROUPS:
             hq_group[group] = keep.tile([P, 2, len(group) * P, PACK], BF16, name="hq" + str(group[0]), align_bytes=64)
@@ -194,13 +194,13 @@ def tile_list_ckg_none_kernel(
 
         def entity(i):
             aer[i] = project(i, w1, s1, wer_w, FP8X4, "wer", "ent")
-            aei[i] = project(i, w1, s1, wei_w, FP8X4, "wei", "ent")
             if i in SHARED:
-                aei_sb[i] = ring.tile([P, PACK, P], F32, name="aei_sb", bufs=2)
-                nc.scalar.copy(out=aei_sb[i][:], in_=by_slot(aei[i]))
+                aer_sb[i] = ring.tile([P, PACK, P], F32, name="aer_sb", bufs=2)
+                nc.scalar.copy(out=aer_sb[i][:], in_=by_slot(aer[i]))
+            aei[i] = project(i, w1, s1, wei_w, FP8X4, "wei", "ent")
 
         def hr_term(name, acc, i, part):
-            made = ring.tile([P, 2, P, 2], F32, name=name, bufs=2)
+            made = ring.tile([P, 2, P, 2], F32, name=name)
             nc.vector.tensor_tensor(
                 out=made[:], in0=by_pair(acc), in1=rel[i][:, part].rearrange("j (u e) m -> j u m e", e=2), op=MULT
             )
@@ -316,19 +316,18 @@ def tile_list_ckg_none_kernel(
             if 1 <= i < TILES - 2:
                 relation(i + 2)
             if i == 0:
-                real_imag = hi_term("real_imag", nc.vector, by_slot(aer[i]), i, 1)
                 gather_relation(J // CHUNK - 1)
             imag_imag = hr_term("imag_imag", aei[i], i, 1)
             if i in SHARED:
-                imag_real = hi_term("imag_real", nc.gpsimd, aei_sb[i][:], i, 0)
+                real_imag = hi_term("real_imag", nc.gpsimd, aer_sb[i][:], i, 1)
             subtract(i, real_real, imag_imag)
             if 2 <= i + 1 < J // CHUNK:
                 gather_entity(i + 1)
             if i >= 1:
                 turn_hr(i - 1, "y", nc.scalar.copy)
-                real_imag = hi_term("real_imag", nc.vector, by_slot(aer[i]), i, 1)
             if i not in SHARED:
-                imag_real = hi_term("imag_real", nc.vector, by_slot(aei[i]), i, 0)
+                real_imag = hi_term("real_imag", nc.vector, by_slot(aer[i]), i, 1)
+            imag_real = hi_term("imag_real", nc.vector, by_slot(aei[i]), i, 0)
             turn_hi(i, (real_imag, imag_real))
             if i + 2 < TILES:
                 entity(i + 2)

@@ -15,16 +15,16 @@ U8 = mybir.dt.uint8
 FP8X4 = mybir.dt.float8_e4m3fn_x4
 FP4X4 = mybir.dt.float4_e2m1fn_x4
 MULT = mybir.AluOpType.mult
-SUBTRACT = mybir.AluOpType.subtract
+ADD = mybir.AluOpType.add
 
 P = 128
 PACK = 4
 ROWS = 16
 TILES = J // P
 CHUNK = 2 * P
-PARTS = ((0, CHUNK), (CHUNK, J))
-GROUPS = ((0, 1), (2, 3), (4,), (5,), (6,), (7,))
-SHARED = (0, 1, 2, 4)
+GROUPS = ((0, 1), (2, 3), (4, 5), (6,), (7,))
+AER_ON_GPSIMD = (0, 1, 3)
+R_FIRST = (2, 4, 5)
 
 
 def tile_list_ckg_none_kernel(
@@ -34,45 +34,35 @@ def tile_list_ckg_none_kernel(
     nc = tc.nc
     with ExitStack() as ctx:
         keep = ctx.enter_context(tc.tile_pool(name="keep", bufs=1))
-        first = ctx.enter_context(tc.tile_pool(name="first", bufs=1))
-        second = ctx.enter_context(tc.tile_pool(name="second", bufs=1))
+        early = ctx.enter_context(tc.tile_pool(name="early", bufs=1))
+        held = ctx.enter_context(tc.tile_pool(name="held", bufs=1))
+        late = ctx.enter_context(tc.tile_pool(name="late", bufs=1))
         ring = ctx.enter_context(tc.tile_pool(name="ring", bufs=3))
         psum = ctx.enter_context(tc.psum_pool(name="psum", bufs=1))
 
+        def kept(name, width, dtype=I32):
+            return keep.tile([P, width], dtype, name=name, align_bytes=64)
+
         list1 = keep.tile([P, J // 16], U16, name="list1")
         list2 = keep.tile([P, J // 16], U16, name="list2")
-        tab1_w = keep.tile([P, T], I32, name="tab1_w", align_bytes=64)
-        tab2_w = keep.tile([P, T], I32, name="tab2_w", align_bytes=64)
-        tab1_s = keep.tile([P, T // 4], I32, name="tab1_s", align_bytes=64)
-        tab2_s = keep.tile([P, T // 4], I32, name="tab2_s", align_bytes=64)
-        wrr_w = keep.tile([P, R // 2], I32, name="wrr_w", align_bytes=64)
-        wri_w = keep.tile([P, R // 2], I32, name="wri_w", align_bytes=64)
-
-        wer_w = first.tile([P, R], I32, name="wer_w", align_bytes=64, offset=0)
-        wei_w = first.tile([P, R], I32, name="wei_w", align_bytes=64, offset=4 * R)
-        staged1 = first.tile([P, R], I32, name="staged1", align_bytes=64, offset=0)
-        picked_s = [
-            first.tile([P, 2 * CHUNK], U8, name="picked_s0", align_bytes=64, offset=4 * R),
-            second.tile([P, 2 * (J - CHUNK)], U8, name="picked_s1", align_bytes=64, offset=2 * N),
-        ]
-        nr_w = second.tile([P, N], I32, name="nr_w", align_bytes=64, offset=0)
-        staged2 = second.tile([P, N // 2], I32, name="staged2", align_bytes=64, offset=4 * N)
-        ni_w = second.tile([P, N // 2], I32, name="ni_w", align_bytes=64, offset=6 * N)
-
-        planes_t = [keep.tile([P, (hi - lo) // 2], I32, name="planes_t" + str(lo), align_bytes=64) for lo, hi in PARTS]
-        planes1 = keep.tile([P, R], I32, name="planes1", align_bytes=64)
-        planes2 = keep.tile([P, N // 2], I32, name="planes2", align_bytes=64)
+        tab1_w, tab2_w = kept("tab1_w", T), kept("tab2_w", T)
+        tab1_s, tab2_s = kept("tab1_s", T // 4), kept("tab2_s", T // 4)
+        wrr_w, wri_w = kept("wrr_w", R // 2), kept("wri_w", R // 2)
+        wer_w, wei_w = kept("wer_w", R), kept("wei_w", R)
+        nr_w, ni_w = kept("nr_w", N), kept("ni_w", N // 2)
+        staged = {
+            "rel": kept("staged_rel", R // 2),
+            "ent": kept("staged_ent", R // 2),
+            "out": kept("staged_out", N // 2),
+        }
+        planes = {"rel": kept("planes_rel", R // 2), "ent": kept("planes_ent", R // 2), "out": kept("planes_out", N // 2)}
         ident = keep.tile([P, P], F32, name="ident")
 
-        plane_at = {
-            "wrr": (staged1, planes1, 0), "wri": (staged1, planes1, R),
-            "wer": (staged1, planes1, 2 * R), "wei": (staged1, planes1, 3 * R),
-            "nr": (staged2, planes2, 0), "ni": (staged2, planes2, N),
-        }
+        plane_at = {"wrr": ("rel", 0), "wri": ("rel", R), "wer": ("ent", 0), "wei": ("ent", R), "nr": ("out", 0), "ni": ("out", N)}
 
         def plane(name, lo, hi):
-            tile, base = plane_at[name][1:]
-            return tile[:].bitcast(U8)[:, base + lo : base + hi]
+            pair, base = plane_at[name]
+            return planes[pair][:].bitcast(U8)[:, base + lo : base + hi]
 
         def load_words(queue, tile, words):
             src = words[0]
@@ -80,260 +70,335 @@ def tile_list_ckg_none_kernel(
                 src = src.rearrange("p n t -> p (n t)")
             queue.dma_start(out=tile[:], in_=src.bitcast(I32))
 
-        def load_table_words(tile, words):
-            src = words[0].rearrange("p n t -> p (n t)").bitcast(I32)
-            for lo in range(0, T, T // 2):
-                nc.gpsimd.dma_start(out=tile[:, lo : lo + T // 2], in_=src[:, lo : lo + T // 2])
-
-        def load_table_scales(queue, tile, scales):
-            queue.dma_start(out=tile[P - ROWS : P, :], in_=scales[0].bitcast(I32))
-
         def stage_scales(queue, name, scales):
-            tile, base = plane_at[name][0], plane_at[name][2]
+            pair, base = plane_at[name]
             rows = scales[0].bitcast(I32)
-            queue.dma_start(out=tile[0:ROWS, base // 4 : base // 4 + rows.shape[1]], in_=rows)
+            queue.dma_start(out=staged[pair][0:ROWS, base // 4 : base // 4 + rows.shape[1]], in_=rows)
 
-        def spread_scales(queues, planes, rows, first_row):
+        def place_rows(queues, tile, rows):
             for q in range(4):
-                at = first_row + 4 * q
-                queues[q % len(queues)].dma_start(out=planes[32 * q : 32 * q + 4, :], in_=rows[at : at + 4, :])
+                queues[q].dma_start(out=tile[32 * q : 32 * q + 4, :], in_=rows[4 * q : 4 * q + 4, :])
 
-        nc.vector.memset(tab2_s[0 : P - ROWS, :], 0)
-        nc.vector.memset(tab1_s[0 : P - ROWS, :], 0)
-        nc.vector.memset(planes1[:], 0)
-        nc.vector.memset(planes_t[0][:], 0)
-        nc.vector.memset(planes_t[1][:], 0)
-        nc.vector.memset(planes2[:], 0)
-        load_table_words(tab2_w, tab2_words)
-        load_table_words(tab1_w, tab_words)
+        nc.vector.memset(tab2_s[:], 0)
+        nc.vector.memset(planes["rel"][:], 0)
+        nc.vector.memset(tab1_s[:], 0)
+        nc.vector.memset(planes["ent"][:], 0)
+        nc.vector.memset(planes["out"][:], 0)
+        load_words(nc.gpsimd, tab2_w, tab2_words)
         make_identity(nc, ident[:])
+        load_words(nc.gpsimd, tab1_w, tab_words)
+        load_words(nc.gpsimd, wer_w, wer_words)
+        load_words(nc.gpsimd, wei_w, wei_words)
 
-        nc.sync.dma_start(list2[:], offs2)
-        nc.sync.dma_start(list1[:], offs)
-        stage_scales(nc.scalar, "wrr", wrr_scales)
-        stage_scales(nc.scalar, "wri", wri_scales)
-        stage_scales(nc.sync, "wer", wer_scales)
-        stage_scales(nc.scalar, "wei", wei_scales)
-        load_table_scales(nc.sync, tab2_s, tab2_scales)
-        load_table_scales(nc.scalar, tab1_s, tab_scales)
-        load_words(nc.sync, wrr_w, wrr_words)
-        load_words(nc.scalar, wri_w, wri_words)
-        spread_scales((nc.sync, nc.scalar), planes1, staged1, 0)
-        load_words(nc.scalar, wer_w, wer_words)
+        sync, scalar = nc.sync, nc.scalar
+        sync.dma_start(list2[:], offs2)
+        stage_scales(scalar, "wrr", wrr_scales)
+        stage_scales(sync, "wri", wri_scales)
+        stage_scales(scalar, "wer", wer_scales)
+        place_rows((sync, scalar, sync, scalar), tab2_s, tab2_scales[0].bitcast(I32))
 
-        def gather(picked, table, view, offsets, lo, hi):
-            nc.vector.tensor_copy(picked, table[:].bitcast(view).indirect(offsets[:, lo // 16 : hi // 16]))
+        load_words(sync, wrr_w, wrr_words)
+        load_words(sync, wri_w, wri_words)
+        place_rows((sync, sync, sync, sync), planes["rel"], staged["rel"])
+        sync.dma_start(list1[:], offs)
+        stage_scales(sync, "wei", wei_scales)
+        place_rows((sync, sync, sync, sync), tab1_s, tab_scales[0].bitcast(I32))
+        place_rows((sync, sync, sync, sync), planes["ent"], staged["ent"])
+
+        stage_scales(sync, "nr", nr_scales)
+        stage_scales(sync, "ni", ni_scales)
+        load_words(sync, nr_w, nr_words)
+        load_words(sync, ni_w, ni_words)
+        place_rows((sync, sync, sync, sync), planes["out"], staged["out"])
 
         s1, s2, w1, w2 = {}, {}, {}, {}
 
-        def gather_scales(part):
-            lo, hi = PARTS[part]
-            width = hi - lo
-            gather(picked_s[part][:, 0:width], tab2_s, U8, list2, lo, hi)
-            gather(picked_s[part][:, width : 2 * width], tab1_s, U8, list1, lo, hi)
-            spread_scales((nc.sync,), planes_t[part], picked_s[part][:].bitcast(I32), P - ROWS)
+        def gather(found, picked, table, offsets, lo, hi):
+            window = table[:].bitcast(picked.dtype)
+            nc.vector.tensor_copy(picked[:], window.indirect(offsets[:, lo // 16 : hi // 16]))
             for i in range(lo // P, hi // P):
-                s2[i] = planes_t[part][:].bitcast(U8)[:, i * P - lo : (i + 1) * P - lo]
-                s1[i] = planes_t[part][:].bitcast(U8)[:, width + i * P - lo : width + (i + 1) * P - lo]
+                found[i] = picked[:, i * P - lo : (i + 1) * P - lo]
 
-        gather_scales(0)
-        load_words(nc.sync, wei_w, wei_words)
-        gather_scales(1)
+        banks = {
+            kind: [psum.tile([P, R], F32, name=kind + str(n)) for n in range(count)]
+            for kind, count in (("rel", 2), ("scalar", 3), ("vector", 3))
+        }
 
-        stage_scales(nc.sync, "nr", nr_scales)
-        stage_scales(nc.sync, "ni", ni_scales)
-        load_words(nc.sync, nr_w, nr_words)
-        load_words(nc.sync, ni_w, ni_words)
-        spread_scales((nc.sync,), planes2, staged2, 0)
+        def bank(kind):
+            in_turn = banks[kind]
+            in_turn.append(in_turn.pop(0))
+            return in_turn[-1]
 
-        def gather_words(found, table, offsets, name, c, bufs):
-            picked = ring.tile([P, CHUNK], U32, name=name, bufs=bufs, align_bytes=64)
-            gather(picked[:], table, U32, offsets, c * CHUNK, (c + 1) * CHUNK)
-            for n in range(CHUNK // P):
-                found[c * CHUNK // P + n] = picked[:, n * P : (n + 1) * P]
+        dealt_w = {
+            "wrr": kept("wrr_dealt", R // 2), "wri": kept("wri_dealt", R // 2),
+            "wer": held.tile([P, R], I32, name="wer_dealt", align_bytes=64, offset=0),
+            "wei": held.tile([P, R], I32, name="wei_dealt", align_bytes=64, offset=4 * R),
+        }
+        dealt_s = {"rel": kept("rel_dealt", 2 * R, U8), "ent": kept("ent_dealt", 2 * R, U8)}
 
-        def gather_relation(c):
-            gather_words(w2, tab2_w, list2, "w2", c, 3)
+        def deal_words(name, weight, word):
+            nc.scalar.copy(
+                out=dealt_w[name][:].bitcast(word).rearrange("p (t m) -> p m t", t=PACK),
+                in_=weight[:].bitcast(word).rearrange("p (m t) -> p m t", t=PACK),
+            )
 
-        def gather_entity(c):
-            gather_words(w1, tab1_w, list1, "w1", c, 2)
-
-        def bank(tag, shape, dtype):
-            return psum.tile(shape, dtype, name=tag, bufs={"ent": 4, "rel": 2}.get(tag, 1))
+        def deal_scales(pair):
+            nc.gpsimd.tensor_copy(
+                dealt_s[pair][:].rearrange("p (w t m) -> p w t m", w=2, t=PACK),
+                planes[pair][:].bitcast(U8).rearrange("p (w m t) -> p w t m", w=2, t=PACK),
+            )
 
         def project(i, codes, scales, weight, fmt, name, tag):
-            acc = bank(tag, [P, R], F32)
-            nc.tensor.matmul_mx(
-                out=acc[:],
-                lhsT=codes[i].bitcast(FP8X4),
-                lhsT_scale=scales[i],
-                rhs=weight[:].bitcast(fmt),
-                rhs_scale=plane(name, 0, R),
-                start=True,
-                stop=True,
-            )
-            return acc
+            acc = bank(tag)
+            if i not in R_FIRST:
+                nc.tensor.matmul_mx(
+                    out=acc[:], lhsT=codes[i].bitcast(FP8X4), lhsT_scale=scales[i],
+                    rhs=weight[:].bitcast(fmt), rhs_scale=plane(name, 0, R), start=True, stop=True,
+                )
+                return acc[:].rearrange("j (m t) -> j t m", t=PACK)
+            pair, base = plane_at[name]
+            columns = dealt_w[name][:].bitcast(fmt)
+            for t in range(PACK):
+                nc.tensor.matmul_mx(
+                    out=acc[:, t * P : (t + 1) * P],
+                    lhsT=columns[:, t * P : (t + 1) * P],
+                    lhsT_scale=dealt_s[pair][:, base + t * P : base + (t + 1) * P],
+                    rhs=codes[i].bitcast(FP8X4), rhs_scale=scales[i], start=True, stop=True,
+                )
+            return acc[:].rearrange("p (t j) -> p j t", t=PACK)
 
-        def by_slot(acc):
-            return acc[:].rearrange("j (m t) -> j t m", t=PACK)
+        def shaped(i, flat):
+            if i in R_FIRST:
+                return flat[:].rearrange("p c (j t) -> p c j t", t=PACK)
+            return flat[:].rearrange("j c (t m) -> j c t m", t=PACK)
 
-        def by_pair(acc):
-            return acc[:].rearrange("j (m u e) -> j u m e", u=2, e=2)
+        def twice(slots):
+            return slots.unsqueeze(1).to_broadcast([P, 2] + list(slots.shape[1:]))
 
-        aer, aei, aer_sb, rel, hr, hq = {}, {}, {}, {}, {}, {}
+        aer, aei, rel, hq, by_aer, by_aei = {}, {}, {}, {}, {}, {}
         hq_group = {}
         for group in GROUPS:
-            hq_group[group] = keep.tile([P, 2, len(group) * P, PACK], BF16, name="hq" + str(group[0]), align_bytes=64)
+            shape, name = [P, 2, len(group) * P, PACK], "hq" + str(group[0])
+            if group == GROUPS[0]:
+                hq_group[group] = late.tile(shape, BF16, name=name, align_bytes=64, offset=12 * R)
+            else:
+                hq_group[group] = keep.tile(shape, BF16, name=name, align_bytes=64)
             for n, i in enumerate(group):
                 hq[i] = hq_group[group][:, :, n * P : (n + 1) * P]
 
-        def relation(i):
-            rel[i] = ring.tile([P, 2, PACK, P], F32, name="rel_sb", align_bytes=64)
+        rel_buffers = [keep.tile([P, 2, R], F32, name="rel_sb" + str(n)) for n in range(5)]
+
+        def relation(i, kinds=("rel", "rel")):
+            rel[i] = shaped(i, rel_buffers[i % 5])
             for part, weight, name in ((0, wrr_w, "wrr"), (1, wri_w, "wri")):
-                nc.scalar.copy(out=rel[i][:, part], in_=by_slot(project(i, w2, s2, weight, FP4X4, name, "rel")))
+                nc.scalar.copy(out=rel[i][:, part], in_=project(i, w2, s2, weight, FP4X4, name, kinds[part]))
 
-        def entity(i):
-            aer[i] = project(i, w1, s1, wer_w, FP8X4, "wer", "ent")
-            if i in SHARED:
-                aer_sb[i] = ring.tile([P, PACK, P], F32, name="aer_sb", bufs=2)
-                nc.scalar.copy(out=aer_sb[i][:], in_=by_slot(aer[i]))
-            aei[i] = project(i, w1, s1, wei_w, FP8X4, "wei", "ent")
+        def entity_real(i):
+            if i in AER_ON_GPSIMD:
+                copied = keep.tile([P, PACK, P], F32, name="aer" + str(i))
+                nc.scalar.copy(out=copied[:], in_=project(i, w1, s1, wer_w, FP8X4, "wer", "rel"))
+                aer[i] = copied[:]
+            else:
+                aer[i] = project(i, w1, s1, wer_w, FP8X4, "wer", "vector")
 
-        def hr_term(name, acc, i, part):
-            made = ring.tile([P, 2, P, 2], F32, name=name)
-            nc.vector.tensor_tensor(
-                out=made[:], in0=by_pair(acc), in1=rel[i][:, part].rearrange("j (u e) m -> j u m e", e=2), op=MULT
+        def entity_imag(i):
+            aei[i] = project(i, w1, s1, wei_w, FP8X4, "wei", "vector")
+
+        def products_of_aer(i):
+            if i == R_FIRST[-1]:
+                made = late.tile([P, 2, R], F32, name="by_aer" + str(i), align_bytes=64, offset=0)
+            elif i == TILES - 1:
+                made = late.tile([P, 2, R], F32, name="by_aer" + str(i), align_bytes=64, offset=8 * R)
+            else:
+                made = ring.tile([P, 2, R], F32, name="by_aer", bufs=4)
+            by_aer[i] = shaped(i, made)
+            engine = nc.gpsimd if i in AER_ON_GPSIMD else nc.vector
+            engine.tensor_tensor(out=by_aer[i], in0=twice(aer[i]), in1=rel[i], op=MULT)
+
+        def imag_imag(i):
+            if i < 2:
+                at = i * 8 * R
+                made = early.tile([P, 2, R], F32, name="by_aei" + str(i), align_bytes=64, offset=at)
+            elif i == TILES - 1:
+                made = late.tile([P, 2, R], F32, name="by_aei" + str(i), align_bytes=64, offset=16 * R)
+            else:
+                made = ring.tile([P, 2, R], F32, name="by_aei", bufs=4)
+            by_aei[i] = shaped(i, made)
+            nc.vector.scalar_tensor_tensor(
+                out=by_aei[i][:, 0], in0=aei[i], scalar=-1.0, in1=rel[i][:, 1], op0=MULT, op1=MULT
             )
-            return made
 
-        def hi_term(name, engine, entity_part, i, part):
-            made = ring.tile([P, PACK, P], F32, name=name, bufs=2)
-            engine.tensor_tensor(out=made[:], in0=entity_part, in1=rel[i][:, part], op=MULT)
-            return made
+        def imag_real(i):
+            nc.vector.tensor_tensor(out=by_aei[i][:, 1], in0=aei[i], in1=rel[i][:, 0], op=MULT)
 
-        def subtract(i, real_real, imag_imag):
-            hr[i] = ring.tile([P, 2, P, 2], BF16, name="hr", bufs=2, align_bytes=64)
-            nc.gpsimd.tensor_tensor(out=hr[i][:], in0=real_real[:], in1=imag_imag[:], op=SUBTRACT)
+        def add_up(i):
+            nc.gpsimd.tensor_tensor(out=hq[i], in0=by_aer[i], in1=by_aei[i], op=ADD)
 
-        def turn_hr(i, tag, copy):
-            words = hr[i][:].rearrange("j u m e -> j (u m e)").bitcast(F32)
-            turned = bank(tag, [P, 2, P], F32)
-            for u in range(2):
-                nc.tensor.transpose(turned[:, u, :], words[:, u * P : (u + 1) * P], ident[:])
-            pairs = hq[i][:, 0].rearrange("p j t -> p (j t)").bitcast(F32).rearrange("p (j u) -> p j u", u=2)
-            copy(pairs, turned[:].rearrange("p u j -> p j u"))
+        turned = {}
 
-        def turn_hi(i, terms):
-            turned = bank("turned_hi", [P, PACK, P], F32)
-            for n, term in enumerate(terms):
-                for t in range(PACK):
-                    nc.tensor.matmul(
-                        out=turned[:, t, :], lhsT=term[:, t, :], rhs=ident[:], is_transpose=True,
-                        start=(n == 0 and t == 0), stop=(n == 1 and t == PACK - 1),
-                    )
-            nc.scalar.copy(out=hq[i][:, 1], in_=turned[:].rearrange("p t j -> p j t"))
+        def turn(i, part, term):
+            first = (i, part) not in turned
+            if first:
+                turned[i, part] = bank("scalar")[:].rearrange("p (t j) -> p t j", t=PACK)
+            for t in range(PACK):
+                nc.tensor.matmul(
+                    out=turned[i, part][:, t, :], lhsT=term[i][:, part, t, :], rhs=ident[:], is_transpose=True,
+                    start=(first and t == 0), stop=(not first and t == PACK - 1),
+                )
+            if not first:
+                nc.scalar.copy(out=hq[i][:, part], in_=turned[i, part].rearrange("p t j -> p j t"))
 
-        def quantise(group, room, lo, hi):
-            codes, scales = room
+        def turn_sum(i, part):
+            for term in (by_aer, by_aei) if i in AER_ON_GPSIMD and i > 1 else (by_aei, by_aer):
+                turn(i, part, term)
+
+        room = {}
+
+        def quantise(group, lo, hi):
             width = len(group) * P
+            if group not in room:
+                name = str(group[0])
+                if group in GROUPS[0:2]:
+                    codes = late.tile([P, 2 * width], U32, name="codes" + name, align_bytes=64, offset=4 * R * GROUPS.index(group))
+                else:
+                    codes = kept("codes" + name, 2 * width, U32)
+                room[group] = (codes, kept("scales" + name, 2 * width, U8))
+            codes, scales = room[group]
             nc.vector.quantize_mx(
                 out=codes[:, lo * width : hi * width].bitcast(FP8X4),
                 scales=scales[:, lo * width : hi * width],
                 in_=hq_group[group][:, lo:hi].rearrange("p c j t -> p (c j t)"),
             )
 
-        def score_pass(y, group, room, part, h):
-            codes, scales = room
+        def score_pass(y, group, part, h):
+            codes, scales = room[group]
             width = len(group) * P
             if part == 0:
                 weight = nr_w[:, h * P : (h + 1) * P].bitcast(FP8X4)
             else:
                 weight = ni_w[:, h * P // 2 : (h + 1) * P // 2].bitcast(FP4X4)
             nc.tensor.matmul_mx(
-                out=y,
-                lhsT=weight,
-                lhsT_scale=plane(("nr", "ni")[part], h * P, (h + 1) * P),
+                out=y, lhsT=weight, lhsT_scale=plane(("nr", "ni")[part], h * P, (h + 1) * P),
                 rhs=codes[:, part * width : (part + 1) * width].bitcast(FP8X4),
                 rhs_scale=scales[:, part * width : (part + 1) * width],
-                start=(part == 0),
-                stop=(part == 1),
+                start=(part == 0), stop=(part == 1),
             )
 
-        def quantised_tiles(groups):
-            room = ring.tile([P, 2 * R], U32, name="rel_sb", align_bytes=64)
-            planes = room[:, 6 * P :].bitcast(U8)
-            found = {}
-            for group in groups:
-                lo = 2 * P * (group[0] - groups[0][0])
-                hi = lo + 2 * P * len(group)
-                found[group] = (room[:, lo:hi], planes[:, lo:hi])
-            return found
-
-        def score(group, tag, room):
+        def score(group):
             width = len(group) * P
-            y = bank(tag, [P, N // P, width], F32)
-            quantise(group, room, 0, 2)
+            y = bank("rel")[:, 0 : N // P * width].rearrange("p (h j) -> p h j", j=width)
             for h in range(N // P):
                 for part in range(2):
-                    score_pass(y[:, h, :], group, room, part, h)
+                    score_pass(y[:, h, :], group, part, h)
             y_sb = keep.tile([P, N // P, width], F32, name="y_sb" + str(group[0]))
-            nc.scalar.copy(out=y_sb[:], in_=y[:])
+            nc.scalar.copy(out=y_sb[:], in_=y)
             columns = out[:, group[0] * P : group[0] * P + width]
             nc.sync.dma_start(out=columns.rearrange("(h p) j -> p h j", p=P), in_=y_sb[:])
 
-        def score_last(group, room):
+        def score_last(group):
             i = group[0]
-            y = [bank("ent", [P, P], F32) for h in range(N // P)]
+            y = [bank("vector")[:, 0:P], bank("vector")[:, 0:P]]
             for part in range(2):
-                quantise(group, room, part, part + 1)
+                quantise(group, part, part + 1)
                 for h in range(N // P):
-                    score_pass(y[h][:], group, room, part, h)
+                    score_pass(y[h], group, part, h)
             low = keep.tile([P, P], F32, name="last_low")
-            nc.vector.tensor_copy(low[:], y[0][:])
+            nc.vector.tensor_copy(low[:], y[0])
             nc.sync.dma_start(out=out[0:P, i * P : (i + 1) * P], in_=low[:])
             high = keep.tile([P, P], F32, name="last_high")
-            nc.scalar.copy(out=high[:], in_=y[1][:])
+            nc.scalar.copy(out=high[:], in_=y[1])
             nc.scalar.dma_start(out=out[P:N, i * P : (i + 1) * P], in_=high[:])
 
-        for c in range(3):
-            gather_relation(c)
-        for c in range(2):
-            gather_entity(c)
-        relation(0)
-        entity(0)
-        relation(1)
-        entity(1)
-        relation(2)
+        gather(s2, kept("s2", J, U8), tab2_s, list2, 0, J)
+        gather(w2, kept("w2_first", CHUNK, U32), tab2_w, list2, 0, CHUNK)
+        w2_mid = early.tile([P, P], U32, name="w2_mid", align_bytes=64, offset=8 * R - 2 * P)
+        gather(w2, w2_mid, tab2_w, list2, CHUNK, CHUNK + P)
+        gather(w2, kept("w2_rest", J - CHUNK - P, U32), tab2_w, list2, CHUNK + P, J)
+        gather(w1, held.tile([P, CHUNK], U32, name="w1_first", align_bytes=64, offset=4 * R - 2 * CHUNK), tab1_w, list1, 0, CHUNK)
+        gather(s1, held.tile([P, CHUNK], U8, name="s1_first", align_bytes=64, offset=8 * R), tab1_s, list1, 0, CHUNK)
+        gather(s1, kept("s1_rest", J - CHUNK, U8), tab1_s, list1, CHUNK, J)
+        gather(w1, held.tile([P, J - CHUNK], U32, name="w1_rest", align_bytes=64, offset=8 * R), tab1_w, list1, CHUNK, J)
+        deal_words("wrr", wrr_w, U16)
+        deal_words("wri", wri_w, U16)
+        deal_scales("rel")
+        deal_scales("ent")
+        relation(0, ("rel", "scalar"))
+        relation(1, ("scalar", "scalar"))
+        entity_real(0)
+        entity_real(1)
+        relation(2, ("vector", "rel"))
+        entity_imag(0)
+        entity_imag(1)
+        products_of_aer(0)
+        products_of_aer(1)
+        deal_words("wer", wer_w, U32)
+        deal_words("wei", wei_w, U32)
+        relation(3)
+        entity_real(2)
+        entity_real(3)
 
-        for i in range(TILES):
-            real_real = hr_term("real_real", aer[i], i, 0)
-            if i == TILES - 2:
-                score(GROUPS[0], "rel", quantised_tiles(GROUPS[0:1])[GROUPS[0]])
-            if i == TILES - 1:
-                room = quantised_tiles(GROUPS[1:3])
-                score(GROUPS[1], "rel", room[GROUPS[1]])
-                score(GROUPS[2], "ent", room[GROUPS[2]])
-            if 1 <= i < TILES - 2:
-                relation(i + 2)
-            if i == 0:
-                gather_relation(J // CHUNK - 1)
-            imag_imag = hr_term("imag_imag", aei[i], i, 1)
-            if i in SHARED:
-                real_imag = hi_term("real_imag", nc.gpsimd, aer_sb[i][:], i, 1)
-            subtract(i, real_real, imag_imag)
-            if 2 <= i + 1 < J // CHUNK:
-                gather_entity(i + 1)
-            if i >= 1:
-                turn_hr(i - 1, "y", nc.scalar.copy)
-            if i not in SHARED:
-                real_imag = hi_term("real_imag", nc.vector, by_slot(aer[i]), i, 1)
-            imag_real = hi_term("imag_real", nc.vector, by_slot(aei[i]), i, 0)
-            turn_hi(i, (real_imag, imag_real))
-            if i + 2 < TILES:
-                entity(i + 2)
-        turn_hr(TILES - 1, "y", nc.vector.tensor_copy)
+        imag_imag(0)
+        imag_real(0)
+        entity_imag(2)
+        relation(4)
+        imag_imag(1)
+        imag_real(1)
+        entity_imag(3)
+        products_of_aer(3)
+        turn_sum(0, 0)
+        turn_sum(0, 1)
 
-        room = quantised_tiles(GROUPS[3:])
-        score(GROUPS[3], "ent", room[GROUPS[3]])
-        score(GROUPS[4], "rel", room[GROUPS[4]])
-        score_last(GROUPS[5], room[GROUPS[5]])
+        products_of_aer(2)
+        entity_real(4)
+        relation(5)
+        imag_imag(2)
+        imag_real(2)
+        entity_imag(4)
+        add_up(2)
+        turn_sum(1, 0)
+        turn_sum(1, 1)
+
+        imag_imag(3)
+        imag_real(3)
+        entity_real(5)
+
+        products_of_aer(4)
+        entity_imag(5)
+        relation(6)
+        imag_imag(4)
+        imag_real(4)
+        add_up(4)
+        entity_real(6)
+        turn_sum(3, 0)
+        turn_sum(3, 1)
+
+        products_of_aer(5)
+        entity_imag(6)
+        relation(7)
+        imag_imag(5)
+        imag_real(5)
+        add_up(5)
+        entity_real(7)
+
+        products_of_aer(6)
+        entity_imag(7)
+        imag_imag(6)
+        turn_sum(6, 0)
+        imag_real(6)
+        turn_sum(6, 1)
+        quantise(GROUPS[0], 0, 2)
+
+        products_of_aer(7)
+        score(GROUPS[0])
+        turn(7, 0, by_aer)
+        turn(7, 1, by_aer)
+        quantise(GROUPS[1], 0, 2)
+        imag_imag(7)
+        imag_real(7)
+        turn(7, 0, by_aei)
+        turn(7, 1, by_aei)
+        score(GROUPS[1])
+        for group in GROUPS[2:4]:
+            quantise(group, 0, 2)
+            score(group)
+        score_last(GROUPS[4])

@@ -22,9 +22,10 @@ PACK = 4
 ROWS = 16
 TILES = J // P
 CHUNK = 2 * P
+PARTS = ((0, CHUNK), (CHUNK, J))
 GROUPS = ((0, 1), (2, 3), (4, 5), (6,), (7,))
-AER_ON_GPSIMD = (0, 1, 3)
-R_FIRST = (2, 4, 5)
+AER_ON_GPSIMD = (0, 1, 2)
+R_FIRST = (3, 4, 5)
 
 
 def tile_list_ckg_none_kernel(
@@ -34,7 +35,8 @@ def tile_list_ckg_none_kernel(
     nc = tc.nc
     with ExitStack() as ctx:
         keep = ctx.enter_context(tc.tile_pool(name="keep", bufs=1))
-        early = ctx.enter_context(tc.tile_pool(name="early", bufs=1))
+        first = ctx.enter_context(tc.tile_pool(name="first", bufs=1))
+        second = ctx.enter_context(tc.tile_pool(name="second", bufs=1))
         held = ctx.enter_context(tc.tile_pool(name="held", bufs=1))
         late = ctx.enter_context(tc.tile_pool(name="late", bufs=1))
         ring = ctx.enter_context(tc.tile_pool(name="ring", bufs=3))
@@ -45,24 +47,38 @@ def tile_list_ckg_none_kernel(
 
         list1 = keep.tile([P, J // 16], U16, name="list1")
         list2 = keep.tile([P, J // 16], U16, name="list2")
-        tab1_w, tab2_w = kept("tab1_w", T), kept("tab2_w", T)
-        tab1_s, tab2_s = kept("tab1_s", T // 4), kept("tab2_s", T // 4)
-        wrr_w, wri_w = kept("wrr_w", R // 2), kept("wri_w", R // 2)
-        wer_w, wei_w = kept("wer_w", R), kept("wei_w", R)
-        nr_w, ni_w = kept("nr_w", N), kept("ni_w", N // 2)
-        staged = {
-            "rel": kept("staged_rel", R // 2),
-            "ent": kept("staged_ent", R // 2),
-            "out": kept("staged_out", N // 2),
-        }
-        planes = {"rel": kept("planes_rel", R // 2), "ent": kept("planes_ent", R // 2), "out": kept("planes_out", N // 2)}
+        tab1_w = keep.tile([P, T], I32, name="tab1_w", align_bytes=64)
+        tab2_w = keep.tile([P, T], I32, name="tab2_w", align_bytes=64)
+        tab1_s = keep.tile([P, T // 4], I32, name="tab1_s", align_bytes=64)
+        tab2_s = keep.tile([P, T // 4], I32, name="tab2_s", align_bytes=64)
+        wrr_w = keep.tile([P, R // 2], I32, name="wrr_w", align_bytes=64)
+        wri_w = keep.tile([P, R // 2], I32, name="wri_w", align_bytes=64)
+
+        wer_w = first.tile([P, R], I32, name="wer_w", align_bytes=64, offset=0)
+        wei_w = first.tile([P, R], I32, name="wei_w", align_bytes=64, offset=4 * R)
+        staged1 = first.tile([P, R], I32, name="staged1", align_bytes=64, offset=0)
+        picked_s = [
+            first.tile([P, 2 * CHUNK], U8, name="picked_s0", align_bytes=64, offset=4 * R),
+            second.tile([P, 2 * (J - CHUNK)], U8, name="picked_s1", align_bytes=64, offset=2 * N),
+        ]
+        nr_w = second.tile([P, N], I32, name="nr_w", align_bytes=64, offset=0)
+        staged2 = second.tile([P, N // 2], I32, name="staged2", align_bytes=64, offset=4 * N)
+        ni_w = second.tile([P, N // 2], I32, name="ni_w", align_bytes=64, offset=6 * N)
+
+        planes_t = [keep.tile([P, (hi - lo) // 2], I32, name="planes_t" + str(lo), align_bytes=64) for lo, hi in PARTS]
+        planes1 = keep.tile([P, R], I32, name="planes1", align_bytes=64)
+        planes2 = keep.tile([P, N // 2], I32, name="planes2", align_bytes=64)
         ident = keep.tile([P, P], F32, name="ident")
 
-        plane_at = {"wrr": ("rel", 0), "wri": ("rel", R), "wer": ("ent", 0), "wei": ("ent", R), "nr": ("out", 0), "ni": ("out", N)}
+        plane_at = {
+            "wrr": (staged1, planes1, 0), "wri": (staged1, planes1, R),
+            "wer": (staged1, planes1, 2 * R), "wei": (staged1, planes1, 3 * R),
+            "nr": (staged2, planes2, 0), "ni": (staged2, planes2, N),
+        }
 
         def plane(name, lo, hi):
-            pair, base = plane_at[name]
-            return planes[pair][:].bitcast(U8)[:, base + lo : base + hi]
+            tile, base = plane_at[name][1:]
+            return tile[:].bitcast(U8)[:, base + lo : base + hi]
 
         def load_words(queue, tile, words):
             src = words[0]
@@ -70,54 +86,86 @@ def tile_list_ckg_none_kernel(
                 src = src.rearrange("p n t -> p (n t)")
             queue.dma_start(out=tile[:], in_=src.bitcast(I32))
 
+        def load_table_words(tile, words):
+            src = words[0].rearrange("p n t -> p (n t)").bitcast(I32)
+            for lo in range(0, T, T // 2):
+                nc.gpsimd.dma_start(out=tile[:, lo : lo + T // 2], in_=src[:, lo : lo + T // 2])
+
+        def load_table_scales(queue, tile, scales):
+            queue.dma_start(out=tile[P - ROWS : P, :], in_=scales[0].bitcast(I32))
+
         def stage_scales(queue, name, scales):
-            pair, base = plane_at[name]
+            tile, base = plane_at[name][0], plane_at[name][2]
             rows = scales[0].bitcast(I32)
-            queue.dma_start(out=staged[pair][0:ROWS, base // 4 : base // 4 + rows.shape[1]], in_=rows)
+            queue.dma_start(out=tile[0:ROWS, base // 4 : base // 4 + rows.shape[1]], in_=rows)
 
-        def place_rows(queues, tile, rows):
+        def spread_scales(queues, planes, rows, first_row):
             for q in range(4):
-                queues[q].dma_start(out=tile[32 * q : 32 * q + 4, :], in_=rows[4 * q : 4 * q + 4, :])
+                at = first_row + 4 * q
+                queues[q % len(queues)].dma_start(out=planes[32 * q : 32 * q + 4, :], in_=rows[at : at + 4, :])
 
-        nc.vector.memset(tab2_s[:], 0)
-        nc.vector.memset(planes["rel"][:], 0)
-        nc.vector.memset(tab1_s[:], 0)
-        nc.vector.memset(planes["ent"][:], 0)
-        nc.vector.memset(planes["out"][:], 0)
-        load_words(nc.gpsimd, tab2_w, tab2_words)
+        nc.vector.memset(tab2_s[0 : P - ROWS, :], 0)
+        nc.vector.memset(tab1_s[0 : P - ROWS, :], 0)
+        nc.vector.memset(planes1[:], 0)
+        nc.vector.memset(planes_t[0][:], 0)
+        load_table_words(tab2_w, tab2_words)
+        load_table_words(tab1_w, tab_words)
+        nc.gpsimd.memset(planes_t[1][:], 0)
+        nc.gpsimd.memset(planes2[:], 0)
         make_identity(nc, ident[:])
-        load_words(nc.gpsimd, tab1_w, tab_words)
-        load_words(nc.gpsimd, wer_w, wer_words)
-        load_words(nc.gpsimd, wei_w, wei_words)
 
-        sync, scalar = nc.sync, nc.scalar
-        sync.dma_start(list2[:], offs2)
-        stage_scales(scalar, "wrr", wrr_scales)
-        stage_scales(sync, "wri", wri_scales)
-        stage_scales(scalar, "wer", wer_scales)
-        place_rows((sync, scalar, sync, scalar), tab2_s, tab2_scales[0].bitcast(I32))
+        nc.sync.dma_start(list2[:], offs2)
+        nc.sync.dma_start(list1[:], offs)
+        stage_scales(nc.scalar, "wrr", wrr_scales)
+        stage_scales(nc.scalar, "wri", wri_scales)
+        stage_scales(nc.sync, "wer", wer_scales)
+        stage_scales(nc.scalar, "wei", wei_scales)
+        load_table_scales(nc.sync, tab2_s, tab2_scales)
+        load_table_scales(nc.scalar, tab1_s, tab_scales)
+        load_words(nc.sync, wrr_w, wrr_words)
+        load_words(nc.scalar, wri_w, wri_words)
+        spread_scales((nc.sync, nc.scalar), planes1, staged1, 0)
+        load_words(nc.scalar, wer_w, wer_words)
 
-        load_words(sync, wrr_w, wrr_words)
-        load_words(sync, wri_w, wri_words)
-        place_rows((sync, sync, sync, sync), planes["rel"], staged["rel"])
-        sync.dma_start(list1[:], offs)
-        stage_scales(sync, "wei", wei_scales)
-        place_rows((sync, sync, sync, sync), tab1_s, tab_scales[0].bitcast(I32))
-        place_rows((sync, sync, sync, sync), planes["ent"], staged["ent"])
-
-        stage_scales(sync, "nr", nr_scales)
-        stage_scales(sync, "ni", ni_scales)
-        load_words(sync, nr_w, nr_words)
-        load_words(sync, ni_w, ni_words)
-        place_rows((sync, sync, sync, sync), planes["out"], staged["out"])
+        def gather(picked, table, view, offsets, lo, hi):
+            nc.vector.tensor_copy(picked, table[:].bitcast(view).indirect(offsets[:, lo // 16 : hi // 16]))
 
         s1, s2, w1, w2 = {}, {}, {}, {}
 
-        def gather(found, picked, table, offsets, lo, hi):
-            window = table[:].bitcast(picked.dtype)
-            nc.vector.tensor_copy(picked[:], window.indirect(offsets[:, lo // 16 : hi // 16]))
+        def gather_scales(part):
+            lo, hi = PARTS[part]
+            width = hi - lo
+            gather(picked_s[part][:, 0:width], tab2_s, U8, list2, lo, hi)
+            gather(picked_s[part][:, width : 2 * width], tab1_s, U8, list1, lo, hi)
+            spread_scales((nc.sync,), planes_t[part], picked_s[part][:].bitcast(I32), P - ROWS)
             for i in range(lo // P, hi // P):
-                found[i] = picked[:, i * P - lo : (i + 1) * P - lo]
+                s2[i] = planes_t[part][:].bitcast(U8)[:, i * P - lo : (i + 1) * P - lo]
+                s1[i] = planes_t[part][:].bitcast(U8)[:, width + i * P - lo : width + (i + 1) * P - lo]
+
+        gather_scales(0)
+        load_words(nc.sync, wei_w, wei_words)
+        gather_scales(1)
+
+        stage_scales(nc.sync, "nr", nr_scales)
+        stage_scales(nc.sync, "ni", ni_scales)
+        load_words(nc.sync, nr_w, nr_words)
+        load_words(nc.sync, ni_w, ni_words)
+        spread_scales((nc.sync,), planes2, staged2, 0)
+
+        def gather_words(found, table, offsets, name, c, bufs):
+            if found is w1 and c == 0:
+                picked = held.tile([P, CHUNK], U32, name="w1_first", align_bytes=64, offset=0)
+            else:
+                picked = ring.tile([P, CHUNK], U32, name=name, bufs=bufs, align_bytes=64)
+            gather(picked[:], table, U32, offsets, c * CHUNK, (c + 1) * CHUNK)
+            for n in range(CHUNK // P):
+                found[c * CHUNK // P + n] = picked[:, n * P : (n + 1) * P]
+
+        def gather_relation(c):
+            gather_words(w2, tab2_w, list2, "w2", c, 3)
+
+        def gather_entity(c):
+            gather_words(w1, tab1_w, list1, "w1", c, 3)
 
         banks = {
             kind: [psum.tile([P, R], F32, name=kind + str(n)) for n in range(count)]
@@ -131,21 +179,20 @@ def tile_list_ckg_none_kernel(
 
         dealt_w = {
             "wrr": kept("wrr_dealt", R // 2), "wri": kept("wri_dealt", R // 2),
-            "wer": held.tile([P, R], I32, name="wer_dealt", align_bytes=64, offset=0),
-            "wei": held.tile([P, R], I32, name="wei_dealt", align_bytes=64, offset=4 * R),
+            "wer": kept("wer_dealt", R), "wei": held.tile([P, R], I32, name="wei_dealt", align_bytes=64, offset=0),
         }
-        dealt_s = {"rel": kept("rel_dealt", 2 * R, U8), "ent": kept("ent_dealt", 2 * R, U8)}
+        dealt_s = kept("planes_dealt", 4 * R, U8)
 
-        def deal_words(name, weight, word):
-            nc.scalar.copy(
-                out=dealt_w[name][:].bitcast(word).rearrange("p (t m) -> p m t", t=PACK),
-                in_=weight[:].bitcast(word).rearrange("p (m t) -> p m t", t=PACK),
+        def dealt_views(name, weight, word, run):
+            return (
+                dealt_w[name][:].bitcast(word).rearrange("p (t c i) -> p c t i", t=PACK, i=run),
+                weight[:].bitcast(word).rearrange("p (c i t) -> p c t i", t=PACK, i=run),
             )
 
-        def deal_scales(pair):
+        def deal_scales():
             nc.gpsimd.tensor_copy(
-                dealt_s[pair][:].rearrange("p (w t m) -> p w t m", w=2, t=PACK),
-                planes[pair][:].bitcast(U8).rearrange("p (w m t) -> p w t m", w=2, t=PACK),
+                dealt_s[:].rearrange("p (w t m) -> p w t m", w=4, t=PACK),
+                planes1[:].bitcast(U8).rearrange("p (w m t) -> p w t m", w=4, t=PACK),
             )
 
         def project(i, codes, scales, weight, fmt, name, tag):
@@ -156,13 +203,13 @@ def tile_list_ckg_none_kernel(
                     rhs=weight[:].bitcast(fmt), rhs_scale=plane(name, 0, R), start=True, stop=True,
                 )
                 return acc[:].rearrange("j (m t) -> j t m", t=PACK)
-            pair, base = plane_at[name]
+            base = plane_at[name][2]
             columns = dealt_w[name][:].bitcast(fmt)
             for t in range(PACK):
                 nc.tensor.matmul_mx(
                     out=acc[:, t * P : (t + 1) * P],
                     lhsT=columns[:, t * P : (t + 1) * P],
-                    lhsT_scale=dealt_s[pair][:, base + t * P : base + (t + 1) * P],
+                    lhsT_scale=dealt_s[:, base + t * P : base + (t + 1) * P],
                     rhs=codes[i].bitcast(FP8X4), rhs_scale=scales[i], start=True, stop=True,
                 )
             return acc[:].rearrange("p (t j) -> p j t", t=PACK)
@@ -178,25 +225,25 @@ def tile_list_ckg_none_kernel(
         aer, aei, rel, hq, by_aer, by_aei = {}, {}, {}, {}, {}, {}
         hq_group = {}
         for group in GROUPS:
-            shape, name = [P, 2, len(group) * P, PACK], "hq" + str(group[0])
-            if group == GROUPS[0]:
-                hq_group[group] = late.tile(shape, BF16, name=name, align_bytes=64, offset=12 * R)
-            else:
-                hq_group[group] = keep.tile(shape, BF16, name=name, align_bytes=64)
+            hq_group[group] = keep.tile([P, 2, len(group) * P, PACK], BF16, name="hq" + str(group[0]), align_bytes=64)
             for n, i in enumerate(group):
                 hq[i] = hq_group[group][:, :, n * P : (n + 1) * P]
 
-        rel_buffers = [keep.tile([P, 2, R], F32, name="rel_sb" + str(n)) for n in range(5)]
+        rel_buffers = [keep.tile([P, 2, R], F32, name="rel_sb" + str(n)) for n in range(6)]
 
-        def relation(i, kinds=("rel", "rel")):
-            rel[i] = shaped(i, rel_buffers[i % 5])
-            for part, weight, name in ((0, wrr_w, "wrr"), (1, wri_w, "wri")):
+        def relation(i, kinds=("rel", "rel"), parts=(0, 1)):
+            if i == TILES - 2:
+                rel[i] = shaped(i, late.tile([P, 2, R], F32, name="rel_late", align_bytes=64, offset=8 * R))
+            else:
+                rel[i] = shaped(i, rel_buffers[i % 6])
+            for part in parts:
+                weight, name = ((wrr_w, "wrr"), (wri_w, "wri"))[part]
                 nc.scalar.copy(out=rel[i][:, part], in_=project(i, w2, s2, weight, FP4X4, name, kinds[part]))
 
-        def entity_real(i):
+        def entity_real(i, kind="rel"):
             if i in AER_ON_GPSIMD:
                 copied = keep.tile([P, PACK, P], F32, name="aer" + str(i))
-                nc.scalar.copy(out=copied[:], in_=project(i, w1, s1, wer_w, FP8X4, "wer", "rel"))
+                nc.scalar.copy(out=copied[:], in_=project(i, w1, s1, wer_w, FP8X4, "wer", kind))
                 aer[i] = copied[:]
             else:
                 aer[i] = project(i, w1, s1, wer_w, FP8X4, "wer", "vector")
@@ -207,8 +254,6 @@ def tile_list_ckg_none_kernel(
         def products_of_aer(i):
             if i == R_FIRST[-1]:
                 made = late.tile([P, 2, R], F32, name="by_aer" + str(i), align_bytes=64, offset=0)
-            elif i == TILES - 1:
-                made = late.tile([P, 2, R], F32, name="by_aer" + str(i), align_bytes=64, offset=8 * R)
             else:
                 made = ring.tile([P, 2, R], F32, name="by_aer", bufs=4)
             by_aer[i] = shaped(i, made)
@@ -216,13 +261,7 @@ def tile_list_ckg_none_kernel(
             engine.tensor_tensor(out=by_aer[i], in0=twice(aer[i]), in1=rel[i], op=MULT)
 
         def imag_imag(i):
-            if i < 2:
-                at = i * 8 * R
-                made = early.tile([P, 2, R], F32, name="by_aei" + str(i), align_bytes=64, offset=at)
-            elif i == TILES - 1:
-                made = late.tile([P, 2, R], F32, name="by_aei" + str(i), align_bytes=64, offset=16 * R)
-            else:
-                made = ring.tile([P, 2, R], F32, name="by_aei", bufs=4)
+            made = ring.tile([P, 2, R], F32, name="by_aei", bufs=4)
             by_aei[i] = shaped(i, made)
             nc.vector.scalar_tensor_tensor(
                 out=by_aei[i][:, 0], in0=aei[i], scalar=-1.0, in1=rel[i][:, 1], op0=MULT, op1=MULT
@@ -236,10 +275,10 @@ def tile_list_ckg_none_kernel(
 
         turned = {}
 
-        def turn(i, part, term):
+        def turn(i, part, term, kind="scalar"):
             first = (i, part) not in turned
             if first:
-                turned[i, part] = bank("scalar")[:].rearrange("p (t j) -> p t j", t=PACK)
+                turned[i, part] = bank(kind)[:].rearrange("p (t j) -> p t j", t=PACK)
             for t in range(PACK):
                 nc.tensor.matmul(
                     out=turned[i, part][:, t, :], lhsT=term[i][:, part, t, :], rhs=ident[:], is_transpose=True,
@@ -248,21 +287,21 @@ def tile_list_ckg_none_kernel(
             if not first:
                 nc.scalar.copy(out=hq[i][:, part], in_=turned[i, part].rearrange("p t j -> p j t"))
 
-        def turn_sum(i, part):
-            for term in (by_aer, by_aei) if i in AER_ON_GPSIMD and i > 1 else (by_aei, by_aer):
-                turn(i, part, term)
+        def turn_sum(i, part, kind="scalar"):
+            for term in (by_aei, by_aer):
+                turn(i, part, term, kind)
 
         room = {}
 
+        def make_room():
+            codes = late.tile([P, 2 * J], U32, name="codes", align_bytes=64, offset=4 * R)
+            scales = kept("scales", 2 * J, U8)
+            for group in GROUPS:
+                lo, hi = 2 * P * group[0], 2 * P * (group[-1] + 1)
+                room[group] = (codes[:, lo:hi], scales[:, lo:hi])
+
         def quantise(group, lo, hi):
             width = len(group) * P
-            if group not in room:
-                name = str(group[0])
-                if group in GROUPS[0:2]:
-                    codes = late.tile([P, 2 * width], U32, name="codes" + name, align_bytes=64, offset=4 * R * GROUPS.index(group))
-                else:
-                    codes = kept("codes" + name, 2 * width, U32)
-                room[group] = (codes, kept("scales" + name, 2 * width, U8))
             codes, scales = room[group]
             nc.vector.quantize_mx(
                 out=codes[:, lo * width : hi * width].bitcast(FP8X4),
@@ -284,22 +323,21 @@ def tile_list_ckg_none_kernel(
                 start=(part == 0), stop=(part == 1),
             )
 
-        def score(group):
+        def score(group, kind, copy):
             width = len(group) * P
-            y = bank("rel")[:, 0 : N // P * width].rearrange("p (h j) -> p h j", j=width)
+            y = bank(kind)[:, 0 : N // P * width].rearrange("p (h j) -> p h j", j=width)
             for h in range(N // P):
                 for part in range(2):
                     score_pass(y[:, h, :], group, part, h)
             y_sb = keep.tile([P, N // P, width], F32, name="y_sb" + str(group[0]))
-            nc.scalar.copy(out=y_sb[:], in_=y)
+            copy(y_sb[:], y)
             columns = out[:, group[0] * P : group[0] * P + width]
             nc.sync.dma_start(out=columns.rearrange("(h p) j -> p h j", p=P), in_=y_sb[:])
 
         def score_last(group):
             i = group[0]
-            y = [bank("vector")[:, 0:P], bank("vector")[:, 0:P]]
+            y = [bank("vector")[:, 0:P], bank("rel")[:, 0:P]]
             for part in range(2):
-                quantise(group, part, part + 1)
                 for h in range(N // P):
                     score_pass(y[h], group, part, h)
             low = keep.tile([P, P], F32, name="last_low")
@@ -309,76 +347,54 @@ def tile_list_ckg_none_kernel(
             nc.scalar.copy(out=high[:], in_=y[1])
             nc.scalar.dma_start(out=out[P:N, i * P : (i + 1) * P], in_=high[:])
 
-        gather(s2, kept("s2", J, U8), tab2_s, list2, 0, J)
-        gather(w2, kept("w2_first", CHUNK, U32), tab2_w, list2, 0, CHUNK)
-        w2_mid = early.tile([P, P], U32, name="w2_mid", align_bytes=64, offset=8 * R - 2 * P)
-        gather(w2, w2_mid, tab2_w, list2, CHUNK, CHUNK + P)
-        gather(w2, kept("w2_rest", J - CHUNK - P, U32), tab2_w, list2, CHUNK + P, J)
-        gather(w1, held.tile([P, CHUNK], U32, name="w1_first", align_bytes=64, offset=4 * R - 2 * CHUNK), tab1_w, list1, 0, CHUNK)
-        gather(s1, held.tile([P, CHUNK], U8, name="s1_first", align_bytes=64, offset=8 * R), tab1_s, list1, 0, CHUNK)
-        gather(s1, kept("s1_rest", J - CHUNK, U8), tab1_s, list1, CHUNK, J)
-        gather(w1, held.tile([P, J - CHUNK], U32, name="w1_rest", align_bytes=64, offset=8 * R), tab1_w, list1, CHUNK, J)
-        deal_words("wrr", wrr_w, U16)
-        deal_words("wri", wri_w, U16)
-        deal_scales("rel")
-        deal_scales("ent")
-        relation(0, ("rel", "scalar"))
-        relation(1, ("scalar", "scalar"))
+        for c in range(3):
+            gather_relation(c)
+        for c in range(J // CHUNK):
+            gather_entity(c)
+        deal_scales()
+        nc.scalar.copy(*dealt_views("wrr", wrr_w, U16, 8))
+        nc.scalar.copy(*dealt_views("wri", wri_w, U16, 8))
+        nc.gpsimd.tensor_copy(*dealt_views("wer", wer_w, U32, 4))
+        relation(0)
         entity_real(0)
-        entity_real(1)
-        relation(2, ("vector", "rel"))
-        entity_imag(0)
-        entity_imag(1)
         products_of_aer(0)
+        relation(1, ("scalar", "rel"), (0,))
+        entity_real(1)
+        relation(1, ("scalar", "rel"), (1,))
         products_of_aer(1)
-        deal_words("wer", wer_w, U32)
-        deal_words("wei", wei_w, U32)
-        relation(3)
+        for i in AER_ON_GPSIMD:
+            entity_imag(i)
+        relation(2)
+        nc.scalar.copy(*dealt_views("wei", wei_w, U32, 4))
+        relation(3, ("scalar", "scalar"))
+        gather_relation(3)
         entity_real(2)
-        entity_real(3)
-
-        imag_imag(0)
-        imag_real(0)
-        entity_imag(2)
-        relation(4)
-        imag_imag(1)
-        imag_real(1)
-        entity_imag(3)
-        products_of_aer(3)
-        turn_sum(0, 0)
-        turn_sum(0, 1)
-
         products_of_aer(2)
+        relation(4)
+
+        for i in AER_ON_GPSIMD:
+            imag_imag(i)
+            imag_real(i)
+        entity_real(3)
+        entity_imag(3)
         entity_real(4)
+
+        banks["pair"] = banks["scalar"][1:3]
         relation(5)
-        imag_imag(2)
-        imag_real(2)
-        entity_imag(4)
-        add_up(2)
-        turn_sum(1, 0)
-        turn_sum(1, 1)
-
-        imag_imag(3)
-        imag_real(3)
-        entity_real(5)
-
-        products_of_aer(4)
-        entity_imag(5)
-        relation(6)
-        imag_imag(4)
-        imag_real(4)
-        add_up(4)
-        entity_real(6)
-        turn_sum(3, 0)
-        turn_sum(3, 1)
-
-        products_of_aer(5)
-        entity_imag(6)
-        relation(7)
-        imag_imag(5)
-        imag_real(5)
-        add_up(5)
-        entity_real(7)
+        turn_sum(0, 0, "pair")
+        turn_sum(0, 1, "pair")
+        for i in R_FIRST:
+            products_of_aer(i)
+            entity_imag(i + 1)
+            if i + 3 < TILES:
+                relation(i + 3)
+            imag_imag(i)
+            imag_real(i)
+            add_up(i)
+            entity_real(i + 2)
+            if i - 2 in AER_ON_GPSIMD:
+                turn_sum(i - 2, 0, "pair")
+                turn_sum(i - 2, 1, "pair")
 
         products_of_aer(6)
         entity_imag(7)
@@ -386,19 +402,23 @@ def tile_list_ckg_none_kernel(
         turn_sum(6, 0)
         imag_real(6)
         turn_sum(6, 1)
-        quantise(GROUPS[0], 0, 2)
 
+        make_room()
         products_of_aer(7)
-        score(GROUPS[0])
         turn(7, 0, by_aer)
         turn(7, 1, by_aer)
-        quantise(GROUPS[1], 0, 2)
+        for group in GROUPS[0:2]:
+            quantise(group, 0, 2)
+        score(GROUPS[0], "rel", nc.scalar.copy)
         imag_imag(7)
         imag_real(7)
+        score(GROUPS[1], "rel", nc.scalar.copy)
         turn(7, 0, by_aei)
         turn(7, 1, by_aei)
-        score(GROUPS[1])
         for group in GROUPS[2:4]:
             quantise(group, 0, 2)
-            score(group)
+        for part in range(2):
+            quantise(GROUPS[4], part, part + 1)
+        score(GROUPS[2], "vector", nc.vector.tensor_copy)
+        score(GROUPS[3], "vector", nc.scalar.copy)
         score_last(GROUPS[4])

@@ -190,9 +190,9 @@ def tile_list_ckg_none_kernel(
             )
 
         def deal_scales():
-            nc.gpsimd.tensor_copy(
-                dealt_s[:].rearrange("p (w t m) -> p w t m", w=4, t=PACK),
-                planes1[:].bitcast(U8).rearrange("p (w m t) -> p w t m", w=4, t=PACK),
+            nc.vector.tensor_copy(
+                dealt_s[:].rearrange("p (w t c i) -> p w c t i", w=4, t=PACK, i=16),
+                planes1[:].bitcast(U8).rearrange("p (w c i t) -> p w c t i", w=4, t=PACK, i=16),
             )
 
         def project(i, codes, scales, weight, fmt, name, tag):
@@ -349,9 +349,9 @@ def tile_list_ckg_none_kernel(
 
         for c in range(3):
             gather_relation(c)
+        deal_scales()
         for c in range(J // CHUNK):
             gather_entity(c)
-        deal_scales()
         nc.scalar.copy(*dealt_views("wrr", wrr_w, U16, 8))
         nc.scalar.copy(*dealt_views("wri", wri_w, U16, 8))
         nc.gpsimd.tensor_copy(*dealt_views("wer", wer_w, U32, 4))

@@ -23,7 +23,8 @@ ROWS = 16
 TILES = J // P
 CHUNK = 2 * P
 PARTS = ((0, CHUNK), (CHUNK, J))
-GROUPS = ((0, 1), (2, 3), (4, 5), (6,), (7,))
+RELATION_CHUNKS = ((0, 1), (1, 3), (3, 5), (5, 8))
+GROUPS = ((0, 1), (2, 3), (4,), (5,), (6,), (7,))
 AER_ON_GPSIMD = (0, 1, 2)
 R_FIRST = (3, 4, 5)
 
@@ -38,6 +39,7 @@ def tile_list_ckg_none_kernel(
         first = ctx.enter_context(tc.tile_pool(name="first", bufs=1))
         second = ctx.enter_context(tc.tile_pool(name="second", bufs=1))
         held = ctx.enter_context(tc.tile_pool(name="held", bufs=1))
+        chunks = ctx.enter_context(tc.tile_pool(name="chunks", bufs=1))
         late = ctx.enter_context(tc.tile_pool(name="late", bufs=1))
         ring = ctx.enter_context(tc.tile_pool(name="ring", bufs=3))
         psum = ctx.enter_context(tc.psum_pool(name="psum", bufs=1))
@@ -55,10 +57,10 @@ def tile_list_ckg_none_kernel(
         wri_w = keep.tile([P, R // 2], I32, name="wri_w", align_bytes=64)
 
         wer_w = first.tile([P, R], I32, name="wer_w", align_bytes=64, offset=0)
-        wei_w = first.tile([P, R], I32, name="wei_w", align_bytes=64, offset=4 * R)
-        staged1 = first.tile([P, R], I32, name="staged1", align_bytes=64, offset=0)
+        wei_w = first.tile([P, R], I32, name="wei_w", align_bytes=64, offset=8 * R)
+        staged1 = first.tile([P, R], I32, name="staged1", align_bytes=64, offset=3 * R)
         picked_s = [
-            first.tile([P, 2 * CHUNK], U8, name="picked_s0", align_bytes=64, offset=4 * R),
+            first.tile([P, 2 * CHUNK], U8, name="picked_s0", align_bytes=64, offset=8 * R),
             second.tile([P, 2 * (J - CHUNK)], U8, name="picked_s1", align_bytes=64, offset=2 * N),
         ]
         nr_w = second.tile([P, N], I32, name="nr_w", align_bytes=64, offset=0)
@@ -162,7 +164,12 @@ def tile_list_ckg_none_kernel(
                 found[c * CHUNK // P + n] = picked[:, n * P : (n + 1) * P]
 
         def gather_relation(c):
-            gather_words(w2, tab2_w, list2, "w2", c, 3)
+            lo, hi = RELATION_CHUNKS[c]
+            at = (6 * P, 24 * P, 0, 8 * P)[c]
+            picked = chunks.tile([P, (hi - lo) * P], U32, name="w2_" + str(c), align_bytes=64, offset=at)
+            gather(picked[:], tab2_w, U32, list2, lo * P, hi * P)
+            for i in range(lo, hi):
+                w2[i] = picked[:, (i - lo) * P : (i - lo + 1) * P]
 
         def gather_entity(c):
             gather_words(w1, tab1_w, list1, "w1", c, 3)
@@ -178,10 +185,11 @@ def tile_list_ckg_none_kernel(
             return in_turn[-1]
 
         dealt_w = {
-            "wrr": kept("wrr_dealt", R // 2), "wri": kept("wri_dealt", R // 2),
+            "wrr": first.tile([P, R // 2], I32, name="wrr_dealt", align_bytes=64, offset=4 * R),
+            "wri": first.tile([P, R // 2], I32, name="wri_dealt", align_bytes=64, offset=6 * R),
             "wer": kept("wer_dealt", R), "wei": held.tile([P, R], I32, name="wei_dealt", align_bytes=64, offset=0),
         }
-        dealt_s = kept("planes_dealt", 4 * R, U8)
+        dealt_s = [kept("rel_dealt", 2 * R, U8), kept("ent_dealt", 2 * R, U8)]
 
         def dealt_views(name, weight, word, run):
             return (
@@ -189,10 +197,10 @@ def tile_list_ckg_none_kernel(
                 weight[:].bitcast(word).rearrange("p (c i t) -> p c t i", t=PACK, i=run),
             )
 
-        def deal_scales():
-            nc.vector.tensor_copy(
-                dealt_s[:].rearrange("p (w t c i) -> p w c t i", w=4, t=PACK, i=16),
-                planes1[:].bitcast(U8).rearrange("p (w c i t) -> p w c t i", w=4, t=PACK, i=16),
+        def deal_scales(engine, lo):
+            engine.tensor_copy(
+                dealt_s[lo // (2 * R)][:].rearrange("p (w t c i) -> p w c t i", w=2, t=PACK, i=16),
+                planes1[:].bitcast(U8)[:, lo : lo + 2 * R].rearrange("p (w c i t) -> p w c t i", w=2, t=PACK, i=16),
             )
 
         def project(i, codes, scales, weight, fmt, name, tag):
@@ -209,7 +217,7 @@ def tile_list_ckg_none_kernel(
                 nc.tensor.matmul_mx(
                     out=acc[:, t * P : (t + 1) * P],
                     lhsT=columns[:, t * P : (t + 1) * P],
-                    lhsT_scale=dealt_s[:, base + t * P : base + (t + 1) * P],
+                    lhsT_scale=dealt_s[base // (2 * R)][:, base % (2 * R) + t * P : base % (2 * R) + (t + 1) * P],
                     rhs=codes[i].bitcast(FP8X4), rhs_scale=scales[i], start=True, stop=True,
                 )
             return acc[:].rearrange("p (t j) -> p j t", t=PACK)
@@ -225,15 +233,20 @@ def tile_list_ckg_none_kernel(
         aer, aei, rel, hq, by_aer, by_aei = {}, {}, {}, {}, {}, {}
         hq_group = {}
         for group in GROUPS:
-            hq_group[group] = keep.tile([P, 2, len(group) * P, PACK], BF16, name="hq" + str(group[0]), align_bytes=64)
+            shape, name = [P, 2, len(group) * P, PACK], "hq" + str(group[0])
+            if group[0] in (0, R_FIRST[-1]):
+                hq_group[group] = late.tile(shape, BF16, name=name, align_bytes=64, offset=32 * R)
+            else:
+                hq_group[group] = keep.tile(shape, BF16, name=name, align_bytes=64)
             for n, i in enumerate(group):
                 hq[i] = hq_group[group][:, :, n * P : (n + 1) * P]
 
         rel_buffers = [keep.tile([P, 2, R], F32, name="rel_sb" + str(n)) for n in range(6)]
 
         def relation(i, kinds=("rel", "rel"), parts=(0, 1)):
-            if i == TILES - 2:
-                rel[i] = shaped(i, late.tile([P, 2, R], F32, name="rel_late", align_bytes=64, offset=8 * R))
+            if i - 1 in R_FIRST[1:]:
+                at = 8 * R + 16 * R * R_FIRST[1:].index(i - 1)
+                rel[i] = shaped(i, late.tile([P, 2, R], F32, name="rel_late" + str(i), align_bytes=64, offset=at))
             else:
                 rel[i] = shaped(i, rel_buffers[i % 6])
             for part in parts:
@@ -252,8 +265,9 @@ def tile_list_ckg_none_kernel(
             aei[i] = project(i, w1, s1, wei_w, FP8X4, "wei", "vector")
 
         def products_of_aer(i):
-            if i == R_FIRST[-1]:
-                made = late.tile([P, 2, R], F32, name="by_aer" + str(i), align_bytes=64, offset=0)
+            if i in R_FIRST[1:]:
+                at = 16 * R * R_FIRST[1:].index(i)
+                made = late.tile([P, 2, R], F32, name="by_aer" + str(i), align_bytes=64, offset=at)
             else:
                 made = ring.tile([P, 2, R], F32, name="by_aer", bufs=4)
             by_aer[i] = shaped(i, made)
@@ -293,12 +307,15 @@ def tile_list_ckg_none_kernel(
 
         room = {}
 
-        def make_room():
-            codes = late.tile([P, 2 * J], U32, name="codes", align_bytes=64, offset=4 * R)
-            scales = kept("scales", 2 * J, U8)
-            for group in GROUPS:
+        scales = kept("scales", 2 * J, U8)
+
+        def make_room(groups, at):
+            first_tile = groups[0][0]
+            width = 2 * P * (groups[-1][-1] + 1 - first_tile)
+            codes = late.tile([P, width], U32, name="codes" + str(first_tile), align_bytes=64, offset=at)
+            for group in groups:
                 lo, hi = 2 * P * group[0], 2 * P * (group[-1] + 1)
-                room[group] = (codes[:, lo:hi], scales[:, lo:hi])
+                room[group] = (codes[:, lo - 2 * P * first_tile : hi - 2 * P * first_tile], scales[:, lo:hi])
 
         def quantise(group, lo, hi):
             width = len(group) * P
@@ -347,9 +364,10 @@ def tile_list_ckg_none_kernel(
             nc.scalar.copy(out=high[:], in_=y[1])
             nc.scalar.dma_start(out=out[P:N, i * P : (i + 1) * P], in_=high[:])
 
-        for c in range(3):
+        for c in range(2):
             gather_relation(c)
-        deal_scales()
+        deal_scales(nc.gpsimd, 0)
+        deal_scales(nc.vector, 2 * R)
         for c in range(J // CHUNK):
             gather_entity(c)
         nc.scalar.copy(*dealt_views("wrr", wrr_w, U16, 8))
@@ -358,6 +376,7 @@ def tile_list_ckg_none_kernel(
         relation(0)
         entity_real(0)
         products_of_aer(0)
+        gather_relation(2)
         relation(1, ("scalar", "rel"), (0,))
         entity_real(1)
         relation(1, ("scalar", "rel"), (1,))
@@ -390,6 +409,9 @@ def tile_list_ckg_none_kernel(
                 relation(i + 3)
             imag_imag(i)
             imag_real(i)
+            if i == R_FIRST[-1]:
+                make_room(GROUPS[0:1], 6 * R)
+                quantise(GROUPS[0], 0, 2)
             add_up(i)
             entity_real(i + 2)
             if i - 2 in AER_ON_GPSIMD:
@@ -397,28 +419,28 @@ def tile_list_ckg_none_kernel(
                 turn_sum(i - 2, 1, "pair")
 
         products_of_aer(6)
+        score(GROUPS[0], "rel", nc.scalar.copy)
         entity_imag(7)
         imag_imag(6)
         turn_sum(6, 0)
         imag_real(6)
         turn_sum(6, 1)
 
-        make_room()
+        make_room(GROUPS[1:], 20 * R)
         products_of_aer(7)
         turn(7, 0, by_aer)
         turn(7, 1, by_aer)
-        for group in GROUPS[0:2]:
-            quantise(group, 0, 2)
-        score(GROUPS[0], "rel", nc.scalar.copy)
         imag_imag(7)
-        imag_real(7)
-        score(GROUPS[1], "rel", nc.scalar.copy)
         turn(7, 0, by_aei)
+        quantise(GROUPS[1], 0, 2)
+        score(GROUPS[1], "rel", nc.scalar.copy)
+        imag_real(7)
         turn(7, 1, by_aei)
-        for group in GROUPS[2:4]:
+        for group in GROUPS[2:5]:
             quantise(group, 0, 2)
         for part in range(2):
-            quantise(GROUPS[4], part, part + 1)
+            quantise(GROUPS[5], part, part + 1)
         score(GROUPS[2], "vector", nc.vector.tensor_copy)
         score(GROUPS[3], "vector", nc.scalar.copy)
-        score_last(GROUPS[4])
+        score(GROUPS[4], "rel", nc.scalar.copy)
+        score_last(GROUPS[5])

@@ -23,7 +23,7 @@ ROWS = 16
 TILES = J // P
 CHUNK = 2 * P
 PARTS = ((0, CHUNK), (CHUNK, J))
-RELATION_CHUNKS = ((0, 1), (1, 3), (3, 5), (5, 8))
+RELATION_CHUNKS = ((0, 1), (1, 4), (4, 6), (6, 8))
 GROUPS = ((0, 1), (2, 3), (4,), (5,), (6,), (7,))
 AER_ON_GPSIMD = (0, 1, 2)
 R_FIRST = (3, 4, 5)
@@ -234,8 +234,9 @@ def tile_list_ckg_none_kernel(
         hq_group = {}
         for group in GROUPS:
             shape, name = [P, 2, len(group) * P, PACK], "hq" + str(group[0])
-            if group[0] in (0, R_FIRST[-1]):
-                hq_group[group] = late.tile(shape, BF16, name=name, align_bytes=64, offset=32 * R)
+            at = {0: 32 * R, 2: 40 * R, R_FIRST[-1]: 38 * R}.get(group[0])
+            if at:
+                hq_group[group] = late.tile(shape, BF16, name=name, align_bytes=64, offset=at)
             else:
                 hq_group[group] = keep.tile(shape, BF16, name=name, align_bytes=64)
             for n, i in enumerate(group):
@@ -340,12 +341,16 @@ def tile_list_ckg_none_kernel(
                 start=(part == 0), stop=(part == 1),
             )
 
-        def score(group, kind, copy):
+        def score_passes(group, kind):
             width = len(group) * P
             y = bank(kind)[:, 0 : N // P * width].rearrange("p (h j) -> p h j", j=width)
             for h in range(N // P):
                 for part in range(2):
                     score_pass(y[:, h, :], group, part, h)
+            return y
+
+        def store(group, y, copy):
+            width = len(group) * P
             y_sb = keep.tile([P, N // P, width], F32, name="y_sb" + str(group[0]))
             copy(y_sb[:], y)
             columns = out[:, group[0] * P : group[0] * P + width]
@@ -353,7 +358,7 @@ def tile_list_ckg_none_kernel(
 
         def score_last(group):
             i = group[0]
-            y = [bank("vector")[:, 0:P], bank("rel")[:, 0:P]]
+            y = [bank("vector")[:, 0:P], bank("vector")[:, 0:P]]
             for part in range(2):
                 for h in range(N // P):
                     score_pass(y[h], group, part, h)
@@ -405,42 +410,47 @@ def tile_list_ckg_none_kernel(
         for i in R_FIRST:
             products_of_aer(i)
             entity_imag(i + 1)
-            if i + 3 < TILES:
+            if i + 3 < TILES - 1:
                 relation(i + 3)
             imag_imag(i)
             imag_real(i)
-            if i == R_FIRST[-1]:
-                make_room(GROUPS[0:1], 6 * R)
-                quantise(GROUPS[0], 0, 2)
-            add_up(i)
+            if i < R_FIRST[-1]:
+                add_up(i)
             entity_real(i + 2)
             if i - 2 in AER_ON_GPSIMD:
                 turn_sum(i - 2, 0, "pair")
                 turn_sum(i - 2, 1, "pair")
+            if i + 3 == TILES - 1:
+                relation(i + 3)
 
         products_of_aer(6)
-        score(GROUPS[0], "rel", nc.scalar.copy)
+        make_room(GROUPS[0:2], 4 * R)
+        for group in GROUPS[0:2]:
+            quantise(group, 0, 2)
+        add_up(R_FIRST[-1])
         entity_imag(7)
+        turn(6, 0, by_aer)
+        turn(6, 1, by_aer)
+        store(GROUPS[0], score_passes(GROUPS[0], "rel"), nc.scalar.copy)
         imag_imag(6)
-        turn_sum(6, 0)
+        turn(6, 0, by_aei)
         imag_real(6)
-        turn_sum(6, 1)
+        turn(6, 1, by_aei)
+        store(GROUPS[1], score_passes(GROUPS[1], "vector"), nc.scalar.copy)
 
-        make_room(GROUPS[1:], 20 * R)
+        make_room(GROUPS[2:], 20 * R)
         products_of_aer(7)
         turn(7, 0, by_aer)
         turn(7, 1, by_aer)
         imag_imag(7)
         turn(7, 0, by_aei)
-        quantise(GROUPS[1], 0, 2)
-        score(GROUPS[1], "rel", nc.scalar.copy)
         imag_real(7)
         turn(7, 1, by_aei)
         for group in GROUPS[2:5]:
             quantise(group, 0, 2)
         for part in range(2):
             quantise(GROUPS[5], part, part + 1)
-        score(GROUPS[2], "vector", nc.vector.tensor_copy)
-        score(GROUPS[3], "vector", nc.scalar.copy)
-        score(GROUPS[4], "rel", nc.scalar.copy)
+        store(GROUPS[2], score_passes(GROUPS[2], "vector"), nc.vector.tensor_copy)
+        store(GROUPS[3], score_passes(GROUPS[3], "rel"), nc.scalar.copy)
+        store(GROUPS[4], score_passes(GROUPS[4], "rel"), nc.scalar.copy)
         score_last(GROUPS[5])

@@ -27,6 +27,9 @@ RELATION_CHUNKS = ((0, 1), (1, 4), (4, 6), (6, 8))
 GROUPS = ((0, 1), (2, 3), (4,), (5,), (6,), (7,))
 AER_ON_GPSIMD = (0, 1, 2)
 R_FIRST = (3, 4, 5)
+REL_BUFFERS = 6
+PAIR = 8 * R
+LINE = 16
 
 
 def tile_list_ckg_none_kernel(
@@ -154,15 +157,6 @@ def tile_list_ckg_none_kernel(
         load_words(nc.sync, ni_w, ni_words)
         spread_scales((nc.sync,), planes2, staged2, 0)
 
-        def gather_words(found, table, offsets, name, c, bufs):
-            if found is w1 and c == 0:
-                picked = held.tile([P, CHUNK], U32, name="w1_first", align_bytes=64, offset=0)
-            else:
-                picked = ring.tile([P, CHUNK], U32, name=name, bufs=bufs, align_bytes=64)
-            gather(picked[:], table, U32, offsets, c * CHUNK, (c + 1) * CHUNK)
-            for n in range(CHUNK // P):
-                found[c * CHUNK // P + n] = picked[:, n * P : (n + 1) * P]
-
         def gather_relation(c):
             lo, hi = RELATION_CHUNKS[c]
             at = (6 * P, 24 * P, 0, 8 * P)[c]
@@ -172,7 +166,13 @@ def tile_list_ckg_none_kernel(
                 w2[i] = picked[:, (i - lo) * P : (i - lo + 1) * P]
 
         def gather_entity(c):
-            gather_words(w1, tab1_w, list1, "w1", c, 3)
+            if c == 0:
+                picked = held.tile([P, CHUNK], U32, name="w1_first", align_bytes=64, offset=0)
+            else:
+                picked = ring.tile([P, CHUNK], U32, name="w1", align_bytes=64)
+            gather(picked[:], tab1_w, U32, list1, c * CHUNK, (c + 1) * CHUNK)
+            for n in range(CHUNK // P):
+                w1[c * CHUNK // P + n] = picked[:, n * P : (n + 1) * P]
 
         banks = {
             kind: [psum.tile([P, R], F32, name=kind + str(n)) for n in range(count)]
@@ -187,7 +187,8 @@ def tile_list_ckg_none_kernel(
         dealt_w = {
             "wrr": first.tile([P, R // 2], I32, name="wrr_dealt", align_bytes=64, offset=4 * R),
             "wri": first.tile([P, R // 2], I32, name="wri_dealt", align_bytes=64, offset=6 * R),
-            "wer": kept("wer_dealt", R), "wei": held.tile([P, R], I32, name="wei_dealt", align_bytes=64, offset=0),
+            "wer": kept("wer_dealt", R),
+            "wei": held.tile([P, R], I32, name="wei_dealt", align_bytes=64, offset=0),
         }
         dealt_s = [kept("rel_dealt", 2 * R, U8), kept("ent_dealt", 2 * R, U8)]
 
@@ -197,10 +198,11 @@ def tile_list_ckg_none_kernel(
                 weight[:].bitcast(word).rearrange("p (c i t) -> p c t i", t=PACK, i=run),
             )
 
-        def deal_scales(engine, lo):
+        def deal_scales(engine, side):
+            both = planes1[:].bitcast(U8)[:, side * 2 * R : (side + 1) * 2 * R]
             engine.tensor_copy(
-                dealt_s[lo // (2 * R)][:].rearrange("p (w t c i) -> p w c t i", w=2, t=PACK, i=16),
-                planes1[:].bitcast(U8)[:, lo : lo + 2 * R].rearrange("p (w c i t) -> p w c t i", w=2, t=PACK, i=16),
+                dealt_s[side][:].rearrange("p (w t c i) -> p w c t i", w=2, t=PACK, i=LINE),
+                both.rearrange("p (w c i t) -> p w c t i", w=2, t=PACK, i=LINE),
             )
 
         def project(i, codes, scales, weight, fmt, name, tag):
@@ -211,13 +213,13 @@ def tile_list_ckg_none_kernel(
                     rhs=weight[:].bitcast(fmt), rhs_scale=plane(name, 0, R), start=True, stop=True,
                 )
                 return acc[:].rearrange("j (m t) -> j t m", t=PACK)
-            base = plane_at[name][2]
+            side, base = plane_at[name][2] // (2 * R), plane_at[name][2] % (2 * R)
             columns = dealt_w[name][:].bitcast(fmt)
             for t in range(PACK):
                 nc.tensor.matmul_mx(
                     out=acc[:, t * P : (t + 1) * P],
                     lhsT=columns[:, t * P : (t + 1) * P],
-                    lhsT_scale=dealt_s[base // (2 * R)][:, base % (2 * R) + t * P : base % (2 * R) + (t + 1) * P],
+                    lhsT_scale=dealt_s[side][:, base + t * P : base + (t + 1) * P],
                     rhs=codes[i].bitcast(FP8X4), rhs_scale=scales[i], start=True, stop=True,
                 )
             return acc[:].rearrange("p (t j) -> p j t", t=PACK)
@@ -231,10 +233,11 @@ def tile_list_ckg_none_kernel(
             return slots.unsqueeze(1).to_broadcast([P, 2] + list(slots.shape[1:]))
 
         aer, aei, rel, hq, by_aer, by_aei = {}, {}, {}, {}, {}, {}
+
         hq_group = {}
         for group in GROUPS:
             shape, name = [P, 2, len(group) * P, PACK], "hq" + str(group[0])
-            at = {0: 32 * R, 2: 40 * R, R_FIRST[-1]: 38 * R}.get(group[0])
+            at = {0: 4 * PAIR, 2: 5 * PAIR, R_FIRST[-1]: 5 * PAIR - PAIR // 4}.get(group[0])
             if at:
                 hq_group[group] = late.tile(shape, BF16, name=name, align_bytes=64, offset=at)
             else:
@@ -242,22 +245,22 @@ def tile_list_ckg_none_kernel(
             for n, i in enumerate(group):
                 hq[i] = hq_group[group][:, :, n * P : (n + 1) * P]
 
-        rel_buffers = [keep.tile([P, 2, R], F32, name="rel_sb" + str(n)) for n in range(6)]
+        rel_buffers = [keep.tile([P, 2, R], F32, name="rel_sb" + str(n)) for n in range(REL_BUFFERS)]
 
         def relation(i, kinds=("rel", "rel"), parts=(0, 1)):
             if i - 1 in R_FIRST[1:]:
-                at = 8 * R + 16 * R * R_FIRST[1:].index(i - 1)
+                at = PAIR + 2 * PAIR * R_FIRST[1:].index(i - 1)
                 rel[i] = shaped(i, late.tile([P, 2, R], F32, name="rel_late" + str(i), align_bytes=64, offset=at))
             else:
-                rel[i] = shaped(i, rel_buffers[i % 6])
+                rel[i] = shaped(i, rel_buffers[i % REL_BUFFERS])
             for part in parts:
                 weight, name = ((wrr_w, "wrr"), (wri_w, "wri"))[part]
                 nc.scalar.copy(out=rel[i][:, part], in_=project(i, w2, s2, weight, FP4X4, name, kinds[part]))
 
-        def entity_real(i, kind="rel"):
+        def entity_real(i):
             if i in AER_ON_GPSIMD:
                 copied = keep.tile([P, PACK, P], F32, name="aer" + str(i))
-                nc.scalar.copy(out=copied[:], in_=project(i, w1, s1, wer_w, FP8X4, "wer", kind))
+                nc.scalar.copy(out=copied[:], in_=project(i, w1, s1, wer_w, FP8X4, "wer", "rel"))
                 aer[i] = copied[:]
             else:
                 aer[i] = project(i, w1, s1, wer_w, FP8X4, "wer", "vector")
@@ -267,7 +270,7 @@ def tile_list_ckg_none_kernel(
 
         def products_of_aer(i):
             if i in R_FIRST[1:]:
-                at = 16 * R * R_FIRST[1:].index(i)
+                at = 2 * PAIR * R_FIRST[1:].index(i)
                 made = late.tile([P, 2, R], F32, name="by_aer" + str(i), align_bytes=64, offset=at)
             else:
                 made = ring.tile([P, 2, R], F32, name="by_aer", bufs=4)
@@ -276,7 +279,7 @@ def tile_list_ckg_none_kernel(
             engine.tensor_tensor(out=by_aer[i], in0=twice(aer[i]), in1=rel[i], op=MULT)
 
         def imag_imag(i):
-            made = ring.tile([P, 2, R], F32, name="by_aei", bufs=4)
+            made = ring.tile([P, 2, R], F32, name="by_aei", bufs=6)
             by_aei[i] = shaped(i, made)
             nc.vector.scalar_tensor_tensor(
                 out=by_aei[i][:, 0], in0=aei[i], scalar=-1.0, in1=rel[i][:, 1], op0=MULT, op1=MULT
@@ -291,24 +294,24 @@ def tile_list_ckg_none_kernel(
         turned = {}
 
         def turn(i, part, term, kind="scalar"):
-            first = (i, part) not in turned
-            if first:
+            opens = (i, part) not in turned
+            if opens:
                 turned[i, part] = bank(kind)[:].rearrange("p (t j) -> p t j", t=PACK)
             for t in range(PACK):
                 nc.tensor.matmul(
                     out=turned[i, part][:, t, :], lhsT=term[i][:, part, t, :], rhs=ident[:], is_transpose=True,
-                    start=(first and t == 0), stop=(not first and t == PACK - 1),
+                    start=(opens and t == 0), stop=(not opens and t == PACK - 1),
                 )
-            if not first:
+            if not opens:
                 nc.scalar.copy(out=hq[i][:, part], in_=turned[i, part].rearrange("p t j -> p j t"))
 
-        def turn_sum(i, part, kind="scalar"):
-            for term in (by_aei, by_aer):
-                turn(i, part, term, kind)
+        def turn_tile(i):
+            for part in range(2):
+                for term in (by_aei, by_aer):
+                    turn(i, part, term, "pair")
 
         room = {}
-
-        scales = kept("scales", 2 * J, U8)
+        hq_planes = kept("scales", 2 * J, U8)
 
         def make_room(groups, at):
             first_tile = groups[0][0]
@@ -316,7 +319,7 @@ def tile_list_ckg_none_kernel(
             codes = late.tile([P, width], U32, name="codes" + str(first_tile), align_bytes=64, offset=at)
             for group in groups:
                 lo, hi = 2 * P * group[0], 2 * P * (group[-1] + 1)
-                room[group] = (codes[:, lo - 2 * P * first_tile : hi - 2 * P * first_tile], scales[:, lo:hi])
+                room[group] = (codes[:, lo - 2 * P * first_tile : hi - 2 * P * first_tile], hq_planes[:, lo:hi])
 
         def quantise(group, lo, hi):
             width = len(group) * P
@@ -372,12 +375,13 @@ def tile_list_ckg_none_kernel(
         for c in range(2):
             gather_relation(c)
         deal_scales(nc.gpsimd, 0)
-        deal_scales(nc.vector, 2 * R)
+        deal_scales(nc.vector, 1)
         for c in range(J // CHUNK):
             gather_entity(c)
-        nc.scalar.copy(*dealt_views("wrr", wrr_w, U16, 8))
-        nc.scalar.copy(*dealt_views("wri", wri_w, U16, 8))
-        nc.gpsimd.tensor_copy(*dealt_views("wer", wer_w, U32, 4))
+        nc.scalar.copy(*dealt_views("wrr", wrr_w, U16, LINE // 2))
+        nc.scalar.copy(*dealt_views("wri", wri_w, U16, LINE // 2))
+        nc.gpsimd.tensor_copy(*dealt_views("wer", wer_w, U32, LINE // 4))
+
         relation(0)
         entity_real(0)
         products_of_aer(0)
@@ -389,7 +393,7 @@ def tile_list_ckg_none_kernel(
         for i in AER_ON_GPSIMD:
             entity_imag(i)
         relation(2)
-        nc.scalar.copy(*dealt_views("wei", wei_w, U32, 4))
+        nc.scalar.copy(*dealt_views("wei", wei_w, U32, LINE // 4))
         relation(3, ("scalar", "scalar"))
         gather_relation(3)
         entity_real(2)
@@ -405,8 +409,7 @@ def tile_list_ckg_none_kernel(
 
         banks["pair"] = banks["scalar"][1:3]
         relation(5)
-        turn_sum(0, 0, "pair")
-        turn_sum(0, 1, "pair")
+        turn_tile(0)
         for i in R_FIRST:
             products_of_aer(i)
             entity_imag(i + 1)
@@ -418,13 +421,12 @@ def tile_list_ckg_none_kernel(
                 add_up(i)
             entity_real(i + 2)
             if i - 2 in AER_ON_GPSIMD:
-                turn_sum(i - 2, 0, "pair")
-                turn_sum(i - 2, 1, "pair")
+                turn_tile(i - 2)
             if i + 3 == TILES - 1:
                 relation(i + 3)
 
         products_of_aer(6)
-        make_room(GROUPS[0:2], 4 * R)
+        make_room(GROUPS[0:2], PAIR // 2)
         for group in GROUPS[0:2]:
             quantise(group, 0, 2)
         add_up(R_FIRST[-1])
@@ -438,7 +440,7 @@ def tile_list_ckg_none_kernel(
         turn(6, 1, by_aei)
         store(GROUPS[1], score_passes(GROUPS[1], "vector"), nc.scalar.copy)
 
-        make_room(GROUPS[2:], 20 * R)
+        make_room(GROUPS[2:], 2 * PAIR + PAIR // 2)
         products_of_aer(7)
         turn(7, 0, by_aer)
         turn(7, 1, by_aer)

from contextlib import ExitStack

import concourse.mybir as mybir
from concourse.masks import make_identity

K, L, R, N, T, J = 512, 512, 512, 256, 2048, 1024
FLOPS = 2 * 4 * K * R * J + 2 * 2 * R * N * J

F32 = mybir.dt.float32
BF16 = mybir.dt.bfloat16
I32 = mybir.dt.int32
U32 = mybir.dt.uint32
U16 = mybir.dt.uint16
U8 = mybir.dt.uint8
FP8X4 = mybir.dt.float8_e4m3fn_x4
FP4X4 = mybir.dt.float4_e2m1fn_x4
MULT = mybir.AluOpType.mult
ADD = mybir.AluOpType.add

P = 128
PACK = 4
ROWS = 16
TILES = J // P
CHUNK = 2 * P
PARTS = ((0, CHUNK), (CHUNK, J))
RELATION_CHUNKS = ((0, 1), (1, 4), (4, 6), (6, 8))
GROUPS = ((0, 1), (2, 3), (4,), (5,), (6,), (7,))
AER_ON_GPSIMD = (0, 1, 2)
R_FIRST = (3, 4, 5)
REL_BUFFERS = 6
PAIR = 8 * R
LINE = 16


def tile_list_ckg_none_kernel(
    tc, tab_words, tab_scales, tab2_words, tab2_scales, wer_words, wer_scales, wei_words, wei_scales,
    wrr_words, wrr_scales, wri_words, wri_scales, nr_words, nr_scales, ni_words, ni_scales, offs, offs2, out,
):
    nc = tc.nc
    with ExitStack() as ctx:
        keep = ctx.enter_context(tc.tile_pool(name="keep", bufs=1))
        first = ctx.enter_context(tc.tile_pool(name="first", bufs=1))
        second = ctx.enter_context(tc.tile_pool(name="second", bufs=1))
        held = ctx.enter_context(tc.tile_pool(name="held", bufs=1))
        chunks = ctx.enter_context(tc.tile_pool(name="chunks", bufs=1))
        late = ctx.enter_context(tc.tile_pool(name="late", bufs=1))
        ring = ctx.enter_context(tc.tile_pool(name="ring", bufs=3))
        psum = ctx.enter_context(tc.psum_pool(name="psum", bufs=1))

        def kept(name, width, dtype=I32):
            return keep.tile([P, width], dtype, name=name, align_bytes=64)

        list1 = keep.tile([P, J // 16], U16, name="list1")
        list2 = keep.tile([P, J // 16], U16, name="list2")
        tab1_w = keep.tile([P, T], I32, name="tab1_w", align_bytes=64)
        tab2_w = keep.tile([P, T], I32, name="tab2_w", align_bytes=64)
        tab1_s = keep.tile([P, T // 4], I32, name="tab1_s", align_bytes=64)
        tab2_s = keep.tile([P, T // 4], I32, name="tab2_s", align_bytes=64)
        wrr_w = keep.tile([P, R // 2], I32, name="wrr_w", align_bytes=64)
        wri_w = keep.tile([P, R // 2], I32, name="wri_w", align_bytes=64)

        wer_w = first.tile([P, R], I32, name="wer_w", align_bytes=64, offset=0)
        wei_w = first.tile([P, R], I32, name="wei_w", align_bytes=64, offset=8 * R)
        staged1 = first.tile([P, R], I32, name="staged1", align_bytes=64, offset=3 * R)
        picked_s = [
            first.tile([P, 2 * CHUNK], U8, name="picked_s0", align_bytes=64, offset=8 * R),
            second.tile([P, 2 * (J - CHUNK)], U8, name="picked_s1", align_bytes=64, offset=2 * N),
        ]
        nr_w = second.tile([P, N], I32, name="nr_w", align_bytes=64, offset=0)
        staged2 = second.tile([P, N // 2], I32, name="staged2", align_bytes=64, offset=4 * N)
        ni_w = second.tile([P, N // 2], I32, name="ni_w", align_bytes=64, offset=6 * N)

        planes_t = [keep.tile([P, (hi - lo) // 2], I32, name="planes_t" + str(lo), align_bytes=64) for lo, hi in PARTS]
        planes1 = keep.tile([P, R], I32, name="planes1", align_bytes=64)
        planes2 = keep.tile([P, N // 2], I32, name="planes2", align_bytes=64)
        ident = keep.tile([P, P], F32, name="ident")

        plane_at = {
            "wrr": (staged1, planes1, 0), "wri": (staged1, planes1, R),
            "wer": (staged1, planes1, 2 * R), "wei": (staged1, planes1, 3 * R),
            "nr": (staged2, planes2, 0), "ni": (staged2, planes2, N),
        }

        def plane(name, lo, hi):
            tile, base = plane_at[name][1:]
            return tile[:].bitcast(U8)[:, base + lo : base + hi]

        def load_words(queue, tile, words):
            src = words[0]
            if len(src.shape) == 3:
                src = src.rearrange("p n t -> p (n t)")
            queue.dma_start(out=tile[:], in_=src.bitcast(I32))

        def load_table_words(tile, words):
            src = words[0].rearrange("p n t -> p (n t)").bitcast(I32)
            for lo in range(0, T, T // 2):
                nc.gpsimd.dma_start(out=tile[:, lo : lo + T // 2], in_=src[:, lo : lo + T // 2])

        def load_table_scales(queue, tile, scales):
            queue.dma_start(out=tile[P - ROWS : P, :], in_=scales[0].bitcast(I32))

        def stage_scales(queue, name, scales):
            tile, base = plane_at[name][0], plane_at[name][2]
            rows = scales[0].bitcast(I32)
            queue.dma_start(out=tile[0:ROWS, base // 4 : base // 4 + rows.shape[1]], in_=rows)

        def spread_scales(queues, planes, rows, first_row):
            for q in range(4):
                at = first_row + 4 * q
                queues[q % len(queues)].dma_start(out=planes[32 * q : 32 * q + 4, :], in_=rows[at : at + 4, :])

        nc.vector.memset(tab2_s[0 : P - ROWS, :], 0)
        nc.vector.memset(tab1_s[0 : P - ROWS, :], 0)
        nc.vector.memset(planes1[:], 0)
        nc.vector.memset(planes_t[0][:], 0)
        load_table_words(tab2_w, tab2_words)
        load_table_words(tab1_w, tab_words)
        nc.gpsimd.memset(planes_t[1][:], 0)
        nc.gpsimd.memset(planes2[:], 0)
        make_identity(nc, ident[:])

        nc.sync.dma_start(list2[:], offs2)
        nc.sync.dma_start(list1[:], offs)
        stage_scales(nc.scalar, "wrr", wrr_scales)
        stage_scales(nc.scalar, "wri", wri_scales)
        stage_scales(nc.sync, "wer", wer_scales)
        stage_scales(nc.scalar, "wei", wei_scales)
        load_table_scales(nc.sync, tab2_s, tab2_scales)
        load_table_scales(nc.scalar, tab1_s, tab_scales)
        load_words(nc.sync, wrr_w, wrr_words)
        load_words(nc.scalar, wri_w, wri_words)
        spread_scales((nc.sync, nc.scalar), planes1, staged1, 0)
        load_words(nc.scalar, wer_w, wer_words)

        def gather(picked, table, view, offsets, lo, hi):
            nc.vector.tensor_copy(picked, table[:].bitcast(view).indirect(offsets[:, lo // 16 : hi // 16]))

        s1, s2, w1, w2 = {}, {}, {}, {}

        def gather_scales(part):
            lo, hi = PARTS[part]
            width = hi - lo
            gather(picked_s[part][:, 0:width], tab2_s, U8, list2, lo, hi)
            gather(picked_s[part][:, width : 2 * width], tab1_s, U8, list1, lo, hi)
            spread_scales((nc.sync,), planes_t[part], picked_s[part][:].bitcast(I32), P - ROWS)
            for i in range(lo // P, hi // P):
                s2[i] = planes_t[part][:].bitcast(U8)[:, i * P - lo : (i + 1) * P - lo]
                s1[i] = planes_t[part][:].bitcast(U8)[:, width + i * P - lo : width + (i + 1) * P - lo]

        gather_scales(0)
        load_words(nc.sync, wei_w, wei_words)
        gather_scales(1)

        stage_scales(nc.sync, "nr", nr_scales)
        stage_scales(nc.sync, "ni", ni_scales)
        load_words(nc.sync, nr_w, nr_words)
        load_words(nc.sync, ni_w, ni_words)
        spread_scales((nc.sync,), planes2, staged2, 0)

        def gather_relation(c):
            lo, hi = RELATION_CHUNKS[c]
            at = (6 * P, 24 * P, 0, 8 * P)[c]
            picked = chunks.tile([P, (hi - lo) * P], U32, name="w2_" + str(c), align_bytes=64, offset=at)
            gather(picked[:], tab2_w, U32, list2, lo * P, hi * P)
            for i in range(lo, hi):
                w2[i] = picked[:, (i - lo) * P : (i - lo + 1) * P]

        def gather_entity(c):
            if c == 0:
                picked = held.tile([P, CHUNK], U32, name="w1_first", align_bytes=64, offset=0)
            else:
                picked = ring.tile([P, CHUNK], U32, name="w1", align_bytes=64)
            gather(picked[:], tab1_w, U32, list1, c * CHUNK, (c + 1) * CHUNK)
            for n in range(CHUNK // P):
                w1[c * CHUNK // P + n] = picked[:, n * P : (n + 1) * P]

        banks = {
            kind: [psum.tile([P, R], F32, name=kind + str(n)) for n in range(count)]
            for kind, count in (("rel", 2), ("scalar", 3), ("vector", 3))
        }

        def bank(kind):
            in_turn = banks[kind]
            in_turn.append(in_turn.pop(0))
            return in_turn[-1]

        dealt_w = {
            "wrr": first.tile([P, R // 2], I32, name="wrr_dealt", align_bytes=64, offset=4 * R),
            "wri": first.tile([P, R // 2], I32, name="wri_dealt", align_bytes=64, offset=6 * R),
            "wer": kept("wer_dealt", R),
            "wei": held.tile([P, R], I32, name="wei_dealt", align_bytes=64, offset=0),
        }
        dealt_s = [kept("rel_dealt", 2 * R, U8), kept("ent_dealt", 2 * R, U8)]

        def dealt_views(name, weight, word, run):
            return (
                dealt_w[name][:].bitcast(word).rearrange("p (t c i) -> p c t i", t=PACK, i=run),
                weight[:].bitcast(word).rearrange("p (c i t) -> p c t i", t=PACK, i=run),
            )

        def deal_scales(engine, side):
            both = planes1[:].bitcast(U8)[:, side * 2 * R : (side + 1) * 2 * R]
            engine.tensor_copy(
                dealt_s[side][:].rearrange("p (w t c i) -> p w c t i", w=2, t=PACK, i=LINE),
                both.rearrange("p (w c i t) -> p w c t i", w=2, t=PACK, i=LINE),
            )

        def project(i, codes, scales, weight, fmt, name, tag):
            acc = bank(tag)
            if i not in R_FIRST:
                nc.tensor.matmul_mx(
                    out=acc[:], lhsT=codes[i].bitcast(FP8X4), lhsT_scale=scales[i],
                    rhs=weight[:].bitcast(fmt), rhs_scale=plane(name, 0, R), start=True, stop=True,
                )
                return acc[:].rearrange("j (m t) -> j t m", t=PACK)
            side, base = plane_at[name][2] // (2 * R), plane_at[name][2] % (2 * R)
            columns = dealt_w[name][:].bitcast(fmt)
            for t in range(PACK):
                nc.tensor.matmul_mx(
                    out=acc[:, t * P : (t + 1) * P],
                    lhsT=columns[:, t * P : (t + 1) * P],
                    lhsT_scale=dealt_s[side][:, base + t * P : base + (t + 1) * P],
                    rhs=codes[i].bitcast(FP8X4), rhs_scale=scales[i], start=True, stop=True,
                )
            return acc[:].rearrange("p (t j) -> p j t", t=PACK)

        def shaped(i, flat):
            if i in R_FIRST:
                return flat[:].rearrange("p c (j t) -> p c j t", t=PACK)
            return flat[:].rearrange("j c (t m) -> j c t m", t=PACK)

        def twice(slots):
            return slots.unsqueeze(1).to_broadcast([P, 2] + list(slots.shape[1:]))

        aer, aei, rel, hq, by_aer, by_aei = {}, {}, {}, {}, {}, {}

        hq_group = {}
        for group in GROUPS:
            shape, name = [P, 2, len(group) * P, PACK], "hq" + str(group[0])
            at = {0: 4 * PAIR, 2: 5 * PAIR, R_FIRST[-1]: 5 * PAIR - PAIR // 4}.get(group[0])
            if at:
                hq_group[group] = late.tile(shape, BF16, name=name, align_bytes=64, offset=at)
            else:
                hq_group[group] = keep.tile(shape, BF16, name=name, align_bytes=64)
            for n, i in enumerate(group):
                hq[i] = hq_group[group][:, :, n * P : (n + 1) * P]

        rel_buffers = [keep.tile([P, 2, R], F32, name="rel_sb" + str(n)) for n in range(REL_BUFFERS)]

        def relation(i, kinds=("rel", "rel"), parts=(0, 1)):
            if i - 1 in R_FIRST[1:]:
                at = PAIR + 2 * PAIR * R_FIRST[1:].index(i - 1)
                rel[i] = shaped(i, late.tile([P, 2, R], F32, name="rel_late" + str(i), align_bytes=64, offset=at))
            else:
                rel[i] = shaped(i, rel_buffers[i % REL_BUFFERS])
            for part in parts:
                weight, name = ((wrr_w, "wrr"), (wri_w, "wri"))[part]
                nc.scalar.copy(out=rel[i][:, part], in_=project(i, w2, s2, weight, FP4X4, name, kinds[part]))

        def entity_real(i):
            if i in AER_ON_GPSIMD:
                copied = keep.tile([P, PACK, P], F32, name="aer" + str(i))
                nc.scalar.copy(out=copied[:], in_=project(i, w1, s1, wer_w, FP8X4, "wer", "rel"))
                aer[i] = copied[:]
            else:
                aer[i] = project(i, w1, s1, wer_w, FP8X4, "wer", "vector")

        def entity_imag(i):
            aei[i] = project(i, w1, s1, wei_w, FP8X4, "wei", "vector")

        def products_of_aer(i):
            if i in R_FIRST[1:]:
                at = 2 * PAIR * R_FIRST[1:].index(i)
                made = late.tile([P, 2, R], F32, name="by_aer" + str(i), align_bytes=64, offset=at)
            else:
                made = ring.tile([P, 2, R], F32, name="by_aer", bufs=4)
            by_aer[i] = shaped(i, made)
            engine = nc.gpsimd if i in AER_ON_GPSIMD else nc.vector
            engine.tensor_tensor(out=by_aer[i], in0=twice(aer[i]), in1=rel[i], op=MULT)

        def imag_imag(i):
            made = ring.tile([P, 2, R], F32, name="by_aei", bufs=6)
            by_aei[i] = shaped(i, made)
            nc.vector.scalar_tensor_tensor(
                out=by_aei[i][:, 0], in0=aei[i], scalar=-1.0, in1=rel[i][:, 1], op0=MULT, op1=MULT
            )

        def imag_real(i):
            nc.vector.tensor_tensor(out=by_aei[i][:, 1], in0=aei[i], in1=rel[i][:, 0], op=MULT)

        def add_up(i):
            nc.gpsimd.tensor_tensor(out=hq[i], in0=by_aer[i], in1=by_aei[i], op=ADD)

        turned = {}

        def turn(i, part, term, kind="scalar"):
            opens = (i, part) not in turned
            if opens:
                turned[i, part] = bank(kind)[:].rearrange("p (t j) -> p t j", t=PACK)
            for t in range(PACK):
                nc.tensor.matmul(
                    out=turned[i, part][:, t, :], lhsT=term[i][:, part, t, :], rhs=ident[:], is_transpose=True,
                    start=(opens and t == 0), stop=(not opens and t == PACK - 1),
                )
            if not opens:
                nc.scalar.copy(out=hq[i][:, part], in_=turned[i, part].rearrange("p t j -> p j t"))

        def turn_tile(i):
            for part in range(2):
                for term in (by_aei, by_aer):
                    turn(i, part, term, "pair")

        room = {}
        hq_planes = kept("scales", 2 * J, U8)

        def make_room(groups, at):
            first_tile = groups[0][0]
            width = 2 * P * (groups[-1][-1] + 1 - first_tile)
            codes = late.tile([P, width], U32, name="codes" + str(first_tile), align_bytes=64, offset=at)
            for group in groups:
                lo, hi = 2 * P * group[0], 2 * P * (group[-1] + 1)
                room[group] = (codes[:, lo - 2 * P * first_tile : hi - 2 * P * first_tile], hq_planes[:, lo:hi])

        def quantise(group, lo, hi):
            width = len(group) * P
            codes, scales = room[group]
            nc.vector.quantize_mx(
                out=codes[:, lo * width : hi * width].bitcast(FP8X4),
                scales=scales[:, lo * width : hi * width],
                in_=hq_group[group][:, lo:hi].rearrange("p c j t -> p (c j t)"),
            )

        def score_pass(y, group, part, h):
            codes, scales = room[group]
            width = len(group) * P
            if part == 0:
                weight = nr_w[:, h * P : (h + 1) * P].bitcast(FP8X4)
            else:
                weight = ni_w[:, h * P // 2 : (h + 1) * P // 2].bitcast(FP4X4)
            nc.tensor.matmul_mx(
                out=y, lhsT=weight, lhsT_scale=plane(("nr", "ni")[part], h * P, (h + 1) * P),
                rhs=codes[:, part * width : (part + 1) * width].bitcast(FP8X4),
                rhs_scale=scales[:, part * width : (part + 1) * width],
                start=(part == 0), stop=(part == 1),
            )

        def score_passes(group, kind):
            width = len(group) * P
            y = bank(kind)[:, 0 : N // P * width].rearrange("p (h j) -> p h j", j=width)
            for h in range(N // P):
                for part in range(2):
                    score_pass(y[:, h, :], group, part, h)
            return y

        def store(group, y, copy):
            width = len(group) * P
            y_sb = keep.tile([P, N // P, width], F32, name="y_sb" + str(group[0]))
            copy(y_sb[:], y)
            columns = out[:, group[0] * P : group[0] * P + width]
            nc.sync.dma_start(out=columns.rearrange("(h p) j -> p h j", p=P), in_=y_sb[:])

        def score_last(group):
            i = group[0]
            y = [bank("vector")[:, 0:P], bank("vector")[:, 0:P]]
            for part in range(2):
                for h in range(N // P):
                    score_pass(y[h], group, part, h)
            low = keep.tile([P, P], F32, name="last_low")
            nc.vector.tensor_copy(low[:], y[0])
            nc.sync.dma_start(out=out[0:P, i * P : (i + 1) * P], in_=low[:])
            high = keep.tile([P, P], F32, name="last_high")
            nc.scalar.copy(out=high[:], in_=y[1])
            nc.scalar.dma_start(out=out[P:N, i * P : (i + 1) * P], in_=high[:])

        for c in range(2):
            gather_relation(c)
        deal_scales(nc.gpsimd, 0)
        deal_scales(nc.vector, 1)
        for c in range(J // CHUNK):
            gather_entity(c)
        nc.scalar.copy(*dealt_views("wrr", wrr_w, U16, LINE // 2))
        nc.scalar.copy(*dealt_views("wri", wri_w, U16, LINE // 2))
        nc.gpsimd.tensor_copy(*dealt_views("wer", wer_w, U32, LINE // 4))

        relation(0)
        entity_real(0)
        products_of_aer(0)
        gather_relation(2)
        relation(1, ("scalar", "rel"), (0,))
        entity_real(1)
        relation(1, ("scalar", "rel"), (1,))
        products_of_aer(1)
        for i in AER_ON_GPSIMD:
            entity_imag(i)
        relation(2)
        nc.scalar.copy(*dealt_views("wei", wei_w, U32, LINE // 4))
        relation(3, ("scalar", "scalar"))
        gather_relation(3)
        entity_real(2)
        products_of_aer(2)
        relation(4)

        for i in AER_ON_GPSIMD:
            imag_imag(i)
            imag_real(i)
        entity_real(3)
        entity_imag(3)
        entity_real(4)

        banks["pair"] = banks["scalar"][1:3]
        relation(5)
        turn_tile(0)
        for i in R_FIRST:
            products_of_aer(i)
            entity_imag(i + 1)
            if i + 3 < TILES - 1:
                relation(i + 3)
            imag_imag(i)
            imag_real(i)
            if i < R_FIRST[-1]:
                add_up(i)
            entity_real(i + 2)
            if i - 2 in AER_ON_GPSIMD:
                turn_tile(i - 2)
            if i + 3 == TILES - 1:
                relation(i + 3)

        products_of_aer(6)
        make_room(GROUPS[0:2], PAIR // 2)
        for group in GROUPS[0:2]:
            quantise(group, 0, 2)
        add_up(R_FIRST[-1])
        entity_imag(7)
        turn(6, 0, by_aer)
        turn(6, 1, by_aer)
        store(GROUPS[0], score_passes(GROUPS[0], "rel"), nc.scalar.copy)
        imag_imag(6)
        turn(6, 0, by_aei)
        imag_real(6)
        turn(6, 1, by_aei)
        store(GROUPS[1], score_passes(GROUPS[1], "vector"), nc.scalar.copy)

        make_room(GROUPS[2:], 2 * PAIR + PAIR // 2)
        products_of_aer(7)
        turn(7, 0, by_aer)
        turn(7, 1, by_aer)
        imag_imag(7)
        turn(7, 0, by_aei)
        imag_real(7)
        turn(7, 1, by_aei)
        for group in GROUPS[2:5]:
            quantise(group, 0, 2)
        for part in range(2):
            quantise(GROUPS[5], part, part + 1)
        store(GROUPS[2], score_passes(GROUPS[2], "vector"), nc.vector.tensor_copy)
        store(GROUPS[3], score_passes(GROUPS[3], "rel"), nc.scalar.copy)
        store(GROUPS[4], score_passes(GROUPS[4], "rel"), nc.scalar.copy)
        score_last(GROUPS[5])
